import numpy as np
import ml_dtypes


def mxq(x, axis, fmt="e4m3"):
    dtype, down = {"e4m3": (ml_dtypes.float8_e4m3fn, 7), "e5m2": (ml_dtypes.float8_e5m2, 14)}[fmt]
    v = np.moveaxis(np.asarray(x, np.float32).astype(ml_dtypes.bfloat16).astype(np.float64), axis, -1)
    blocks = v.reshape(v.shape[:-1] + (-1, 32))
    amax = np.abs(blocks).max(-1, keepdims=True)
    byte = np.maximum(np.where(amax > 0, np.frexp(amax)[1] - 1 + 127, 0) - down, 1)
    scale = np.exp2(byte - 127.0)
    codes = (blocks / scale).astype(np.float32).astype(dtype).astype(np.float64)
    return np.moveaxis((codes * scale).reshape(v.shape), -1, axis)


WIDE = False


def mx_kscale(k):
    if not WIDE:
        return np.ones(k)
    levels = np.array([18, -18])
    if k % 512:
        return np.exp2(np.random.permutation(np.resize(levels, k // 32))).repeat(32)
    a = np.empty((k // 512, 16))
    for p in range(k // 512):
        a[p, :8] = np.random.permutation(np.resize(levels, 8))
        for g in range(8):
            far = levels[np.abs(levels - a[p, g]) >= 10]
            a[p, g + 8] = far[np.random.randint(len(far))]
    return np.exp2(a.ravel()).repeat(32)


def f64(x):
    return np.asarray(x).astype(np.float64)


def striped(idx):
    return np.tile(np.asarray(idx).reshape(-1, 16).T, (8, 1)).astype(np.uint16)


def unstriped(offs):
    return offs[:16].T.reshape(-1).astype(np.int64)

def planes(y):
    n, m = y.shape
    v = y.astype(np.float32).astype(ml_dtypes.bfloat16).astype(np.float64).reshape(n // 32, 32, m)
    top = np.abs(v).max(1)
    byte = np.clip(np.where(top > 0, np.frexp(top)[1] - 1 + 127 - 7, 1), 1, 254)
    codes = (v * np.exp2(127.0 - byte)[:, None, :]).reshape(n, m).astype(np.float32).astype(ml_dtypes.float8_e4m3fn).view(np.uint8)
    words = codes.reshape(n // 512, 128, 4, m).transpose(0, 1, 3, 2)
    return np.ascontiguousarray(words), np.ascontiguousarray(byte.astype(np.uint8).reshape(n // 512, 16, m))


B, N, T, D, R = 1, 512, 2048, 512, 512
LR = 0.1
BETA = 0.9


def setup_inputs():
    n = np.random.standard_normal
    idx = np.random.permutation(T)[:B * N]
    s = mx_kscale(D)[:, None]
    z = mx_kscale(R)[:, None]
    x = n((B, D, R))
    teach = np.exp(n((B, R, N)))
    teach = teach / teach.sum(-1, keepdims=True)
    return {
        "xT": (x * s).astype(np.float32),
        "wT": (n((D, T)) * (0.50 / np.sqrt(D)) / s).astype(np.float32),
        "y": teach.astype(np.float32),
        "wt": (np.random.uniform(0.5, 1.5, (B, R, 1)) * N / np.sqrt(R) * z).astype(np.float32),
        "xm": (x.transpose(0, 2, 1) / z / s[:, 0]).astype(np.float32),
        "mT": (0.3 * n((D, T)) / s).astype(np.float32),
        "offs": striped(idx),
    }


def reference(xT, wT, y, wt, xm, mT, offs):
    idx = unstriped(offs)
    pick = lambda x: x[:, idx].reshape(x.shape[0], B, N).transpose(1, 0, 2)
    w = pick(f64(wT))
    a = mxq(f64(xT), 1, "e4m3").transpose(0, 2, 1) @ mxq(w, 1, "e4m3")
    e = np.exp(a - a.max(-1, keepdims=True))
    g = f64(wt) * (e / e.sum(-1, keepdims=True) - f64(y))
    dw = mxq(f64(xm), 1, "e4m3").transpose(0, 2, 1) @ mxq(g, 1, "e5m2")
    nm = BETA * pick(f64(mT)) + dw
    nw = w - LR * nm
    tables = []
    for old, new in ((wT, nw), (mT, nm),):
        table = f64(old)
        table[:, idx] = new.transpose(1, 0, 2).reshape(D, B * N)
        tables.append(table)
    return tuple(tables) + planes(tables[0])

@@ -1,0 +1,202 @@
+from contextlib import ExitStack
+
+import concourse.mybir as mybir
+
+D, T, N, R = 512, 2048, 512, 512
+LR, BETA = 0.1, 0.9
+FLOPS = 2 * 2 * D * N * R
+
+F32 = mybir.dt.float32
+BF16 = mybir.dt.bfloat16
+I32 = mybir.dt.int32
+U32 = mybir.dt.uint32
+U16 = mybir.dt.uint16
+U8 = mybir.dt.uint8
+E4M3 = mybir.dt.float8_e4m3fn_x4
+E5M2 = mybir.dt.float8_e5m2_x4
+ALU = mybir.AluOpType
+ACT = mybir.ActivationFunctionType
+AXIS = mybir.AxisListType
+
+P = 128
+PACK = 4
+CHUNK = 512
+
+
+def tile_attend_gkl_pl_mom_kernel(tc, xT, wT, y, wt, xm, mT, offs, out_0, out_1, out_2, out_3):
+    nc = tc.nc
+    with ExitStack() as ctx:
+        sb = ctx.enter_context(tc.tile_pool(name="sb", bufs=1))
+        psum = ctx.enter_context(tc.psum_pool(name="psum", bufs=1))
+
+        def tile(shape, dtype, name, tag=None):
+            return sb.tile(shape, dtype, name=name, tag=tag or name, align_bytes=64)
+
+        def plane(table, t):
+            return table.rearrange("(p t) c -> p t c", t=PACK)[:, t, :]
+
+        def quantize(name, grouped, fmt, pieces):
+            width = grouped.shape[1] // PACK
+            codes = tile([P, width], U32, name + "_codes")
+            scales = tile([P, width], U8, name + "_scales")
+            step = width // pieces
+            for a in range(0, width, step):
+                nc.vector.quantize_mx(
+                    out=codes[:, a : a + step].bitcast(fmt),
+                    scales=scales[:, a : a + step],
+                    in_=grouped[:, PACK * a : PACK * (a + step)],
+                )
+            return codes, scales
+
+        offsets = tile([P, N // 16], U16, "offsets")
+        nc.sync.dma_start(offsets[:], offs)
+
+        warm_in = tile([P, 1], F32, "warm_in")
+        warm_out = tile([P, 1], F32, "warm_out")
+        nc.vector.memset(warm_in[:], 0.0)
+        nc.scalar.activation(warm_out[:], warm_in[:], ACT.Exp)
+
+        w_src = [tile([P, T], F32, f"w_src{t}", tag=f"table{t}") for t in range(PACK)]
+        for t in range(PACK):
+            nc.sync.dma_start(w_src[t][:], plane(wT, t))
+        half = R // 2
+        x_rows = xT[0].rearrange("(p t) r -> p t r", t=PACK)
+        x_raw = [tile([P, PACK, half], F32, f"x_raw{h}") for h in range(2)]
+        for h in range(2):
+            nc.sync.dma_start(x_raw[h][:], x_rows[:, :, h * half : (h + 1) * half])
+        wt_sb = tile([P, PACK], F32, "wt_sb")
+        nc.sync.dma_start(wt_sb[:], wt[0].rearrange("(p j) one -> p (j one)", j=PACK))
+        y_sb = tile([P, PACK, N], F32, "y_sb")
+        nc.sync.dma_start(y_sb[:], y[0].rearrange("(p j) i -> p j i", j=PACK))
+        xm_raw = tile([P, PACK, D], F32, "xm_raw")
+        nc.sync.dma_start(xm_raw[:], xm[0].rearrange("(p j) d -> p j d", j=PACK))
+        m_src = [tile([P, T], F32, f"m_src{t}", tag=f"momentum{t}") for t in range(PACK)]
+        for t in range(PACK):
+            nc.sync.dma_start(m_src[t][:], plane(mT, t))
+
+        w_g = tile([P, PACK, N], F32, "w_g")
+        for t in range(PACK):
+            nc.vector.tensor_copy(w_g[:, t, :], w_src[t][:].indirect(offsets[:]))
+        w_dst = [tile([P, T], F32, f"w_dst{t}") for t in range(PACK - 1)]
+        for t in range(PACK - 1):
+            nc.scalar.activation(w_dst[t][:], w_src[t][:], ACT.Copy)
+
+        w_bf = tile([P, N, PACK], BF16, "w_bf")
+        nc.vector.tensor_copy(
+            w_bf[:].rearrange("p (c i) t -> p c t i", i=4),
+            w_g[:].rearrange("p t (c i) -> p c t i", i=4),
+        )
+        w_codes, w_scales = quantize("w", w_bf[:].rearrange("p c t -> p (c t)"), E4M3, 1)
+
+        x_bf = tile([P, PACK, P, PACK], BF16, "x_bf")
+        for h in range(2):
+            nc.scalar.activation(
+                x_bf[:, :, h * (P // 2) : (h + 1) * (P // 2), :].rearrange("p j m t -> p m t j"),
+                x_raw[h][:].rearrange("p t (m j) -> p m t j", j=PACK),
+                ACT.Copy,
+            )
+        x_codes, x_scales = quantize("x", x_bf[:].rearrange("p j m t -> p (j m t)"), E4M3, 1)
+
+        for j in range(PACK):
+            nc.gpsimd.tensor_scalar(y_sb[:, j, :], y_sb[:, j, :], wt_sb[:, j : j + 1], 0.0, ALU.mult, ALU.add)
+
+        neg_max = tile([P, PACK], F32, "neg_max", tag="after_exp")
+        e = tile([P, PACK, N], F32, "e", tag="after_g")
+        sums = tile([P, PACK], F32, "sums")
+        inv = tile([P, PACK], F32, "inv")
+        coef = tile([P, PACK], F32, "coef")
+        g_rows = tile([P, PACK, N], BF16, "g_rows")
+        for j in range(PACK):
+            score = psum.tile([P, N], F32, name=f"score{j}")
+            cols = slice(j * P, (j + 1) * P)
+            nc.tensor.matmul_mx(
+                out=score[:],
+                lhsT=x_codes[:, cols].bitcast(E4M3),
+                lhsT_scale=x_scales[:, cols],
+                rhs=w_codes[:].bitcast(E4M3),
+                rhs_scale=w_scales[:],
+                start=True,
+                stop=True,
+            )
+            nc.vector.tensor_reduce(neg_max[:, j : j + 1], score[:], AXIS.X, ALU.max, negate=True)
+            nc.scalar.activation(
+                e[:, j, :], score[:], ACT.Exp, bias=neg_max[:, j : j + 1], scale=1.0, accum_out=sums[:, j : j + 1]
+            )
+        for a in range(0, PACK, 2):
+            nc.vector.reciprocal(inv[:, a : a + 2], sums[:, a : a + 2])
+            nc.vector.tensor_tensor(coef[:, a : a + 2], inv[:, a : a + 2], wt_sb[:, a : a + 2], ALU.mult)
+            for j in (a, a + 1):
+                nc.vector.scalar_tensor_tensor(
+                    g_rows[:, j, :], e[:, j, :], coef[:, j : j + 1], y_sb[:, j, :], ALU.mult, ALU.subtract
+                )
+
+        xm_bf = tile([P, PACK, P, PACK], BF16, "xm_bf", tag="after_exp")
+        for h in range(2):
+            nc.scalar.activation(
+                xm_bf[:, :, h * (P // 2) : (h + 1) * (P // 2), :].rearrange("p t m j -> p m j t"),
+                xm_raw[:, :, h * (D // 2) : (h + 1) * (D // 2)].rearrange("p j (m t) -> p m j t", t=PACK),
+                ACT.Copy,
+            )
+        g_bf = tile([P, N, PACK], BF16, "g_bf")
+        for a in range(0, N, N // 2):
+            nc.vector.tensor_copy(
+                g_bf[:, a : a + N // 2, :].rearrange("p (c i) j -> p c j i", i=4),
+                g_rows[:, :, a : a + N // 2].rearrange("p j (c i) -> p c j i", i=4),
+            )
+        xm_codes, xm_scales = quantize("xm", xm_bf[:].rearrange("p t m j -> p (t m j)"), E4M3, 1)
+        g_codes, g_scales = quantize("g", g_bf[:].rearrange("p c j -> p (c j)"), E5M2, 2)
+
+        last = tile([P, T], F32, "w_dst3", tag="after_g")
+        nc.scalar.activation(last[:], w_src[PACK - 1][:], ACT.Copy)
+        w_dst.append(last)
+        m_dst = [tile([P, T], F32, f"m_dst{t}", tag=f"table{t}") for t in range(PACK)]
+        for t in range(PACK):
+            nc.sync.dma_start(m_dst[t][:], plane(mT, t))
+
+        m_g = tile([P, PACK, N], F32, "m_g")
+        nm = tile([P, PACK, N], F32, "nm", tag="after_scatters")
+        nw = tile([P, PACK, N], F32, "nw")
+        planes_bf = tile([P, PACK, T], BF16, "planes_bf")
+        for t in range(PACK):
+            dw = psum.tile([P, N], F32, name=f"dw{t}")
+            cols = slice(t * P, (t + 1) * P)
+            nc.tensor.matmul_mx(
+                out=dw[:],
+                lhsT=xm_codes[:, cols].bitcast(E4M3),
+                lhsT_scale=xm_scales[:, cols],
+                rhs=g_codes[:].bitcast(E5M2),
+                rhs_scale=g_scales[:],
+                start=True,
+                stop=True,
+            )
+            nc.vector.tensor_copy(m_g[:, t, :], m_src[t][:].indirect(offsets[:]))
+            nc.vector.scalar_tensor_tensor(nm[:, t, :], m_g[:, t, :], BETA, dw[:], ALU.mult, ALU.add)
+            nc.vector.scalar_tensor_tensor(nw[:, t, :], nm[:, t, :], -LR, w_g[:, t, :], ALU.mult, ALU.add)
+            nc.vector.tensor_copy(w_dst[t][:].indirect(offsets[:]), nw[:, t, :])
+            nc.sync.dma_start(plane(out_0, t), w_dst[t][:])
+            nc.scalar.activation(planes_bf[:, t, :], w_dst[t][:], ACT.Copy)
+
+        for t in range(PACK):
+            nc.vector.tensor_copy(m_dst[t][:].indirect(offsets[:]), nm[:, t, :])
+            nc.sync.dma_start(plane(out_1, t), m_dst[t][:])
+
+        out_codes = tile([P, T], U32, "out_codes", tag="after_scatters")
+        out_scales = tile([P, T], U8, "out_scales")
+        words = out_2[0].rearrange("p c t -> p (c t)").bitcast(I32)
+        for k in range(T // CHUNK):
+            cols = slice(k * CHUNK, (k + 1) * CHUNK)
+            grouped = tile([P, CHUNK, PACK], BF16, f"grouped{k}", tag=f"momentum{k}")
+            nc.scalar.copy(
+                grouped[:].rearrange("p (c i) t -> p c t i", i=4),
+                planes_bf[:, :, cols].rearrange("p t (c i) -> p c t i", i=4),
+            )
+            nc.vector.quantize_mx(
+                out=out_codes[:, cols].bitcast(E4M3),
+                scales=out_scales[:, cols],
+                in_=grouped[:].rearrange("p c t -> p (c t)"),
+            )
+            nc.sync.dma_start(words[:, cols], out_codes[:, cols].bitcast(I32))
+        for q in range(4):
+            nc.sync.dma_start(
+                out_3[0, 4 * q : 4 * q + 4, :].bitcast(I32), out_scales[32 * q : 32 * q + 4, :].bitcast(I32)
+            )

@@ -66,12 +66,15 @@ def tile_attend_gkl_pl_mom_kernel(tc, xT, wT, y, wt, xm, mT, offs, out_0, out_1,
             nc.sync.dma_start(x_raw[h][:], x_rows[:, :, h * half : (h + 1) * half])
         wt_sb = tile([P, PACK], F32, "wt_sb")
         nc.sync.dma_start(wt_sb[:], wt[0].rearrange("(p j) one -> p (j one)", j=PACK))
+        xm_rows = xm[0].rearrange("(p j) d -> p j d", j=PACK)
+        xm_raw = [tile([P, PACK, half], F32, f"xm_raw{h}") for h in range(2)]
         y_sb = tile([P, PACK, N], F32, "y_sb")
-        nc.sync.dma_start(y_sb[:], y[0].rearrange("(p j) i -> p j i", j=PACK))
-        xm_raw = tile([P, PACK, D], F32, "xm_raw")
-        nc.sync.dma_start(xm_raw[:], xm[0].rearrange("(p j) d -> p j d", j=PACK))
         m_src = [tile([P, T], F32, f"m_src{t}", tag=f"momentum{t}") for t in range(PACK)]
-        for t in range(PACK):
+        nc.sync.dma_start(xm_raw[0][:], xm_rows[:, :, :half])
+        nc.sync.dma_start(y_sb[:], y[0].rearrange("(p j) i -> p j i", j=PACK))
+        nc.sync.dma_start(m_src[0][:], plane(mT, 0))
+        nc.sync.dma_start(xm_raw[1][:], xm_rows[:, :, half:])
+        for t in range(1, PACK):
             nc.sync.dma_start(m_src[t][:], plane(mT, t))
 
         w_g = tile([P, PACK, N], F32, "w_g")
@@ -100,12 +103,12 @@ def tile_attend_gkl_pl_mom_kernel(tc, xT, wT, y, wt, xm, mT, offs, out_0, out_1,
         for j in range(PACK):
             nc.gpsimd.tensor_scalar(y_sb[:, j, :], y_sb[:, j, :], wt_sb[:, j : j + 1], 0.0, ALU.mult, ALU.add)
 
-        neg_max = tile([P, PACK], F32, "neg_max", tag="after_exp")
-        e = tile([P, PACK, N], F32, "e", tag="after_g")
+        neg_max = tile([P, PACK], F32, "neg_max")
+        e = tile([P, PACK, N], F32, "e")
         sums = tile([P, PACK], F32, "sums")
         inv = tile([P, PACK], F32, "inv")
         coef = tile([P, PACK], F32, "coef")
-        g_rows = tile([P, PACK, N], BF16, "g_rows")
+        g_rows = tile([P, PACK, N], BF16, "g_rows", tag="after_g")
         for j in range(PACK):
             score = psum.tile([P, N], F32, name=f"score{j}")
             cols = slice(j * P, (j + 1) * P)
@@ -122,24 +125,23 @@ def tile_attend_gkl_pl_mom_kernel(tc, xT, wT, y, wt, xm, mT, offs, out_0, out_1,
             nc.scalar.activation(
                 e[:, j, :], score[:], ACT.Exp, bias=neg_max[:, j : j + 1], scale=1.0, accum_out=sums[:, j : j + 1]
             )
-        for a in range(0, PACK, 2):
-            nc.vector.reciprocal(inv[:, a : a + 2], sums[:, a : a + 2])
-            nc.vector.tensor_tensor(coef[:, a : a + 2], inv[:, a : a + 2], wt_sb[:, a : a + 2], ALU.mult)
-            for j in (a, a + 1):
-                nc.vector.scalar_tensor_tensor(
-                    g_rows[:, j, :], e[:, j, :], coef[:, j : j + 1], y_sb[:, j, :], ALU.mult, ALU.subtract
-                )
+        nc.vector.reciprocal(inv[:], sums[:])
+        nc.vector.tensor_tensor(coef[:], inv[:], wt_sb[:], ALU.mult)
+        for j in range(PACK):
+            nc.vector.scalar_tensor_tensor(
+                g_rows[:, j, :], e[:, j, :], coef[:, j : j + 1], y_sb[:, j, :], ALU.mult, ALU.subtract
+            )
 
-        xm_bf = tile([P, PACK, P, PACK], BF16, "xm_bf", tag="after_exp")
+        xm_bf = tile([P, PACK, P, PACK], BF16, "xm_bf")
         for h in range(2):
             nc.scalar.activation(
                 xm_bf[:, :, h * (P // 2) : (h + 1) * (P // 2), :].rearrange("p t m j -> p m j t"),
-                xm_raw[:, :, h * (D // 2) : (h + 1) * (D // 2)].rearrange("p j (m t) -> p m j t", t=PACK),
+                xm_raw[h][:].rearrange("p j (m t) -> p m j t", t=PACK),
                 ACT.Copy,
             )
         g_bf = tile([P, N, PACK], BF16, "g_bf")
         for a in range(0, N, N // 2):
-            nc.vector.tensor_copy(
+            nc.scalar.copy(
                 g_bf[:, a : a + N // 2, :].rearrange("p (c i) j -> p c j i", i=4),
                 g_rows[:, :, a : a + N // 2].rearrange("p j (c i) -> p c j i", i=4),
             )
@@ -156,7 +158,9 @@ def tile_attend_gkl_pl_mom_kernel(tc, xT, wT, y, wt, xm, mT, offs, out_0, out_1,
         m_g = tile([P, PACK, N], F32, "m_g")
         nm = tile([P, PACK, N], F32, "nm", tag="after_scatters")
         nw = tile([P, PACK, N], F32, "nw")
-        planes_bf = tile([P, PACK, T], BF16, "planes_bf")
+        dw_sb = tile([P, PACK - 1, N], F32, "dw_sb", tag="after_totals")
+        total = tile([P, PACK - 1, N], F32, "total")
+        step = tile([P, PACK - 1, N], F32, "step")
         for t in range(PACK):
             dw = psum.tile([P, N], F32, name=f"dw{t}")
             cols = slice(t * P, (t + 1) * P)
@@ -170,11 +174,22 @@ def tile_attend_gkl_pl_mom_kernel(tc, xT, wT, y, wt, xm, mT, offs, out_0, out_1,
                 stop=True,
             )
             nc.vector.tensor_copy(m_g[:, t, :], m_src[t][:].indirect(offsets[:]))
-            nc.vector.scalar_tensor_tensor(nm[:, t, :], m_g[:, t, :], BETA, dw[:], ALU.mult, ALU.add)
-            nc.vector.scalar_tensor_tensor(nw[:, t, :], nm[:, t, :], -LR, w_g[:, t, :], ALU.mult, ALU.add)
+            if t == 0:
+                nc.vector.scalar_tensor_tensor(nm[:, t, :], m_g[:, t, :], BETA, dw[:], ALU.mult, ALU.add)
+                nc.vector.scalar_tensor_tensor(nw[:, t, :], nm[:, t, :], -LR, w_g[:, t, :], ALU.mult, ALU.add)
+            else:
+                nc.scalar.activation(dw_sb[:, t - 1, :], dw[:], ACT.Copy, scale=1.0 / BETA)
+                nc.gpsimd.tensor_tensor(total[:, t - 1, :], m_g[:, t, :], dw_sb[:, t - 1, :], ALU.add)
+                nc.scalar.activation(step[:, t - 1, :], total[:, t - 1, :], ACT.Copy, scale=-LR * BETA)
+                nc.gpsimd.tensor_tensor(nw[:, t, :], w_g[:, t, :], step[:, t - 1, :], ALU.add)
+        for t in range(1, PACK):
+            nc.gpsimd.tensor_scalar(nm[:, t, :], total[:, t - 1, :], BETA, 0.0, ALU.mult, ALU.add)
+
+        pairs = tile([P, 2, T, 2], BF16, "pairs", tag="after_totals")
+        for t in range(PACK):
             nc.vector.tensor_copy(w_dst[t][:].indirect(offsets[:]), nw[:, t, :])
             nc.sync.dma_start(plane(out_0, t), w_dst[t][:])
-            nc.scalar.activation(planes_bf[:, t, :], w_dst[t][:], ACT.Copy)
+            nc.scalar.activation(pairs[:, t // 2, :, t % 2], w_dst[t][:], ACT.Copy)
 
         for t in range(PACK):
             nc.vector.tensor_copy(m_dst[t][:].indirect(offsets[:]), nm[:, t, :])
@@ -183,17 +198,18 @@ def tile_attend_gkl_pl_mom_kernel(tc, xT, wT, y, wt, xm, mT, offs, out_0, out_1,
         out_codes = tile([P, T], U32, "out_codes", tag="after_scatters")
         out_scales = tile([P, T], U8, "out_scales")
         words = out_2[0].rearrange("p c t -> p (c t)").bitcast(I32)
+        pair_words = pairs[:].rearrange("p u c e -> p (u c e)").bitcast(U32).rearrange("p (u c) -> p u c", u=2)
         for k in range(T // CHUNK):
             cols = slice(k * CHUNK, (k + 1) * CHUNK)
-            grouped = tile([P, CHUNK, PACK], BF16, f"grouped{k}", tag=f"momentum{k}")
+            grouped = tile([P, CHUNK * PACK], BF16, f"grouped{k}", tag=f"momentum{k}")
             nc.scalar.copy(
-                grouped[:].rearrange("p (c i) t -> p c t i", i=4),
-                planes_bf[:, :, cols].rearrange("p t (c i) -> p c t i", i=4),
+                grouped[:].bitcast(U32).rearrange("p (c u) -> p c u", u=2),
+                pair_words[:, :, cols].rearrange("p u c -> p c u"),
             )
             nc.vector.quantize_mx(
                 out=out_codes[:, cols].bitcast(E4M3),
                 scales=out_scales[:, cols],
-                in_=grouped[:].rearrange("p c t -> p (c t)"),
+                in_=grouped[:],
             )
             nc.sync.dma_start(words[:, cols], out_codes[:, cols].bitcast(I32))
         for q in range(4):

@@ -66,14 +66,12 @@ def tile_attend_gkl_pl_mom_kernel(tc, xT, wT, y, wt, xm, mT, offs, out_0, out_1,
             nc.sync.dma_start(x_raw[h][:], x_rows[:, :, h * half : (h + 1) * half])
         wt_sb = tile([P, PACK], F32, "wt_sb")
         nc.sync.dma_start(wt_sb[:], wt[0].rearrange("(p j) one -> p (j one)", j=PACK))
-        xm_rows = xm[0].rearrange("(p j) d -> p j d", j=PACK)
-        xm_raw = [tile([P, PACK, half], F32, f"xm_raw{h}") for h in range(2)]
+        xm_raw = tile([P, PACK, D], F32, "xm_raw")
         y_sb = tile([P, PACK, N], F32, "y_sb")
         m_src = [tile([P, T], F32, f"m_src{t}", tag=f"momentum{t}") for t in range(PACK)]
-        nc.sync.dma_start(xm_raw[0][:], xm_rows[:, :, :half])
         nc.sync.dma_start(y_sb[:], y[0].rearrange("(p j) i -> p j i", j=PACK))
         nc.sync.dma_start(m_src[0][:], plane(mT, 0))
-        nc.sync.dma_start(xm_raw[1][:], xm_rows[:, :, half:])
+        nc.sync.dma_start(xm_raw[:], xm[0].rearrange("(p j) d -> p j d", j=PACK))
         for t in range(1, PACK):
             nc.sync.dma_start(m_src[t][:], plane(mT, t))
 
@@ -98,13 +96,13 @@ def tile_attend_gkl_pl_mom_kernel(tc, xT, wT, y, wt, xm, mT, offs, out_0, out_1,
                 x_raw[h][:].rearrange("p t (m j) -> p m t j", j=PACK),
                 ACT.Copy,
             )
-        x_codes, x_scales = quantize("x", x_bf[:].rearrange("p j m t -> p (j m t)"), E4M3, 1)
+        x_codes, x_scales = quantize("x", x_bf[:].rearrange("p j m t -> p (j m t)"), E4M3, PACK)
 
         for j in range(PACK):
             nc.gpsimd.tensor_scalar(y_sb[:, j, :], y_sb[:, j, :], wt_sb[:, j : j + 1], 0.0, ALU.mult, ALU.add)
 
         neg_max = tile([P, PACK], F32, "neg_max")
-        e = tile([P, PACK, N], F32, "e")
+        e = tile([P, PACK, N], F32, "e", tag="after_rows")
         sums = tile([P, PACK], F32, "sums")
         inv = tile([P, PACK], F32, "inv")
         coef = tile([P, PACK], F32, "coef")
@@ -136,10 +134,10 @@ def tile_attend_gkl_pl_mom_kernel(tc, xT, wT, y, wt, xm, mT, offs, out_0, out_1,
         for h in range(2):
             nc.scalar.activation(
                 xm_bf[:, :, h * (P // 2) : (h + 1) * (P // 2), :].rearrange("p t m j -> p m j t"),
-                xm_raw[h][:].rearrange("p j (m t) -> p m j t", t=PACK),
+                xm_raw[:, :, h * (D // 2) : (h + 1) * (D // 2)].rearrange("p j (m t) -> p m j t", t=PACK),
                 ACT.Copy,
             )
-        g_bf = tile([P, N, PACK], BF16, "g_bf")
+        g_bf = tile([P, N, PACK], BF16, "g_bf", tag="after_g_codes")
         for a in range(0, N, N // 2):
             nc.scalar.copy(
                 g_bf[:, a : a + N // 2, :].rearrange("p (c i) j -> p c j i", i=4),
@@ -155,17 +153,20 @@ def tile_attend_gkl_pl_mom_kernel(tc, xT, wT, y, wt, xm, mT, offs, out_0, out_1,
         for t in range(PACK):
             nc.sync.dma_start(m_dst[t][:], plane(mT, t))
 
-        m_g = tile([P, PACK, N], F32, "m_g")
-        nm = tile([P, PACK, N], F32, "nm", tag="after_scatters")
-        nw = tile([P, PACK, N], F32, "nw")
-        dw_sb = tile([P, PACK - 1, N], F32, "dw_sb", tag="after_totals")
-        total = tile([P, PACK - 1, N], F32, "total")
-        step = tile([P, PACK - 1, N], F32, "step")
+        m_tags = [None, None, None, "after_g_codes"]
+        m_g = [tile([P, N], F32, f"m_g{t}", tag=m_tags[t]) for t in range(PACK - 1)]
+        nw = [tile([P, N], F32, f"nw{t}") for t in range(PACK)]
+        total = tile([P, PACK, N], F32, "total")
+        for t in range(PACK - 1):
+            nc.vector.tensor_copy(m_g[t][:], m_src[t][:].indirect(offsets[:]))
+        base = tile([P, N], F32, "base", tag="after_rows")
+        nc.vector.scalar_tensor_tensor(base[:], m_g[0][:], -LR * BETA, w_g[:, 0, :], ALU.mult, ALU.add)
+        dw = []
         for t in range(PACK):
-            dw = psum.tile([P, N], F32, name=f"dw{t}")
+            bank = psum.tile([P, N], F32, name=f"dw{t}")
             cols = slice(t * P, (t + 1) * P)
             nc.tensor.matmul_mx(
-                out=dw[:],
+                out=bank[:],
                 lhsT=xm_codes[:, cols].bitcast(E4M3),
                 lhsT_scale=xm_scales[:, cols],
                 rhs=g_codes[:].bitcast(E5M2),
@@ -173,21 +174,30 @@ def tile_attend_gkl_pl_mom_kernel(tc, xT, wT, y, wt, xm, mT, offs, out_0, out_1,
                 start=True,
                 stop=True,
             )
-            nc.vector.tensor_copy(m_g[:, t, :], m_src[t][:].indirect(offsets[:]))
-            if t == 0:
-                nc.vector.scalar_tensor_tensor(nm[:, t, :], m_g[:, t, :], BETA, dw[:], ALU.mult, ALU.add)
-                nc.vector.scalar_tensor_tensor(nw[:, t, :], nm[:, t, :], -LR, w_g[:, t, :], ALU.mult, ALU.add)
-            else:
-                nc.scalar.activation(dw_sb[:, t - 1, :], dw[:], ACT.Copy, scale=1.0 / BETA)
-                nc.gpsimd.tensor_tensor(total[:, t - 1, :], m_g[:, t, :], dw_sb[:, t - 1, :], ALU.add)
-                nc.scalar.activation(step[:, t - 1, :], total[:, t - 1, :], ACT.Copy, scale=-LR * BETA)
-                nc.gpsimd.tensor_tensor(nw[:, t, :], w_g[:, t, :], step[:, t - 1, :], ALU.add)
+            dw.append(bank)
+        nc.vector.scalar_tensor_tensor(nw[0][:], dw[0][:], -LR, base[:], ALU.mult, ALU.add)
+        nc.vector.tensor_copy(w_dst[0][:].indirect(offsets[:]), nw[0][:])
+        m_last = tile([P, N], F32, "m_g3", tag=m_tags[3])
+        nc.vector.tensor_copy(m_last[:], m_src[PACK - 1][:].indirect(offsets[:]))
+        m_g.append(m_last)
         for t in range(1, PACK):
-            nc.gpsimd.tensor_scalar(nm[:, t, :], total[:, t - 1, :], BETA, 0.0, ALU.mult, ALU.add)
+            dw_sb = tile([P, N], F32, f"dw_sb{t}", tag="after_totals" if t == 3 else None)
+            nc.scalar.activation(dw_sb[:], dw[t][:], ACT.Copy, scale=1.0 / BETA)
+            nc.gpsimd.tensor_tensor(total[:, t, :], m_g[t][:], dw_sb[:], ALU.add)
+            step = tile([P, N], F32, f"step{t}", tag={1: "after_totals", 3: "after_scatters"}.get(t))
+            nc.scalar.activation(step[:], total[:, t, :], ACT.Copy, scale=-LR * BETA)
+            nc.gpsimd.tensor_tensor(nw[t][:], w_g[:, t, :], step[:], ALU.add)
+        dw_first = tile([P, N], F32, "dw_sb0")
+        nc.scalar.activation(dw_first[:], dw[0][:], ACT.Copy, scale=1.0 / BETA)
+        nc.gpsimd.tensor_tensor(total[:, 0, :], m_g[0][:], dw_first[:], ALU.add)
+        nm = tile([P, PACK, N], F32, "nm", tag="after_scatters")
+        for t in range(PACK):
+            nc.gpsimd.tensor_scalar(nm[:, t, :], total[:, t, :], BETA, 0.0, ALU.mult, ALU.add)
 
         pairs = tile([P, 2, T, 2], BF16, "pairs", tag="after_totals")
         for t in range(PACK):
-            nc.vector.tensor_copy(w_dst[t][:].indirect(offsets[:]), nw[:, t, :])
+            if t > 0:
+                nc.vector.tensor_copy(w_dst[t][:].indirect(offsets[:]), nw[t][:])
             nc.sync.dma_start(plane(out_0, t), w_dst[t][:])
             nc.scalar.activation(pairs[:, t // 2, :, t % 2], w_dst[t][:], ACT.Copy)
 

@@ -35,9 +35,8 @@ def tile_attend_gkl_pl_mom_kernel(tc, xT, wT, y, wt, xm, mT, offs, out_0, out_1,
         def plane(table, t):
             return table.rearrange("(p t) c -> p t c", t=PACK)[:, t, :]
 
-        def quantize(name, grouped, fmt, pieces):
+        def quantize(name, grouped, fmt, pieces, codes):
             width = grouped.shape[1] // PACK
-            codes = tile([P, width], U32, name + "_codes")
             scales = tile([P, width], U8, name + "_scales")
             step = width // pieces
             for a in range(0, width, step):
@@ -87,7 +86,7 @@ def tile_attend_gkl_pl_mom_kernel(tc, xT, wT, y, wt, xm, mT, offs, out_0, out_1,
             w_bf[:].rearrange("p (c i) t -> p c t i", i=4),
             w_g[:].rearrange("p t (c i) -> p c t i", i=4),
         )
-        w_codes, w_scales = quantize("w", w_bf[:].rearrange("p c t -> p (c t)"), E4M3, 1)
+        w_codes, w_scales = quantize("w", w_bf[:].rearrange("p c t -> p (c t)"), E4M3, 1, tile([P, N], U32, "w_codes"))
 
         x_bf = tile([P, PACK, P, PACK], BF16, "x_bf")
         for h in range(2):
@@ -96,7 +95,7 @@ def tile_attend_gkl_pl_mom_kernel(tc, xT, wT, y, wt, xm, mT, offs, out_0, out_1,
                 x_raw[h][:].rearrange("p t (m j) -> p m t j", j=PACK),
                 ACT.Copy,
             )
-        x_codes, x_scales = quantize("x", x_bf[:].rearrange("p j m t -> p (j m t)"), E4M3, PACK)
+        x_codes, x_scales = quantize("x", x_bf[:].rearrange("p j m t -> p (j m t)"), E4M3, PACK, tile([P, R], U32, "x_codes"))
 
         for j in range(PACK):
             nc.gpsimd.tensor_scalar(y_sb[:, j, :], y_sb[:, j, :], wt_sb[:, j : j + 1], 0.0, ALU.mult, ALU.add)
@@ -143,8 +142,12 @@ def tile_attend_gkl_pl_mom_kernel(tc, xT, wT, y, wt, xm, mT, offs, out_0, out_1,
                 g_bf[:, a : a + N // 2, :].rearrange("p (c i) j -> p c j i", i=4),
                 g_rows[:, :, a : a + N // 2].rearrange("p j (c i) -> p c j i", i=4),
             )
-        xm_codes, xm_scales = quantize("xm", xm_bf[:].rearrange("p t m j -> p (t m j)"), E4M3, 1)
-        g_codes, g_scales = quantize("g", g_bf[:].rearrange("p c j -> p (c j)"), E5M2, 2)
+        m_g = [tile([P, N], F32, f"m_g{t}") for t in range(PACK - 1)]
+        for t in range(PACK - 1):
+            nc.vector.tensor_copy(m_g[t][:], m_src[t][:].indirect(offsets[:]))
+        second = tile([P, D + N], U32, "second", tag="momentum2")
+        xm_codes, xm_scales = quantize("xm", xm_bf[:].rearrange("p t m j -> p (t m j)"), E4M3, 1, second[:, :D])
+        g_codes, g_scales = quantize("g", g_bf[:].rearrange("p c j -> p (c j)"), E5M2, 2, second[:, D:])
 
         last = tile([P, T], F32, "w_dst3", tag="after_g")
         nc.scalar.activation(last[:], w_src[PACK - 1][:], ACT.Copy)
@@ -153,41 +156,39 @@ def tile_attend_gkl_pl_mom_kernel(tc, xT, wT, y, wt, xm, mT, offs, out_0, out_1,
         for t in range(PACK):
             nc.sync.dma_start(m_dst[t][:], plane(mT, t))
 
-        m_tags = [None, None, None, "after_g_codes"]
-        m_g = [tile([P, N], F32, f"m_g{t}", tag=m_tags[t]) for t in range(PACK - 1)]
-        nw = [tile([P, N], F32, f"nw{t}") for t in range(PACK)]
+        m_last = tile([P, N], F32, "m_g3", tag="after_g_codes")
+        nc.vector.tensor_copy(m_last[:], m_src[PACK - 1][:].indirect(offsets[:]))
+        m_g.append(m_last)
+        nw = [tile([P, N], F32, f"nw{t}", tag="momentum3" if t == 0 else None) for t in range(PACK)]
         total = tile([P, PACK, N], F32, "total")
-        for t in range(PACK - 1):
-            nc.vector.tensor_copy(m_g[t][:], m_src[t][:].indirect(offsets[:]))
-        base = tile([P, N], F32, "base", tag="after_rows")
-        nc.vector.scalar_tensor_tensor(base[:], m_g[0][:], -LR * BETA, w_g[:, 0, :], ALU.mult, ALU.add)
-        dw = []
-        for t in range(PACK):
+        decay = tile([P, N], F32, "decay", tag="after_rows")
+        nc.gpsimd.tensor_scalar(decay[:], m_g[0][:], -LR * BETA, 0.0, ALU.mult, ALU.add)
+        base = tile([P, N], F32, "base")
+        nc.gpsimd.tensor_tensor(base[:], decay[:], w_g[:, 0, :], ALU.add)
+        dw = {}
+        for t in (1, 0, 2, 3):
             bank = psum.tile([P, N], F32, name=f"dw{t}")
             cols = slice(t * P, (t + 1) * P)
             nc.tensor.matmul_mx(
                 out=bank[:],
                 lhsT=xm_codes[:, cols].bitcast(E4M3),
                 lhsT_scale=xm_scales[:, cols],
-                rhs=g_codes[:].bitcast(E5M2),
+                rhs=g_codes.bitcast(E5M2),
                 rhs_scale=g_scales[:],
                 start=True,
                 stop=True,
             )
-            dw.append(bank)
+            dw[t] = bank
         nc.vector.scalar_tensor_tensor(nw[0][:], dw[0][:], -LR, base[:], ALU.mult, ALU.add)
         nc.vector.tensor_copy(w_dst[0][:].indirect(offsets[:]), nw[0][:])
-        m_last = tile([P, N], F32, "m_g3", tag=m_tags[3])
-        nc.vector.tensor_copy(m_last[:], m_src[PACK - 1][:].indirect(offsets[:]))
-        m_g.append(m_last)
         for t in range(1, PACK):
             dw_sb = tile([P, N], F32, f"dw_sb{t}", tag="after_totals" if t == 3 else None)
             nc.scalar.activation(dw_sb[:], dw[t][:], ACT.Copy, scale=1.0 / BETA)
             nc.gpsimd.tensor_tensor(total[:, t, :], m_g[t][:], dw_sb[:], ALU.add)
-            step = tile([P, N], F32, f"step{t}", tag={1: "after_totals", 3: "after_scatters"}.get(t))
+            step = tile([P, N], F32, f"step{t}", tag={1: "after_totals", 2: "after_third", 3: "after_scatters"}[t])
             nc.scalar.activation(step[:], total[:, t, :], ACT.Copy, scale=-LR * BETA)
             nc.gpsimd.tensor_tensor(nw[t][:], w_g[:, t, :], step[:], ALU.add)
-        dw_first = tile([P, N], F32, "dw_sb0")
+        dw_first = tile([P, N], F32, "dw_sb0", tag="after_third")
         nc.scalar.activation(dw_first[:], dw[0][:], ACT.Copy, scale=1.0 / BETA)
         nc.gpsimd.tensor_tensor(total[:, 0, :], m_g[0][:], dw_first[:], ALU.add)
         nm = tile([P, PACK, N], F32, "nm", tag="after_scatters")

@@ -35,8 +35,9 @@ def tile_attend_gkl_pl_mom_kernel(tc, xT, wT, y, wt, xm, mT, offs, out_0, out_1,
         def plane(table, t):
             return table.rearrange("(p t) c -> p t c", t=PACK)[:, t, :]
 
-        def quantize(name, grouped, fmt, pieces, codes):
+        def quantize(name, grouped, fmt, pieces, tag=None):
             width = grouped.shape[1] // PACK
+            codes = tile([P, width], U32, name + "_codes", tag=tag)
             scales = tile([P, width], U8, name + "_scales")
             step = width // pieces
             for a in range(0, width, step):
@@ -48,16 +49,17 @@ def tile_attend_gkl_pl_mom_kernel(tc, xT, wT, y, wt, xm, mT, offs, out_0, out_1,
             return codes, scales
 
         offsets = tile([P, N // 16], U16, "offsets")
+        w_src = [tile([P, T], F32, f"w_src{t}", tag=f"table{t}") for t in range(PACK)]
+        nc.sync.dma_start(w_src[0][:], plane(wT, 0))
         nc.sync.dma_start(offsets[:], offs)
+        for t in range(1, PACK):
+            nc.sync.dma_start(w_src[t][:], plane(wT, t))
 
         warm_in = tile([P, 1], F32, "warm_in")
         warm_out = tile([P, 1], F32, "warm_out")
         nc.vector.memset(warm_in[:], 0.0)
         nc.scalar.activation(warm_out[:], warm_in[:], ACT.Exp)
 
-        w_src = [tile([P, T], F32, f"w_src{t}", tag=f"table{t}") for t in range(PACK)]
-        for t in range(PACK):
-            nc.sync.dma_start(w_src[t][:], plane(wT, t))
         half = R // 2
         x_rows = xT[0].rearrange("(p t) r -> p t r", t=PACK)
         x_raw = [tile([P, PACK, half], F32, f"x_raw{h}") for h in range(2)]
@@ -69,9 +71,8 @@ def tile_attend_gkl_pl_mom_kernel(tc, xT, wT, y, wt, xm, mT, offs, out_0, out_1,
         y_sb = tile([P, PACK, N], F32, "y_sb")
         m_src = [tile([P, T], F32, f"m_src{t}", tag=f"momentum{t}") for t in range(PACK)]
         nc.sync.dma_start(y_sb[:], y[0].rearrange("(p j) i -> p j i", j=PACK))
-        nc.sync.dma_start(m_src[0][:], plane(mT, 0))
         nc.sync.dma_start(xm_raw[:], xm[0].rearrange("(p j) d -> p j d", j=PACK))
-        for t in range(1, PACK):
+        for t in range(PACK):
             nc.sync.dma_start(m_src[t][:], plane(mT, t))
 
         w_g = tile([P, PACK, N], F32, "w_g")
@@ -86,7 +87,7 @@ def tile_attend_gkl_pl_mom_kernel(tc, xT, wT, y, wt, xm, mT, offs, out_0, out_1,
             w_bf[:].rearrange("p (c i) t -> p c t i", i=4),
             w_g[:].rearrange("p t (c i) -> p c t i", i=4),
         )
-        w_codes, w_scales = quantize("w", w_bf[:].rearrange("p c t -> p (c t)"), E4M3, 1, tile([P, N], U32, "w_codes"))
+        w_codes, w_scales = quantize("w", w_bf[:].rearrange("p c t -> p (c t)"), E4M3, 1)
 
         x_bf = tile([P, PACK, P, PACK], BF16, "x_bf")
         for h in range(2):
@@ -95,17 +96,23 @@ def tile_attend_gkl_pl_mom_kernel(tc, xT, wT, y, wt, xm, mT, offs, out_0, out_1,
                 x_raw[h][:].rearrange("p t (m j) -> p m t j", j=PACK),
                 ACT.Copy,
             )
-        x_codes, x_scales = quantize("x", x_bf[:].rearrange("p j m t -> p (j m t)"), E4M3, PACK, tile([P, R], U32, "x_codes"))
+        x_codes, x_scales = quantize("x", x_bf[:].rearrange("p j m t -> p (j m t)"), E4M3, PACK)
+        last = tile([P, T], F32, "w_dst3", tag="x_raw1")
+        nc.scalar.activation(last[:], w_src[PACK - 1][:], ACT.Copy)
+        w_dst.append(last)
+        m_dst = [tile([P, T], F32, f"m_dst{t}", tag=f"table{t}") for t in range(PACK)]
+        for t in range(PACK):
+            nc.sync.dma_start(m_dst[t][:], plane(mT, t))
 
         for j in range(PACK):
             nc.gpsimd.tensor_scalar(y_sb[:, j, :], y_sb[:, j, :], wt_sb[:, j : j + 1], 0.0, ALU.mult, ALU.add)
 
         neg_max = tile([P, PACK], F32, "neg_max")
-        e = tile([P, PACK, N], F32, "e", tag="after_rows")
+        e = tile([P, PACK, N], F32, "e")
         sums = tile([P, PACK], F32, "sums")
         inv = tile([P, PACK], F32, "inv")
         coef = tile([P, PACK], F32, "coef")
-        g_rows = tile([P, PACK, N], BF16, "g_rows", tag="after_g")
+        g_rows = tile([P, PACK, N], BF16, "g_rows")
         for j in range(PACK):
             score = psum.tile([P, N], F32, name=f"score{j}")
             cols = slice(j * P, (j + 1) * P)
@@ -122,12 +129,13 @@ def tile_attend_gkl_pl_mom_kernel(tc, xT, wT, y, wt, xm, mT, offs, out_0, out_1,
             nc.scalar.activation(
                 e[:, j, :], score[:], ACT.Exp, bias=neg_max[:, j : j + 1], scale=1.0, accum_out=sums[:, j : j + 1]
             )
-        nc.vector.reciprocal(inv[:], sums[:])
-        nc.vector.tensor_tensor(coef[:], inv[:], wt_sb[:], ALU.mult)
-        for j in range(PACK):
-            nc.vector.scalar_tensor_tensor(
-                g_rows[:, j, :], e[:, j, :], coef[:, j : j + 1], y_sb[:, j, :], ALU.mult, ALU.subtract
-            )
+        for a in range(0, PACK, 2):
+            nc.vector.reciprocal(inv[:, a : a + 2], sums[:, a : a + 2])
+            nc.vector.tensor_tensor(coef[:, a : a + 2], inv[:, a : a + 2], wt_sb[:, a : a + 2], ALU.mult)
+            for j in (a, a + 1):
+                nc.vector.scalar_tensor_tensor(
+                    g_rows[:, j, :], e[:, j, :], coef[:, j : j + 1], y_sb[:, j, :], ALU.mult, ALU.subtract
+                )
 
         xm_bf = tile([P, PACK, P, PACK], BF16, "xm_bf")
         for h in range(2):
@@ -136,77 +144,53 @@ def tile_attend_gkl_pl_mom_kernel(tc, xT, wT, y, wt, xm, mT, offs, out_0, out_1,
                 xm_raw[:, :, h * (D // 2) : (h + 1) * (D // 2)].rearrange("p j (m t) -> p m j t", t=PACK),
                 ACT.Copy,
             )
-        g_bf = tile([P, N, PACK], BF16, "g_bf", tag="after_g_codes")
+        g_bf = tile([P, N, PACK], BF16, "g_bf")
         for a in range(0, N, N // 2):
             nc.scalar.copy(
                 g_bf[:, a : a + N // 2, :].rearrange("p (c i) j -> p c j i", i=4),
                 g_rows[:, :, a : a + N // 2].rearrange("p j (c i) -> p c j i", i=4),
             )
-        m_g = [tile([P, N], F32, f"m_g{t}") for t in range(PACK - 1)]
-        for t in range(PACK - 1):
-            nc.vector.tensor_copy(m_g[t][:], m_src[t][:].indirect(offsets[:]))
-        second = tile([P, D + N], U32, "second", tag="momentum2")
-        xm_codes, xm_scales = quantize("xm", xm_bf[:].rearrange("p t m j -> p (t m j)"), E4M3, 1, second[:, :D])
-        g_codes, g_scales = quantize("g", g_bf[:].rearrange("p c j -> p (c j)"), E5M2, 2, second[:, D:])
-
-        last = tile([P, T], F32, "w_dst3", tag="after_g")
-        nc.scalar.activation(last[:], w_src[PACK - 1][:], ACT.Copy)
-        w_dst.append(last)
-        m_dst = [tile([P, T], F32, f"m_dst{t}", tag=f"table{t}") for t in range(PACK)]
+        decayed = [tile([P, N], F32, f"decayed{t}") for t in range(PACK)]
         for t in range(PACK):
-            nc.sync.dma_start(m_dst[t][:], plane(mT, t))
+            nc.vector.tensor_scalar(decayed[t][:], m_src[t][:].indirect(offsets[:]), BETA, 0.0, ALU.mult, ALU.add)
+        xm_codes, xm_scales = quantize("xm", xm_bf[:].rearrange("p t m j -> p (t m j)"), E4M3, 1, "momentum0")
+        g_codes, g_scales = quantize("g", g_bf[:].rearrange("p c j -> p (c j)"), E5M2, 2, "momentum1")
+        base = [tile([P, N], F32, f"base{t}", tag="momentum2" if t == 0 else None) for t in range(PACK)]
+        for t in range(PACK):
+            nc.vector.scalar_tensor_tensor(base[t][:], decayed[t][:], -LR, w_g[:, t, :], ALU.mult, ALU.add)
 
-        m_last = tile([P, N], F32, "m_g3", tag="after_g_codes")
-        nc.vector.tensor_copy(m_last[:], m_src[PACK - 1][:].indirect(offsets[:]))
-        m_g.append(m_last)
-        nw = [tile([P, N], F32, f"nw{t}", tag="momentum3" if t == 0 else None) for t in range(PACK)]
-        total = tile([P, PACK, N], F32, "total")
-        decay = tile([P, N], F32, "decay", tag="after_rows")
-        nc.gpsimd.tensor_scalar(decay[:], m_g[0][:], -LR * BETA, 0.0, ALU.mult, ALU.add)
-        base = tile([P, N], F32, "base")
-        nc.gpsimd.tensor_tensor(base[:], decay[:], w_g[:, 0, :], ALU.add)
-        dw = {}
-        for t in (1, 0, 2, 3):
+        dw = []
+        for t in range(PACK):
             bank = psum.tile([P, N], F32, name=f"dw{t}")
             cols = slice(t * P, (t + 1) * P)
             nc.tensor.matmul_mx(
                 out=bank[:],
                 lhsT=xm_codes[:, cols].bitcast(E4M3),
                 lhsT_scale=xm_scales[:, cols],
-                rhs=g_codes.bitcast(E5M2),
+                rhs=g_codes[:].bitcast(E5M2),
                 rhs_scale=g_scales[:],
                 start=True,
                 stop=True,
             )
-            dw[t] = bank
-        nc.vector.scalar_tensor_tensor(nw[0][:], dw[0][:], -LR, base[:], ALU.mult, ALU.add)
-        nc.vector.tensor_copy(w_dst[0][:].indirect(offsets[:]), nw[0][:])
-        for t in range(1, PACK):
-            dw_sb = tile([P, N], F32, f"dw_sb{t}", tag="after_totals" if t == 3 else None)
-            nc.scalar.activation(dw_sb[:], dw[t][:], ACT.Copy, scale=1.0 / BETA)
-            nc.gpsimd.tensor_tensor(total[:, t, :], m_g[t][:], dw_sb[:], ALU.add)
-            step = tile([P, N], F32, f"step{t}", tag={1: "after_totals", 2: "after_third", 3: "after_scatters"}[t])
-            nc.scalar.activation(step[:], total[:, t, :], ACT.Copy, scale=-LR * BETA)
-            nc.gpsimd.tensor_tensor(nw[t][:], w_g[:, t, :], step[:], ALU.add)
-        dw_first = tile([P, N], F32, "dw_sb0", tag="after_third")
-        nc.scalar.activation(dw_first[:], dw[0][:], ACT.Copy, scale=1.0 / BETA)
-        nc.gpsimd.tensor_tensor(total[:, 0, :], m_g[0][:], dw_first[:], ALU.add)
-        nm = tile([P, PACK, N], F32, "nm", tag="after_scatters")
+            dw.append(bank)
+        step = [tile([P, N], F32, f"step{t}") for t in range(PACK)]
+        grad = [tile([P, N], F32, f"grad{t}") for t in range(PACK)]
         for t in range(PACK):
-            nc.gpsimd.tensor_scalar(nm[:, t, :], total[:, t, :], BETA, 0.0, ALU.mult, ALU.add)
+            nc.scalar.activation(step[t][:], dw[t][:], ACT.Copy, scale=-LR)
+        for t in range(PACK):
+            nc.scalar.activation(grad[t][:], dw[t][:], ACT.Copy)
 
-        pairs = tile([P, 2, T, 2], BF16, "pairs", tag="after_totals")
+        pairs = tile([P, 2, T, 2], BF16, "pairs")
         for t in range(PACK):
-            if t > 0:
-                nc.vector.tensor_copy(w_dst[t][:].indirect(offsets[:]), nw[t][:])
+            nc.vector.tensor_tensor(w_dst[t][:].indirect(offsets[:]), base[t][:], step[t][:], ALU.add)
             nc.sync.dma_start(plane(out_0, t), w_dst[t][:])
             nc.scalar.activation(pairs[:, t // 2, :, t % 2], w_dst[t][:], ACT.Copy)
 
         for t in range(PACK):
-            nc.vector.tensor_copy(m_dst[t][:].indirect(offsets[:]), nm[:, t, :])
+            nc.vector.tensor_tensor(m_dst[t][:].indirect(offsets[:]), decayed[t][:], grad[t][:], ALU.add)
             nc.sync.dma_start(plane(out_1, t), m_dst[t][:])
 
-        out_codes = tile([P, T], U32, "out_codes", tag="after_scatters")
+        out_codes = tile([P, T], U32, "out_codes", tag="grad3")
         out_scales = tile([P, T], U8, "out_scales")
         words = out_2[0].rearrange("p c t -> p (c t)").bitcast(I32)
         pair_words = pairs[:].rearrange("p u c e -> p (u c e)").bitcast(U32).rearrange("p (u c) -> p u c", u=2)

@@ -71,8 +71,9 @@ def tile_attend_gkl_pl_mom_kernel(tc, xT, wT, y, wt, xm, mT, offs, out_0, out_1,
         y_sb = tile([P, PACK, N], F32, "y_sb")
         m_src = [tile([P, T], F32, f"m_src{t}", tag=f"momentum{t}") for t in range(PACK)]
         nc.sync.dma_start(y_sb[:], y[0].rearrange("(p j) i -> p j i", j=PACK))
+        nc.sync.dma_start(m_src[0][:], plane(mT, 0))
         nc.sync.dma_start(xm_raw[:], xm[0].rearrange("(p j) d -> p j d", j=PACK))
-        for t in range(PACK):
+        for t in range(1, PACK):
             nc.sync.dma_start(m_src[t][:], plane(mT, t))
 
         w_g = tile([P, PACK, N], F32, "w_g")
@@ -110,8 +111,6 @@ def tile_attend_gkl_pl_mom_kernel(tc, xT, wT, y, wt, xm, mT, offs, out_0, out_1,
         neg_max = tile([P, PACK], F32, "neg_max")
         e = tile([P, PACK, N], F32, "e")
         sums = tile([P, PACK], F32, "sums")
-        inv = tile([P, PACK], F32, "inv")
-        coef = tile([P, PACK], F32, "coef")
         g_rows = tile([P, PACK, N], BF16, "g_rows")
         for j in range(PACK):
             score = psum.tile([P, N], F32, name=f"score{j}")
@@ -129,13 +128,24 @@ def tile_attend_gkl_pl_mom_kernel(tc, xT, wT, y, wt, xm, mT, offs, out_0, out_1,
             nc.scalar.activation(
                 e[:, j, :], score[:], ACT.Exp, bias=neg_max[:, j : j + 1], scale=1.0, accum_out=sums[:, j : j + 1]
             )
-        for a in range(0, PACK, 2):
-            nc.vector.reciprocal(inv[:, a : a + 2], sums[:, a : a + 2])
-            nc.vector.tensor_tensor(coef[:, a : a + 2], inv[:, a : a + 2], wt_sb[:, a : a + 2], ALU.mult)
-            for j in (a, a + 1):
-                nc.vector.scalar_tensor_tensor(
-                    g_rows[:, j, :], e[:, j, :], coef[:, j : j + 1], y_sb[:, j, :], ALU.mult, ALU.subtract
-                )
+        drift = [tile([P, N], F32, "drift0")]
+        inv_early = tile([P, 2], F32, "inv_early")
+        nc.vector.reciprocal(inv_early[:], sums[:, :2])
+        nc.vector.tensor_scalar(drift[0][:], m_src[0][:].indirect(offsets[:]), -LR * BETA, 0.0, ALU.mult, ALU.add)
+        factors = tile([P, PACK + 2], F32, "factors", tag="momentum0")
+        coef, inv_late = factors[:, :PACK], factors[:, PACK:]
+
+        def gradient_rows(j):
+            nc.vector.scalar_tensor_tensor(
+                g_rows[:, j, :], e[:, j, :], coef[:, j : j + 1], y_sb[:, j, :], ALU.mult, ALU.subtract
+            )
+
+        nc.vector.tensor_tensor(coef[:, :2], inv_early[:], wt_sb[:, :2], ALU.mult)
+        nc.vector.reciprocal(inv_late, sums[:, 2:])
+        gradient_rows(0)
+        nc.vector.tensor_tensor(coef[:, 2:], inv_late, wt_sb[:, 2:], ALU.mult)
+        for j in range(1, PACK):
+            gradient_rows(j)
 
         xm_bf = tile([P, PACK, P, PACK], BF16, "xm_bf")
         for h in range(2):
@@ -150,14 +160,15 @@ def tile_attend_gkl_pl_mom_kernel(tc, xT, wT, y, wt, xm, mT, offs, out_0, out_1,
                 g_bf[:, a : a + N // 2, :].rearrange("p (c i) j -> p c j i", i=4),
                 g_rows[:, :, a : a + N // 2].rearrange("p j (c i) -> p c j i", i=4),
             )
-        decayed = [tile([P, N], F32, f"decayed{t}") for t in range(PACK)]
+        xm_codes, xm_scales = quantize("xm", xm_bf[:].rearrange("p t m j -> p (t m j)"), E4M3, 1)
+        for t in range(1, PACK):
+            gathered = tile([P, N], F32, f"drift{t}", tag="xm_bf" if t == 1 else None)
+            nc.vector.tensor_scalar(gathered[:], m_src[t][:].indirect(offsets[:]), -LR * BETA, 0.0, ALU.mult, ALU.add)
+            drift.append(gathered)
+        g_codes, g_scales = quantize("g", g_bf[:].rearrange("p c j -> p (c j)"), E5M2, 1, "momentum2")
+        base = [tile([P, N], F32, f"base{t}", tag="e" if t == 0 else None) for t in range(PACK)]
         for t in range(PACK):
-            nc.vector.tensor_scalar(decayed[t][:], m_src[t][:].indirect(offsets[:]), BETA, 0.0, ALU.mult, ALU.add)
-        xm_codes, xm_scales = quantize("xm", xm_bf[:].rearrange("p t m j -> p (t m j)"), E4M3, 1, "momentum0")
-        g_codes, g_scales = quantize("g", g_bf[:].rearrange("p c j -> p (c j)"), E5M2, 2, "momentum1")
-        base = [tile([P, N], F32, f"base{t}", tag="momentum2" if t == 0 else None) for t in range(PACK)]
-        for t in range(PACK):
-            nc.vector.scalar_tensor_tensor(base[t][:], decayed[t][:], -LR, w_g[:, t, :], ALU.mult, ALU.add)
+            nc.gpsimd.tensor_tensor(base[t][:], w_g[:, t, :], drift[t][:], ALU.add)
 
         dw = []
         for t in range(PACK):
@@ -173,16 +184,25 @@ def tile_attend_gkl_pl_mom_kernel(tc, xT, wT, y, wt, xm, mT, offs, out_0, out_1,
                 stop=True,
             )
             dw.append(bank)
-        step = [tile([P, N], F32, f"step{t}") for t in range(PACK)]
+        first = tile([P, N], F32, "first", tag="momentum3")
+        nc.vector.scalar_tensor_tensor(first[:], dw[0][:], -LR, base[0][:], ALU.mult, ALU.add)
+        steps = tile([P, PACK - 1, N], F32, "steps", tag="e")
+        step = {t: steps[:, t - 1, :] for t in range(1, PACK)}
         grad = [tile([P, N], F32, f"grad{t}") for t in range(PACK)]
-        for t in range(PACK):
-            nc.scalar.activation(step[t][:], dw[t][:], ACT.Copy, scale=-LR)
+        decayed = [tile([P, N], F32, f"decayed{t}") for t in range(PACK)]
+        for t in range(1, PACK):
+            nc.scalar.activation(step[t], dw[t][:], ACT.Copy, scale=-LR)
         for t in range(PACK):
             nc.scalar.activation(grad[t][:], dw[t][:], ACT.Copy)
+        for t in range(PACK):
+            nc.scalar.activation(decayed[t][:], drift[t][:], ACT.Copy, scale=-1.0 / LR)
 
         pairs = tile([P, 2, T, 2], BF16, "pairs")
         for t in range(PACK):
-            nc.vector.tensor_tensor(w_dst[t][:].indirect(offsets[:]), base[t][:], step[t][:], ALU.add)
+            if t == 0:
+                nc.vector.tensor_copy(w_dst[t][:].indirect(offsets[:]), first[:])
+            else:
+                nc.vector.tensor_tensor(w_dst[t][:].indirect(offsets[:]), base[t][:], step[t], ALU.add)
             nc.sync.dma_start(plane(out_0, t), w_dst[t][:])
             nc.scalar.activation(pairs[:, t // 2, :, t % 2], w_dst[t][:], ACT.Copy)
 

@@ -128,10 +128,10 @@ def tile_attend_gkl_pl_mom_kernel(tc, xT, wT, y, wt, xm, mT, offs, out_0, out_1,
             nc.scalar.activation(
                 e[:, j, :], score[:], ACT.Exp, bias=neg_max[:, j : j + 1], scale=1.0, accum_out=sums[:, j : j + 1]
             )
-        drift = [tile([P, N], F32, "drift0")]
+        m_g = [tile([P, N], F32, "m_g0")]
         inv_early = tile([P, 2], F32, "inv_early")
         nc.vector.reciprocal(inv_early[:], sums[:, :2])
-        nc.vector.tensor_scalar(drift[0][:], m_src[0][:].indirect(offsets[:]), -LR * BETA, 0.0, ALU.mult, ALU.add)
+        nc.vector.tensor_copy(m_g[0][:], m_src[0][:].indirect(offsets[:]))
         factors = tile([P, PACK + 2], F32, "factors", tag="momentum0")
         coef, inv_late = factors[:, :PACK], factors[:, PACK:]
 
@@ -154,6 +154,8 @@ def tile_attend_gkl_pl_mom_kernel(tc, xT, wT, y, wt, xm, mT, offs, out_0, out_1,
                 xm_raw[:, :, h * (D // 2) : (h + 1) * (D // 2)].rearrange("p j (m t) -> p m j t", t=PACK),
                 ACT.Copy,
             )
+        drift = [tile([P, N], F32, f"drift{t}", tag="xm_raw" if t == 0 else None) for t in range(PACK)]
+        nc.scalar.activation(drift[0][:], m_g[0][:], ACT.Copy, scale=-LR * BETA)
         g_bf = tile([P, N, PACK], BF16, "g_bf")
         for a in range(0, N, N // 2):
             nc.scalar.copy(
@@ -162,13 +164,16 @@ def tile_attend_gkl_pl_mom_kernel(tc, xT, wT, y, wt, xm, mT, offs, out_0, out_1,
             )
         xm_codes, xm_scales = quantize("xm", xm_bf[:].rearrange("p t m j -> p (t m j)"), E4M3, 1)
         for t in range(1, PACK):
-            gathered = tile([P, N], F32, f"drift{t}", tag="xm_bf" if t == 1 else None)
-            nc.vector.tensor_scalar(gathered[:], m_src[t][:].indirect(offsets[:]), -LR * BETA, 0.0, ALU.mult, ALU.add)
-            drift.append(gathered)
+            gathered = tile([P, N], F32, f"m_g{t}", tag="xm_bf" if t == 1 else None)
+            nc.vector.tensor_copy(gathered[:], m_src[t][:].indirect(offsets[:]))
+            nc.scalar.activation(drift[t][:], gathered[:], ACT.Copy, scale=-LR * BETA)
+            m_g.append(gathered)
         g_codes, g_scales = quantize("g", g_bf[:].rearrange("p c j -> p (c j)"), E5M2, 1, "momentum2")
-        base = [tile([P, N], F32, f"base{t}", tag="e" if t == 0 else None) for t in range(PACK)]
+        base_first = tile([P, N], F32, "base_first", tag="e")
+        base_rest = tile([P, PACK - 1, N], F32, "base_rest", tag="g_bf")
+        base = [base_first[:]] + [base_rest[:, t, :] for t in range(PACK - 1)]
         for t in range(PACK):
-            nc.gpsimd.tensor_tensor(base[t][:], w_g[:, t, :], drift[t][:], ALU.add)
+            nc.gpsimd.tensor_tensor(base[t], w_g[:, t, :], drift[t][:], ALU.add)
 
         dw = []
         for t in range(PACK):
@@ -185,29 +190,29 @@ def tile_attend_gkl_pl_mom_kernel(tc, xT, wT, y, wt, xm, mT, offs, out_0, out_1,
             )
             dw.append(bank)
         first = tile([P, N], F32, "first", tag="momentum3")
-        nc.vector.scalar_tensor_tensor(first[:], dw[0][:], -LR, base[0][:], ALU.mult, ALU.add)
+        nc.vector.scalar_tensor_tensor(first[:], dw[0][:], -LR, base[0], ALU.mult, ALU.add)
         steps = tile([P, PACK - 1, N], F32, "steps", tag="e")
         step = {t: steps[:, t - 1, :] for t in range(1, PACK)}
         grad = [tile([P, N], F32, f"grad{t}") for t in range(PACK)]
-        decayed = [tile([P, N], F32, f"decayed{t}") for t in range(PACK)]
+        decayed = tile([P, PACK, N], F32, "decayed", tag="g_rows")
         for t in range(1, PACK):
             nc.scalar.activation(step[t], dw[t][:], ACT.Copy, scale=-LR)
         for t in range(PACK):
             nc.scalar.activation(grad[t][:], dw[t][:], ACT.Copy)
         for t in range(PACK):
-            nc.scalar.activation(decayed[t][:], drift[t][:], ACT.Copy, scale=-1.0 / LR)
+            nc.scalar.activation(decayed[:, t, :], m_g[t][:], ACT.Copy, scale=BETA)
 
         pairs = tile([P, 2, T, 2], BF16, "pairs")
         for t in range(PACK):
             if t == 0:
                 nc.vector.tensor_copy(w_dst[t][:].indirect(offsets[:]), first[:])
             else:
-                nc.vector.tensor_tensor(w_dst[t][:].indirect(offsets[:]), base[t][:], step[t], ALU.add)
+                nc.vector.tensor_tensor(w_dst[t][:].indirect(offsets[:]), base[t], step[t], ALU.add)
             nc.sync.dma_start(plane(out_0, t), w_dst[t][:])
             nc.scalar.activation(pairs[:, t // 2, :, t % 2], w_dst[t][:], ACT.Copy)
 
         for t in range(PACK):
-            nc.vector.tensor_tensor(m_dst[t][:].indirect(offsets[:]), decayed[t][:], grad[t][:], ALU.add)
+            nc.vector.tensor_tensor(m_dst[t][:].indirect(offsets[:]), decayed[:, t, :], grad[t][:], ALU.add)
             nc.sync.dma_start(plane(out_1, t), m_dst[t][:])
 
         out_codes = tile([P, T], U32, "out_codes", tag="grad3")

@@ -1,6 +1,7 @@
 from contextlib import ExitStack
 
 import concourse.mybir as mybir
+from concourse.masks import make_identity
 
 D, T, N, R = 512, 2048, 512, 512
 LR, BETA = 0.1, 0.9
@@ -49,10 +50,11 @@ def tile_attend_gkl_pl_mom_kernel(tc, xT, wT, y, wt, xm, mT, offs, out_0, out_1,
             return codes, scales
 
         offsets = tile([P, N // 16], U16, "offsets")
-        w_src = [tile([P, T], F32, f"w_src{t}", tag=f"table{t}") for t in range(PACK)]
-        nc.sync.dma_start(w_src[0][:], plane(wT, 0))
+        arrival = (2, 3, 1, 0)
+        w_src = {t: tile([P, T], F32, f"w_src{t}", tag=f"table{t}") for t in arrival}
+        nc.sync.dma_start(w_src[arrival[0]][:], plane(wT, arrival[0]))
         nc.sync.dma_start(offsets[:], offs)
-        for t in range(1, PACK):
+        for t in arrival[1:]:
             nc.sync.dma_start(w_src[t][:], plane(wT, t))
 
         warm_in = tile([P, 1], F32, "warm_in")
@@ -60,6 +62,8 @@ def tile_attend_gkl_pl_mom_kernel(tc, xT, wT, y, wt, xm, mT, offs, out_0, out_1,
         nc.vector.memset(warm_in[:], 0.0)
         nc.scalar.activation(warm_out[:], warm_in[:], ACT.Exp)
 
+        ident = tile([P, P], F32, "ident")
+        make_identity(nc, ident[:])
         half = R // 2
         x_rows = xT[0].rearrange("(p t) r -> p t r", t=PACK)
         x_raw = [tile([P, PACK, half], F32, f"x_raw{h}") for h in range(2)]
@@ -71,17 +75,21 @@ def tile_attend_gkl_pl_mom_kernel(tc, xT, wT, y, wt, xm, mT, offs, out_0, out_1,
         y_sb = tile([P, PACK, N], F32, "y_sb")
         m_src = [tile([P, T], F32, f"m_src{t}", tag=f"momentum{t}") for t in range(PACK)]
         nc.sync.dma_start(y_sb[:], y[0].rearrange("(p j) i -> p j i", j=PACK))
-        nc.sync.dma_start(m_src[0][:], plane(mT, 0))
         nc.sync.dma_start(xm_raw[:], xm[0].rearrange("(p j) d -> p j d", j=PACK))
-        for t in range(1, PACK):
+        for t in range(PACK):
             nc.sync.dma_start(m_src[t][:], plane(mT, t))
 
+        w_dst = [tile([P, T], F32, f"w_dst{t}") for t in range(PACK)]
+        nc.sync.dma_start(w_dst[0][:, T // 2 :], plane(wT, 0)[:, T // 2 :])
+
         w_g = tile([P, PACK, N], F32, "w_g")
-        for t in range(PACK):
+        for t in arrival:
             nc.vector.tensor_copy(w_g[:, t, :], w_src[t][:].indirect(offsets[:]))
-        w_dst = [tile([P, T], F32, f"w_dst{t}") for t in range(PACK - 1)]
-        for t in range(PACK - 1):
-            nc.scalar.activation(w_dst[t][:], w_src[t][:], ACT.Copy)
+            if t == 1:
+                nc.vector.tensor_copy(w_dst[t][:, T // 2 :], w_src[t][:, T // 2 :])
+        for t in arrival:
+            width = T if t > 1 else T // 2
+            nc.scalar.activation(w_dst[t][:, :width], w_src[t][:, :width], ACT.Copy)
 
         w_bf = tile([P, N, PACK], BF16, "w_bf")
         nc.vector.tensor_copy(
@@ -98,17 +106,16 @@ def tile_attend_gkl_pl_mom_kernel(tc, xT, wT, y, wt, xm, mT, offs, out_0, out_1,
                 ACT.Copy,
             )
         x_codes, x_scales = quantize("x", x_bf[:].rearrange("p j m t -> p (j m t)"), E4M3, PACK)
-        last = tile([P, T], F32, "w_dst3", tag="x_raw1")
-        nc.scalar.activation(last[:], w_src[PACK - 1][:], ACT.Copy)
-        w_dst.append(last)
-        m_dst = [tile([P, T], F32, f"m_dst{t}", tag=f"table{t}") for t in range(PACK)]
+        m_dst = [tile([P, T], F32, f"m_dst{t}", tag=f"table{arrival[t]}") for t in range(PACK)]
         for t in range(PACK):
             nc.sync.dma_start(m_dst[t][:], plane(mT, t))
 
         for j in range(PACK):
             nc.gpsimd.tensor_scalar(y_sb[:, j, :], y_sb[:, j, :], wt_sb[:, j : j + 1], 0.0, ALU.mult, ALU.add)
 
-        neg_max = tile([P, PACK], F32, "neg_max")
+        neg_max = tile([P, PACK], F32, "neg_max", tag="xm_bf")
+        inv = tile([P, PACK], F32, "inv")
+        coef = tile([P, PACK], F32, "coef")
         e = tile([P, PACK, N], F32, "e")
         sums = tile([P, PACK], F32, "sums")
         g_rows = tile([P, PACK, N], BF16, "g_rows")
@@ -124,27 +131,24 @@ def tile_attend_gkl_pl_mom_kernel(tc, xT, wT, y, wt, xm, mT, offs, out_0, out_1,
                 start=True,
                 stop=True,
             )
+            if j == PACK - 1:
+                nc.vector.reciprocal(inv[:, :2], sums[:, :2])
             nc.vector.tensor_reduce(neg_max[:, j : j + 1], score[:], AXIS.X, ALU.max, negate=True)
             nc.scalar.activation(
                 e[:, j, :], score[:], ACT.Exp, bias=neg_max[:, j : j + 1], scale=1.0, accum_out=sums[:, j : j + 1]
             )
-        m_g = [tile([P, N], F32, "m_g0")]
-        inv_early = tile([P, 2], F32, "inv_early")
-        nc.vector.reciprocal(inv_early[:], sums[:, :2])
-        nc.vector.tensor_copy(m_g[0][:], m_src[0][:].indirect(offsets[:]))
-        factors = tile([P, PACK + 2], F32, "factors", tag="momentum0")
-        coef, inv_late = factors[:, :PACK], factors[:, PACK:]
 
         def gradient_rows(j):
             nc.vector.scalar_tensor_tensor(
                 g_rows[:, j, :], e[:, j, :], coef[:, j : j + 1], y_sb[:, j, :], ALU.mult, ALU.subtract
             )
 
-        nc.vector.tensor_tensor(coef[:, :2], inv_early[:], wt_sb[:, :2], ALU.mult)
-        nc.vector.reciprocal(inv_late, sums[:, 2:])
+        nc.vector.tensor_tensor(coef[:, :2], inv[:, :2], wt_sb[:, :2], ALU.mult)
         gradient_rows(0)
-        nc.vector.tensor_tensor(coef[:, 2:], inv_late, wt_sb[:, 2:], ALU.mult)
-        for j in range(1, PACK):
+        nc.vector.reciprocal(inv[:, 2:], sums[:, 2:])
+        gradient_rows(1)
+        nc.vector.tensor_tensor(coef[:, 2:], inv[:, 2:], wt_sb[:, 2:], ALU.mult)
+        for j in range(2, PACK):
             gradient_rows(j)
 
         xm_bf = tile([P, PACK, P, PACK], BF16, "xm_bf")
@@ -154,26 +158,31 @@ def tile_attend_gkl_pl_mom_kernel(tc, xT, wT, y, wt, xm, mT, offs, out_0, out_1,
                 xm_raw[:, :, h * (D // 2) : (h + 1) * (D // 2)].rearrange("p j (m t) -> p m j t", t=PACK),
                 ACT.Copy,
             )
-        drift = [tile([P, N], F32, f"drift{t}", tag="xm_raw" if t == 0 else None) for t in range(PACK)]
-        nc.scalar.activation(drift[0][:], m_g[0][:], ACT.Copy, scale=-LR * BETA)
         g_bf = tile([P, N, PACK], BF16, "g_bf")
         for a in range(0, N, N // 2):
             nc.scalar.copy(
                 g_bf[:, a : a + N // 2, :].rearrange("p (c i) j -> p c j i", i=4),
                 g_rows[:, :, a : a + N // 2].rearrange("p j (c i) -> p c j i", i=4),
             )
+        drift = [tile([P, N], F32, f"drift{t}") for t in range(PACK)]
+        base = {}
+
+        def gather_drift(t):
+            nc.vector.tensor_scalar(drift[t][:], m_src[t][:].indirect(offsets[:]), -LR * BETA, 0.0, ALU.mult, ALU.add)
+
+        def form_base(t, tag):
+            base[t] = tile([P, N], F32, f"base{t}", tag=tag)
+            nc.gpsimd.tensor_tensor(base[t][:], w_g[:, t, :], drift[t][:], ALU.add)
+
         xm_codes, xm_scales = quantize("xm", xm_bf[:].rearrange("p t m j -> p (t m j)"), E4M3, 1)
-        for t in range(1, PACK):
-            gathered = tile([P, N], F32, f"m_g{t}", tag="xm_bf" if t == 1 else None)
-            nc.vector.tensor_copy(gathered[:], m_src[t][:].indirect(offsets[:]))
-            nc.scalar.activation(drift[t][:], gathered[:], ACT.Copy, scale=-LR * BETA)
-            m_g.append(gathered)
-        g_codes, g_scales = quantize("g", g_bf[:].rearrange("p c j -> p (c j)"), E5M2, 1, "momentum2")
-        base_first = tile([P, N], F32, "base_first", tag="e")
-        base_rest = tile([P, PACK - 1, N], F32, "base_rest", tag="g_bf")
-        base = [base_first[:]] + [base_rest[:, t, :] for t in range(PACK - 1)]
-        for t in range(PACK):
-            nc.gpsimd.tensor_tensor(base[t], w_g[:, t, :], drift[t][:], ALU.add)
+        gather_drift(0)
+        form_base(0, None)
+        gather_drift(1)
+        g_codes, g_scales = quantize("g", g_bf[:].rearrange("p c j -> p (c j)"), E5M2, 1, "momentum1")
+        form_base(1, "g_bf")
+        gather_drift(2)
+        form_base(2, None)
+        gather_drift(3)
 
         dw = []
         for t in range(PACK):
@@ -189,39 +198,55 @@ def tile_attend_gkl_pl_mom_kernel(tc, xT, wT, y, wt, xm, mT, offs, out_0, out_1,
                 stop=True,
             )
             dw.append(bank)
-        first = tile([P, N], F32, "first", tag="momentum3")
-        nc.vector.scalar_tensor_tensor(first[:], dw[0][:], -LR, base[0], ALU.mult, ALU.add)
-        steps = tile([P, PACK - 1, N], F32, "steps", tag="e")
-        step = {t: steps[:, t - 1, :] for t in range(1, PACK)}
-        grad = [tile([P, N], F32, f"grad{t}") for t in range(PACK)]
-        decayed = tile([P, PACK, N], F32, "decayed", tag="g_rows")
-        for t in range(1, PACK):
+        first_step = tile([P, N], F32, "first_step")
+        nc.scalar.activation(first_step[:], dw[0][:], ACT.Copy, scale=-LR)
+        later = tile([P, PACK + 1, N], F32, "later", tag="momentum3")
+        grad = [later[:, 0, :], tile([P, N], F32, "grad1", tag="momentum1")[:], later[:, 1, :]]
+        step = [first_step[:]] + [later[:, 2 + t, :] for t in range(PACK - 1)]
+        for t in range(PACK - 1):
+            nc.scalar.activation(grad[t], dw[t][:], ACT.Copy)
+        for t in (3, 1, 2):
             nc.scalar.activation(step[t], dw[t][:], ACT.Copy, scale=-LR)
-        for t in range(PACK):
-            nc.scalar.activation(grad[t][:], dw[t][:], ACT.Copy)
-        for t in range(PACK):
-            nc.scalar.activation(decayed[:, t, :], m_g[t][:], ACT.Copy, scale=BETA)
 
+        turned = psum.tile([P, N], F32, name="turned", tag="score0")
+        for b in range(N // P):
+            cols = slice(b * P, (b + 1) * P)
+            for i, term in enumerate((w_g[:, 3, cols], drift[3][:, cols])):
+                nc.tensor.matmul(turned[:, cols], term, ident[:], is_transpose=True, start=i == 0, stop=i == 1)
+        turned_sb = tile([P, N], F32, "turned_sb")
+        nc.scalar.copy(turned_sb[:], turned[:])
+        back = psum.tile([P, N], F32, name="back", tag="score1")
+        for b in range(N // P):
+            cols = slice(b * P, (b + 1) * P)
+            nc.tensor.transpose(back[:, cols], turned_sb[:, cols], ident[:])
+        base[3] = tile([P, N], F32, "base3")
+        nc.scalar.copy(base[3][:], back[:])
+
+        last_decayed = tile([P, N], F32, "last_decayed")
+        held = tile([P, PACK - 1, N], F32, "held", tag="turned_sb")
+        decayed = [held[:, t, :] for t in range(PACK - 1)] + [last_decayed[:]]
+        for t in (3, 0, 1, 2):
+            nc.scalar.activation(decayed[t], drift[t][:], ACT.Copy, scale=-1.0 / LR)
         pairs = tile([P, 2, T, 2], BF16, "pairs")
         for t in range(PACK):
-            if t == 0:
-                nc.vector.tensor_copy(w_dst[t][:].indirect(offsets[:]), first[:])
-            else:
-                nc.vector.tensor_tensor(w_dst[t][:].indirect(offsets[:]), base[t], step[t], ALU.add)
+            nc.vector.tensor_tensor(w_dst[t][:].indirect(offsets[:]), base[t][:], step[t], ALU.add)
             nc.sync.dma_start(plane(out_0, t), w_dst[t][:])
             nc.scalar.activation(pairs[:, t // 2, :, t % 2], w_dst[t][:], ACT.Copy)
 
-        for t in range(PACK):
-            nc.vector.tensor_tensor(m_dst[t][:].indirect(offsets[:]), decayed[:, t, :], grad[t][:], ALU.add)
+        def scatter_momentum(t):
+            nc.vector.tensor_tensor(m_dst[t][:].indirect(offsets[:]), decayed[t], grad[t], ALU.add)
             nc.sync.dma_start(plane(out_1, t), m_dst[t][:])
 
-        out_codes = tile([P, T], U32, "out_codes", tag="grad3")
+        for t in range(PACK - 1):
+            scatter_momentum(t)
+
+        out_codes = tile([P, T], U32, "out_codes", tag="momentum1")
         out_scales = tile([P, T], U8, "out_scales")
         words = out_2[0].rearrange("p c t -> p (c t)").bitcast(I32)
         pair_words = pairs[:].rearrange("p u c e -> p (u c e)").bitcast(U32).rearrange("p (u c) -> p u c", u=2)
         for k in range(T // CHUNK):
             cols = slice(k * CHUNK, (k + 1) * CHUNK)
-            grouped = tile([P, CHUNK * PACK], BF16, f"grouped{k}", tag=f"momentum{k}")
+            grouped = tile([P, CHUNK * PACK], BF16, f"grouped{k}", tag=("x_raw0", "x_raw1", "w_bf", "x_bf")[k])
             nc.scalar.copy(
                 grouped[:].bitcast(U32).rearrange("p (c u) -> p c u", u=2),
                 pair_words[:, :, cols].rearrange("p u c -> p c u"),
@@ -236,3 +261,6 @@ def tile_attend_gkl_pl_mom_kernel(tc, xT, wT, y, wt, xm, mT, offs, out_0, out_1,
             nc.sync.dma_start(
                 out_3[0, 4 * q : 4 * q + 4, :].bitcast(I32), out_scales[32 * q : 32 * q + 4, :].bitcast(I32)
             )
+        grad.append(tile([P, N], F32, "grad3", tag="pairs")[:])
+        nc.scalar.activation(grad[PACK - 1], dw[PACK - 1][:], ACT.Copy)
+        scatter_momentum(PACK - 1)

@@ -200,11 +200,11 @@ def tile_attend_gkl_pl_mom_kernel(tc, xT, wT, y, wt, xm, mT, offs, out_0, out_1,
             dw.append(bank)
         first_step = tile([P, N], F32, "first_step")
         nc.scalar.activation(first_step[:], dw[0][:], ACT.Copy, scale=-LR)
-        later = tile([P, PACK + 1, N], F32, "later", tag="momentum3")
-        grad = [later[:, 0, :], tile([P, N], F32, "grad1", tag="momentum1")[:], later[:, 1, :]]
-        step = [first_step[:]] + [later[:, 2 + t, :] for t in range(PACK - 1)]
-        for t in range(PACK - 1):
-            nc.scalar.activation(grad[t], dw[t][:], ACT.Copy)
+        later = tile([P, PACK, N], F32, "later", tag="momentum3")
+        decayed = [tile([P, N], F32, f"decayed{t}")[:] for t in range(PACK - 1)] + [later[:, 0, :]]
+        step = [first_step[:]] + [later[:, t, :] for t in range(1, PACK)]
+        for t in range(PACK):
+            nc.scalar.activation(decayed[t], drift[t][:], ACT.Copy, scale=-1.0 / LR)
         for t in (3, 1, 2):
             nc.scalar.activation(step[t], dw[t][:], ACT.Copy, scale=-LR)
 
@@ -222,11 +222,10 @@ def tile_attend_gkl_pl_mom_kernel(tc, xT, wT, y, wt, xm, mT, offs, out_0, out_1,
         base[3] = tile([P, N], F32, "base3")
         nc.scalar.copy(base[3][:], back[:])
 
-        last_decayed = tile([P, N], F32, "last_decayed")
         held = tile([P, PACK - 1, N], F32, "held", tag="turned_sb")
-        decayed = [held[:, t, :] for t in range(PACK - 1)] + [last_decayed[:]]
-        for t in (3, 0, 1, 2):
-            nc.scalar.activation(decayed[t], drift[t][:], ACT.Copy, scale=-1.0 / LR)
+        grad = [held[:, t, :] for t in range(PACK - 1)]
+        for t in range(PACK - 1):
+            nc.scalar.activation(grad[t], dw[t][:], ACT.Copy)
         pairs = tile([P, 2, T, 2], BF16, "pairs")
         for t in range(PACK):
             nc.vector.tensor_tensor(w_dst[t][:].indirect(offsets[:]), base[t][:], step[t], ALU.add)
@@ -240,7 +239,7 @@ def tile_attend_gkl_pl_mom_kernel(tc, xT, wT, y, wt, xm, mT, offs, out_0, out_1,
         for t in range(PACK - 1):
             scatter_momentum(t)
 
-        out_codes = tile([P, T], U32, "out_codes", tag="momentum1")
+        out_codes = tile([P, T], U32, "out_codes", tag="decayed1")
         out_scales = tile([P, T], U8, "out_scales")
         words = out_2[0].rearrange("p c t -> p (c t)").bitcast(I32)
         pair_words = pairs[:].rearrange("p u c e -> p (u c e)").bitcast(U32).rearrange("p (u c) -> p u c", u=2)

@@ -83,26 +83,28 @@ def tile_attend_gkl_pl_mom_kernel(tc, xT, wT, y, wt, xm, mT, offs, out_0, out_1,
         nc.sync.dma_start(w_dst[0][:, T // 2 :], plane(wT, 0)[:, T // 2 :])
 
         w_g = tile([P, PACK, N], F32, "w_g")
+        w_bf = tile([P, N, PACK], BF16, "w_bf")
         for t in arrival:
             nc.vector.tensor_copy(w_g[:, t, :], w_src[t][:].indirect(offsets[:]))
+            if t in (3, 0):
+                pair = slice(t // 2 * 2, t // 2 * 2 + 2)
+                nc.vector.tensor_copy(
+                    w_bf[:, :, pair].rearrange("p (c i) t -> p c t i", i=4),
+                    w_g[:, pair, :].rearrange("p t (c i) -> p c t i", i=4),
+                )
             if t == 1:
                 nc.vector.tensor_copy(w_dst[t][:, T // 2 :], w_src[t][:, T // 2 :])
         for t in arrival:
             width = T if t > 1 else T // 2
             nc.scalar.activation(w_dst[t][:, :width], w_src[t][:, :width], ACT.Copy)
 
-        w_bf = tile([P, N, PACK], BF16, "w_bf")
-        nc.vector.tensor_copy(
-            w_bf[:].rearrange("p (c i) t -> p c t i", i=4),
-            w_g[:].rearrange("p t (c i) -> p c t i", i=4),
-        )
         w_codes, w_scales = quantize("w", w_bf[:].rearrange("p c t -> p (c t)"), E4M3, 1)
 
         x_bf = tile([P, PACK, P, PACK], BF16, "x_bf")
-        for h in range(2):
+        for h, tiles in ((0, slice(0, 4)), (1, slice(0, 2)), (1, slice(2, 4))):
             nc.scalar.activation(
-                x_bf[:, :, h * (P // 2) : (h + 1) * (P // 2), :].rearrange("p j m t -> p m t j"),
-                x_raw[h][:].rearrange("p t (m j) -> p m t j", j=PACK),
+                x_bf[:, tiles, h * (P // 2) : (h + 1) * (P // 2), :].rearrange("p j m t -> p m t j"),
+                x_raw[h][:].rearrange("p t (m j) -> p m t j", j=PACK)[:, :, :, tiles],
                 ACT.Copy,
             )
         x_codes, x_scales = quantize("x", x_bf[:].rearrange("p j m t -> p (j m t)"), E4M3, PACK)

@@ -178,7 +178,7 @@ def tile_attend_gkl_pl_mom_kernel(tc, xT, wT, y, wt, xm, mT, offs, out_0, out_1,
 
         xm_codes, xm_scales = quantize("xm", xm_bf[:].rearrange("p t m j -> p (t m j)"), E4M3, 1)
         gather_drift(0)
-        form_base(0, None)
+        form_base(0, "xm_bf")
         gather_drift(1)
         g_codes, g_scales = quantize("g", g_bf[:].rearrange("p c j -> p (c j)"), E5M2, 1, "momentum1")
         form_base(1, "g_bf")

@@ -50,7 +50,7 @@ def tile_attend_gkl_pl_mom_kernel(tc, xT, wT, y, wt, xm, mT, offs, out_0, out_1,
             return codes, scales
 
         offsets = tile([P, N // 16], U16, "offsets")
-        arrival = (2, 3, 1, 0)
+        arrival = (2, 3, 0, 1)
         w_src = {t: tile([P, T], F32, f"w_src{t}", tag=f"table{t}") for t in arrival}
         nc.sync.dma_start(w_src[arrival[0]][:], plane(wT, arrival[0]))
         nc.sync.dma_start(offsets[:], offs)
@@ -64,6 +64,8 @@ def tile_attend_gkl_pl_mom_kernel(tc, xT, wT, y, wt, xm, mT, offs, out_0, out_1,
 
         ident = tile([P, P], F32, "ident")
         make_identity(nc, ident[:])
+        undo_rate = tile([P, N], F32, "undo_rate")
+        nc.gpsimd.memset(undo_rate[:], -1.0 / LR)
         half = R // 2
         x_rows = xT[0].rearrange("(p t) r -> p t r", t=PACK)
         x_raw = [tile([P, PACK, half], F32, f"x_raw{h}") for h in range(2)]
@@ -76,24 +78,22 @@ def tile_attend_gkl_pl_mom_kernel(tc, xT, wT, y, wt, xm, mT, offs, out_0, out_1,
         m_src = [tile([P, T], F32, f"m_src{t}", tag=f"momentum{t}") for t in range(PACK)]
         nc.sync.dma_start(y_sb[:], y[0].rearrange("(p j) i -> p j i", j=PACK))
         nc.sync.dma_start(xm_raw[:], xm[0].rearrange("(p j) d -> p j d", j=PACK))
+        w_dst = [tile([P, T], F32, f"w_dst{t}") for t in range(PACK)]
         for t in range(PACK):
             nc.sync.dma_start(m_src[t][:], plane(mT, t))
-
-        w_dst = [tile([P, T], F32, f"w_dst{t}") for t in range(PACK)]
-        nc.sync.dma_start(w_dst[0][:, T // 2 :], plane(wT, 0)[:, T // 2 :])
+            if t >= 2:
+                nc.sync.dma_start(w_dst[t - 2][:, T // 2 :], plane(wT, t - 2)[:, T // 2 :])
 
         w_g = tile([P, PACK, N], F32, "w_g")
         w_bf = tile([P, N, PACK], BF16, "w_bf")
         for t in arrival:
             nc.vector.tensor_copy(w_g[:, t, :], w_src[t][:].indirect(offsets[:]))
-            if t in (3, 0):
+            if t in (3, 1):
                 pair = slice(t // 2 * 2, t // 2 * 2 + 2)
                 nc.vector.tensor_copy(
                     w_bf[:, :, pair].rearrange("p (c i) t -> p c t i", i=4),
                     w_g[:, pair, :].rearrange("p t (c i) -> p c t i", i=4),
                 )
-            if t == 1:
-                nc.vector.tensor_copy(w_dst[t][:, T // 2 :], w_src[t][:, T // 2 :])
         for t in arrival:
             width = T if t > 1 else T // 2
             nc.scalar.activation(w_dst[t][:, :width], w_src[t][:, :width], ACT.Copy)
@@ -108,8 +108,8 @@ def tile_attend_gkl_pl_mom_kernel(tc, xT, wT, y, wt, xm, mT, offs, out_0, out_1,
                 ACT.Copy,
             )
         x_codes, x_scales = quantize("x", x_bf[:].rearrange("p j m t -> p (j m t)"), E4M3, PACK)
-        m_dst = [tile([P, T], F32, f"m_dst{t}", tag=f"table{arrival[t]}") for t in range(PACK)]
-        for t in range(PACK):
+        m_dst = [tile([P, T], F32, f"m_dst{t}", tag=f"table{(2, 1, 3, 0)[t]}") for t in range(PACK)]
+        for t in (0, 2, 3, 1):
             nc.sync.dma_start(m_dst[t][:], plane(mT, t))
 
         for j in range(PACK):
@@ -118,7 +118,7 @@ def tile_attend_gkl_pl_mom_kernel(tc, xT, wT, y, wt, xm, mT, offs, out_0, out_1,
         neg_max = tile([P, PACK], F32, "neg_max", tag="xm_bf")
         inv = tile([P, PACK], F32, "inv")
         coef = tile([P, PACK], F32, "coef")
-        e = tile([P, PACK, N], F32, "e")
+        e = [tile([P, N], F32, f"e{j}") for j in range(PACK)]
         sums = tile([P, PACK], F32, "sums")
         g_rows = tile([P, PACK, N], BF16, "g_rows")
         for j in range(PACK):
@@ -137,12 +137,12 @@ def tile_attend_gkl_pl_mom_kernel(tc, xT, wT, y, wt, xm, mT, offs, out_0, out_1,
                 nc.vector.reciprocal(inv[:, :2], sums[:, :2])
             nc.vector.tensor_reduce(neg_max[:, j : j + 1], score[:], AXIS.X, ALU.max, negate=True)
             nc.scalar.activation(
-                e[:, j, :], score[:], ACT.Exp, bias=neg_max[:, j : j + 1], scale=1.0, accum_out=sums[:, j : j + 1]
+                e[j][:], score[:], ACT.Exp, bias=neg_max[:, j : j + 1], scale=1.0, accum_out=sums[:, j : j + 1]
             )
 
-        def gradient_rows(j):
+        def gradient_rows(j, cols=slice(0, N)):
             nc.vector.scalar_tensor_tensor(
-                g_rows[:, j, :], e[:, j, :], coef[:, j : j + 1], y_sb[:, j, :], ALU.mult, ALU.subtract
+                g_rows[:, j, cols], e[j][:, cols], coef[:, j : j + 1], y_sb[:, j, cols], ALU.mult, ALU.subtract
             )
 
         nc.vector.tensor_tensor(coef[:, :2], inv[:, :2], wt_sb[:, :2], ALU.mult)
@@ -150,8 +150,9 @@ def tile_attend_gkl_pl_mom_kernel(tc, xT, wT, y, wt, xm, mT, offs, out_0, out_1,
         nc.vector.reciprocal(inv[:, 2:], sums[:, 2:])
         gradient_rows(1)
         nc.vector.tensor_tensor(coef[:, 2:], inv[:, 2:], wt_sb[:, 2:], ALU.mult)
-        for j in range(2, PACK):
-            gradient_rows(j)
+        for a in range(0, N, N // 2):
+            for j in range(2, PACK):
+                gradient_rows(j, slice(a, a + N // 2))
 
         xm_bf = tile([P, PACK, P, PACK], BF16, "xm_bf")
         for h in range(2):
@@ -166,7 +167,7 @@ def tile_attend_gkl_pl_mom_kernel(tc, xT, wT, y, wt, xm, mT, offs, out_0, out_1,
                 g_bf[:, a : a + N // 2, :].rearrange("p (c i) j -> p c j i", i=4),
                 g_rows[:, :, a : a + N // 2].rearrange("p j (c i) -> p c j i", i=4),
             )
-        drift = [tile([P, N], F32, f"drift{t}") for t in range(PACK)]
+        drift = [tile([P, N], F32, f"drift{t}", tag="e2" if t == 0 else None) for t in range(PACK)]
         base = {}
 
         def gather_drift(t):
@@ -178,13 +179,11 @@ def tile_attend_gkl_pl_mom_kernel(tc, xT, wT, y, wt, xm, mT, offs, out_0, out_1,
 
         xm_codes, xm_scales = quantize("xm", xm_bf[:].rearrange("p t m j -> p (t m j)"), E4M3, 1)
         gather_drift(0)
-        form_base(0, "xm_bf")
+        g_codes, g_scales = quantize("g", g_bf[:].rearrange("p c j -> p (c j)"), E5M2, 1)
+        form_base(0, "g_bf")
         gather_drift(1)
-        g_codes, g_scales = quantize("g", g_bf[:].rearrange("p c j -> p (c j)"), E5M2, 1, "momentum1")
-        form_base(1, "g_bf")
+        form_base(1, None)
         gather_drift(2)
-        form_base(2, None)
-        gather_drift(3)
 
         dw = []
         for t in range(PACK):
@@ -200,57 +199,70 @@ def tile_attend_gkl_pl_mom_kernel(tc, xT, wT, y, wt, xm, mT, offs, out_0, out_1,
                 stop=True,
             )
             dw.append(bank)
-        first_step = tile([P, N], F32, "first_step")
-        nc.scalar.activation(first_step[:], dw[0][:], ACT.Copy, scale=-LR)
-        later = tile([P, PACK, N], F32, "later", tag="momentum3")
-        decayed = [tile([P, N], F32, f"decayed{t}")[:] for t in range(PACK - 1)] + [later[:, 0, :]]
-        step = [first_step[:]] + [later[:, t, :] for t in range(1, PACK)]
+        step = [tile([P, N], F32, f"step{t}") for t in range(PACK)]
+        decayed = [tile([P, N], F32, f"decayed{t}") for t in range(2)]
         for t in range(PACK):
-            nc.scalar.activation(decayed[t], drift[t][:], ACT.Copy, scale=-1.0 / LR)
-        for t in (3, 1, 2):
-            nc.scalar.activation(step[t], dw[t][:], ACT.Copy, scale=-LR)
+            nc.scalar.activation(step[t][:], dw[t][:], ACT.Copy, scale=-LR)
+        for t in range(2):
+            nc.scalar.activation(decayed[t][:], drift[t][:], ACT.Copy, scale=-1.0 / LR)
 
-        turned = psum.tile([P, N], F32, name="turned", tag="score0")
-        for b in range(N // P):
-            cols = slice(b * P, (b + 1) * P)
-            for i, term in enumerate((w_g[:, 3, cols], drift[3][:, cols])):
-                nc.tensor.matmul(turned[:, cols], term, ident[:], is_transpose=True, start=i == 0, stop=i == 1)
-        turned_sb = tile([P, N], F32, "turned_sb")
-        nc.scalar.copy(turned_sb[:], turned[:])
-        back = psum.tile([P, N], F32, name="back", tag="score1")
-        for b in range(N // P):
-            cols = slice(b * P, (b + 1) * P)
-            nc.tensor.transpose(back[:, cols], turned_sb[:, cols], ident[:])
-        base[3] = tile([P, N], F32, "base3")
-        nc.scalar.copy(base[3][:], back[:])
+        change = {}
 
-        held = tile([P, PACK - 1, N], F32, "held", tag="turned_sb")
-        grad = [held[:, t, :] for t in range(PACK - 1)]
-        for t in range(PACK - 1):
-            nc.scalar.activation(grad[t], dw[t][:], ACT.Copy)
-        pairs = tile([P, 2, T, 2], BF16, "pairs")
-        for t in range(PACK):
-            nc.vector.tensor_tensor(w_dst[t][:].indirect(offsets[:]), base[t][:], step[t], ALU.add)
+        def form_change(t, banks, tag):
+            turned = psum.tile([P, N], F32, name=f"turned{t}", tag=banks[0])
+            for b in range(N // P):
+                cols = slice(b * P, (b + 1) * P)
+                for i, term in enumerate((drift[t][:, cols], step[t][:, cols])):
+                    nc.tensor.matmul(turned[:, cols], term, ident[:], is_transpose=True, start=i == 0, stop=i == 1)
+            turned_sb = tile([P, N], F32, f"turned_sb{t}")
+            nc.scalar.copy(turned_sb[:], turned[:])
+            back = psum.tile([P, N], F32, name=f"back{t}", tag=banks[1])
+            for b in range(N // P):
+                cols = slice(b * P, (b + 1) * P)
+                nc.tensor.transpose(back[:, cols], turned_sb[:, cols], ident[:])
+            change[t] = tile([P, N], F32, f"change{t}", tag=tag)
+            nc.scalar.copy(change[t][:], back[:])
+
+        chunks = [slice(a, a + CHUNK) for a in range(0, T, CHUNK)]
+        pairs = [tile([P, 2, CHUNK, 2], BF16, f"pairs{k}") for k in range(len(chunks))]
+
+        def scatter_weights(t, first, second):
+            nc.vector.tensor_tensor(w_dst[t][:].indirect(offsets[:]), first, second, ALU.add)
             nc.sync.dma_start(plane(out_0, t), w_dst[t][:])
-            nc.scalar.activation(pairs[:, t // 2, :, t % 2], w_dst[t][:], ACT.Copy)
 
-        def scatter_momentum(t):
-            nc.vector.tensor_tensor(m_dst[t][:].indirect(offsets[:]), decayed[t], grad[t], ALU.add)
+        def cast_weights(t, k):
+            nc.scalar.activation(pairs[k][:, t // 2, :, t % 2], w_dst[t][:, chunks[k]], ACT.Copy)
+
+        def scatter_momentum(t, first, second, op):
+            nc.vector.tensor_tensor(m_dst[t][:].indirect(offsets[:]), first, second, op)
             nc.sync.dma_start(plane(out_1, t), m_dst[t][:])
 
+        scatter_weights(0, base[0][:], step[0][:])
+        gather_drift(3)
+        form_change(2, ("score0", "score1"), "momentum3")
+        form_change(3, ("score2", "score3"), None)
+        scatter_weights(1, base[1][:], step[1][:])
+        for t in (2, 3):
+            scatter_weights(t, w_g[:, t, :], change[t][:])
+        first_grad = tile([P, N], F32, "first_grad", tag="turned_sb3")
+        nc.scalar.activation(first_grad[:], dw[0][:], ACT.Copy)
         for t in range(PACK - 1):
-            scatter_momentum(t)
+            for k in range(len(chunks)):
+                cast_weights(t, k)
 
-        out_codes = tile([P, T], U32, "out_codes", tag="decayed1")
+        scatter_momentum(0, decayed[0][:], first_grad[:], ALU.add)
+        for t in (2, 3):
+            scatter_momentum(t, change[t][:], undo_rate[:], ALU.mult)
+
+        out_codes = tile([P, T], U32, "out_codes", tag="momentum3")
         out_scales = tile([P, T], U8, "out_scales")
         words = out_2[0].rearrange("p c t -> p (c t)").bitcast(I32)
-        pair_words = pairs[:].rearrange("p u c e -> p (u c e)").bitcast(U32).rearrange("p (u c) -> p u c", u=2)
-        for k in range(T // CHUNK):
-            cols = slice(k * CHUNK, (k + 1) * CHUNK)
+        for k, cols in enumerate(chunks):
+            cast_weights(PACK - 1, k)
             grouped = tile([P, CHUNK * PACK], BF16, f"grouped{k}", tag=("x_raw0", "x_raw1", "w_bf", "x_bf")[k])
             nc.scalar.copy(
                 grouped[:].bitcast(U32).rearrange("p (c u) -> p c u", u=2),
-                pair_words[:, :, cols].rearrange("p u c -> p c u"),
+                pairs[k][:].rearrange("p u c e -> p (u c e)").bitcast(U32).rearrange("p (u c) -> p c u", u=2),
             )
             nc.vector.quantize_mx(
                 out=out_codes[:, cols].bitcast(E4M3),
@@ -262,6 +274,6 @@ def tile_attend_gkl_pl_mom_kernel(tc, xT, wT, y, wt, xm, mT, offs, out_0, out_1,
             nc.sync.dma_start(
                 out_3[0, 4 * q : 4 * q + 4, :].bitcast(I32), out_scales[32 * q : 32 * q + 4, :].bitcast(I32)
             )
-        grad.append(tile([P, N], F32, "grad3", tag="pairs")[:])
-        nc.scalar.activation(grad[PACK - 1], dw[PACK - 1][:], ACT.Copy)
-        scatter_momentum(PACK - 1)
+        last_grad = tile([P, N], F32, "last_grad", tag=f"pairs{len(chunks) - 1}")
+        nc.scalar.activation(last_grad[:], dw[1][:], ACT.Copy)
+        scatter_momentum(1, decayed[1][:], last_grad[:], ALU.add)

@@ -50,7 +50,7 @@ def tile_attend_gkl_pl_mom_kernel(tc, xT, wT, y, wt, xm, mT, offs, out_0, out_1,
             return codes, scales
 
         offsets = tile([P, N // 16], U16, "offsets")
-        arrival = (2, 3, 0, 1)
+        arrival = (2, 3, 1, 0)
         w_src = {t: tile([P, T], F32, f"w_src{t}", tag=f"table{t}") for t in arrival}
         nc.sync.dma_start(w_src[arrival[0]][:], plane(wT, arrival[0]))
         nc.sync.dma_start(offsets[:], offs)
@@ -74,26 +74,28 @@ def tile_attend_gkl_pl_mom_kernel(tc, xT, wT, y, wt, xm, mT, offs, out_0, out_1,
         wt_sb = tile([P, PACK], F32, "wt_sb")
         nc.sync.dma_start(wt_sb[:], wt[0].rearrange("(p j) one -> p (j one)", j=PACK))
         xm_raw = tile([P, PACK, D], F32, "xm_raw")
-        y_sb = tile([P, PACK, N], F32, "y_sb")
+        y_sb = [tile([P, 2, N], F32, f"y_sb{h}") for h in range(2)]
         m_src = [tile([P, T], F32, f"m_src{t}", tag=f"momentum{t}") for t in range(PACK)]
-        nc.sync.dma_start(y_sb[:], y[0].rearrange("(p j) i -> p j i", j=PACK))
+        for h in range(2):
+            nc.sync.dma_start(y_sb[h][:], y[0].rearrange("(p j) i -> p j i", j=PACK)[:, 2 * h : 2 * h + 2, :])
         nc.sync.dma_start(xm_raw[:], xm[0].rearrange("(p j) d -> p j d", j=PACK))
         w_dst = [tile([P, T], F32, f"w_dst{t}") for t in range(PACK)]
         for t in range(PACK):
             nc.sync.dma_start(m_src[t][:], plane(mT, t))
-            if t >= 2:
-                nc.sync.dma_start(w_dst[t - 2][:, T // 2 :], plane(wT, t - 2)[:, T // 2 :])
+        nc.sync.dma_start(w_dst[0][:, T // 2 :], plane(wT, 0)[:, T // 2 :])
 
         w_g = tile([P, PACK, N], F32, "w_g")
         w_bf = tile([P, N, PACK], BF16, "w_bf")
         for t in arrival:
             nc.vector.tensor_copy(w_g[:, t, :], w_src[t][:].indirect(offsets[:]))
-            if t in (3, 1):
+            if t in (3, 0):
                 pair = slice(t // 2 * 2, t // 2 * 2 + 2)
                 nc.vector.tensor_copy(
                     w_bf[:, :, pair].rearrange("p (c i) t -> p c t i", i=4),
                     w_g[:, pair, :].rearrange("p t (c i) -> p c t i", i=4),
                 )
+            if t == 1:
+                nc.vector.tensor_copy(w_dst[t][:, T // 2 :], w_src[t][:, T // 2 :])
         for t in arrival:
             width = T if t > 1 else T // 2
             nc.scalar.activation(w_dst[t][:, :width], w_src[t][:, :width], ACT.Copy)
@@ -108,16 +110,19 @@ def tile_attend_gkl_pl_mom_kernel(tc, xT, wT, y, wt, xm, mT, offs, out_0, out_1,
                 ACT.Copy,
             )
         x_codes, x_scales = quantize("x", x_bf[:].rearrange("p j m t -> p (j m t)"), E4M3, PACK)
-        m_dst = [tile([P, T], F32, f"m_dst{t}", tag=f"table{(2, 1, 3, 0)[t]}") for t in range(PACK)]
+        m_dst = [tile([P, T], F32, f"m_dst{t}", tag=f"table{(2, 0, 3, 1)[t]}") for t in range(PACK)]
         for t in (0, 2, 3, 1):
             nc.sync.dma_start(m_dst[t][:], plane(mT, t))
 
-        for j in range(PACK):
-            nc.gpsimd.tensor_scalar(y_sb[:, j, :], y_sb[:, j, :], wt_sb[:, j : j + 1], 0.0, ALU.mult, ALU.add)
+        target = [y_sb[j // 2][:, j % 2, :] for j in range(PACK)]
+        for j in range(2):
+            nc.scalar.activation(target[j], target[j], ACT.Copy, scale=wt_sb[:, j : j + 1])
+        for j in range(2, PACK):
+            nc.gpsimd.tensor_scalar(target[j], target[j], wt_sb[:, j : j + 1], 0.0, ALU.mult, ALU.add)
 
         neg_max = tile([P, PACK], F32, "neg_max", tag="xm_bf")
         inv = tile([P, PACK], F32, "inv")
-        coef = tile([P, PACK], F32, "coef")
+        coef = {}
         e = [tile([P, N], F32, f"e{j}") for j in range(PACK)]
         sums = tile([P, PACK], F32, "sums")
         g_rows = tile([P, PACK, N], BF16, "g_rows")
@@ -142,14 +147,20 @@ def tile_attend_gkl_pl_mom_kernel(tc, xT, wT, y, wt, xm, mT, offs, out_0, out_1,
 
         def gradient_rows(j, cols=slice(0, N)):
             nc.vector.scalar_tensor_tensor(
-                g_rows[:, j, cols], e[j][:, cols], coef[:, j : j + 1], y_sb[:, j, cols], ALU.mult, ALU.subtract
+                g_rows[:, j, cols], e[j][:, cols], coef[j], target[j][:, cols], ALU.mult, ALU.subtract
             )
 
-        nc.vector.tensor_tensor(coef[:, :2], inv[:, :2], wt_sb[:, :2], ALU.mult)
+        def form_coef(engine, j):
+            both = tile([P, 2], F32, f"coef{j}")
+            engine.tensor_tensor(both[:], inv[:, j : j + 2], wt_sb[:, j : j + 2], ALU.mult)
+            coef[j], coef[j + 1] = both[:, 0:1], both[:, 1:2]
+
+        form_coef(nc.gpsimd, 0)
         gradient_rows(0)
         nc.vector.reciprocal(inv[:, 2:], sums[:, 2:])
-        gradient_rows(1)
-        nc.vector.tensor_tensor(coef[:, 2:], inv[:, 2:], wt_sb[:, 2:], ALU.mult)
+        gradient_rows(1, slice(0, N // 2))
+        form_coef(nc.vector, 2)
+        gradient_rows(1, slice(N // 2, N))
         for a in range(0, N, N // 2):
             for j in range(2, PACK):
                 gradient_rows(j, slice(a, a + N // 2))
@@ -184,6 +195,7 @@ def tile_attend_gkl_pl_mom_kernel(tc, xT, wT, y, wt, xm, mT, offs, out_0, out_1,
         gather_drift(1)
         form_base(1, None)
         gather_drift(2)
+        gather_drift(3)
 
         dw = []
         for t in range(PACK):
@@ -199,7 +211,7 @@ def tile_attend_gkl_pl_mom_kernel(tc, xT, wT, y, wt, xm, mT, offs, out_0, out_1,
                 stop=True,
             )
             dw.append(bank)
-        step = [tile([P, N], F32, f"step{t}") for t in range(PACK)]
+        step = [tile([P, N], F32, f"step{t}", tag="momentum3" if t == 1 else None) for t in range(PACK)]
         decayed = [tile([P, N], F32, f"decayed{t}") for t in range(2)]
         for t in range(PACK):
             nc.scalar.activation(step[t][:], dw[t][:], ACT.Copy, scale=-LR)
@@ -208,7 +220,7 @@ def tile_attend_gkl_pl_mom_kernel(tc, xT, wT, y, wt, xm, mT, offs, out_0, out_1,
 
         change = {}
 
-        def form_change(t, banks, tag):
+        def form_change(t, banks):
             turned = psum.tile([P, N], F32, name=f"turned{t}", tag=banks[0])
             for b in range(N // P):
                 cols = slice(b * P, (b + 1) * P)
@@ -220,7 +232,7 @@ def tile_attend_gkl_pl_mom_kernel(tc, xT, wT, y, wt, xm, mT, offs, out_0, out_1,
             for b in range(N // P):
                 cols = slice(b * P, (b + 1) * P)
                 nc.tensor.transpose(back[:, cols], turned_sb[:, cols], ident[:])
-            change[t] = tile([P, N], F32, f"change{t}", tag=tag)
+            change[t] = tile([P, N], F32, f"change{t}")
             nc.scalar.copy(change[t][:], back[:])
 
         chunks = [slice(a, a + CHUNK) for a in range(0, T, CHUNK)]
@@ -237,11 +249,10 @@ def tile_attend_gkl_pl_mom_kernel(tc, xT, wT, y, wt, xm, mT, offs, out_0, out_1,
             nc.vector.tensor_tensor(m_dst[t][:].indirect(offsets[:]), first, second, op)
             nc.sync.dma_start(plane(out_1, t), m_dst[t][:])
 
-        scatter_weights(0, base[0][:], step[0][:])
-        gather_drift(3)
-        form_change(2, ("score0", "score1"), "momentum3")
-        form_change(3, ("score2", "score3"), None)
-        scatter_weights(1, base[1][:], step[1][:])
+        form_change(2, ("score0", "score1"))
+        form_change(3, ("score2", "score3"))
+        for t in (0, 1):
+            scatter_weights(t, base[t][:], step[t][:])
         for t in (2, 3):
             scatter_weights(t, w_g[:, t, :], change[t][:])
         first_grad = tile([P, N], F32, "first_grad", tag="turned_sb3")
@@ -254,7 +265,7 @@ def tile_attend_gkl_pl_mom_kernel(tc, xT, wT, y, wt, xm, mT, offs, out_0, out_1,
         for t in (2, 3):
             scatter_momentum(t, change[t][:], undo_rate[:], ALU.mult)
 
-        out_codes = tile([P, T], U32, "out_codes", tag="momentum3")
+        out_codes = tile([P, T], U32, "out_codes", tag="change2")
         out_scales = tile([P, T], U8, "out_scales")
         words = out_2[0].rearrange("p c t -> p (c t)").bitcast(I32)
         for k, cols in enumerate(chunks):

@@ -86,21 +86,32 @@ def tile_attend_gkl_pl_mom_kernel(tc, xT, wT, y, wt, xm, mT, offs, out_0, out_1,
 
         w_g = tile([P, PACK, N], F32, "w_g")
         w_bf = tile([P, N, PACK], BF16, "w_bf")
-        for t in arrival:
-            nc.vector.tensor_copy(w_g[:, t, :], w_src[t][:].indirect(offsets[:]))
-            if t in (3, 0):
-                pair = slice(t // 2 * 2, t // 2 * 2 + 2)
-                nc.vector.tensor_copy(
-                    w_bf[:, :, pair].rearrange("p (c i) t -> p c t i", i=4),
-                    w_g[:, pair, :].rearrange("p t (c i) -> p c t i", i=4),
-                )
-            if t == 1:
-                nc.vector.tensor_copy(w_dst[t][:, T // 2 :], w_src[t][:, T // 2 :])
+
+        def gather_weights(t, slots):
+            listed = offsets[:, slots.start // 16 : slots.stop // 16]
+            nc.vector.tensor_copy(w_g[:, t, slots], w_src[t][:].indirect(listed))
+
+        def group_weights(pair, slots):
+            nc.vector.tensor_copy(
+                w_bf[:, slots, pair].rearrange("p (c i) t -> p c t i", i=4),
+                w_g[:, pair, slots].rearrange("p t (c i) -> p c t i", i=4),
+            )
+
+        halves = (slice(0, N // 2), slice(N // 2, N))
+        gather_weights(2, slice(0, N))
+        gather_weights(3, slice(0, N))
+        group_weights(slice(2, 4), slice(0, N))
+        gather_weights(1, slice(0, N))
+        nc.vector.tensor_copy(w_dst[1][:, T // 2 :], w_src[1][:, T // 2 :])
+        for slots in halves:
+            gather_weights(0, slots)
+        for slots in halves:
+            group_weights(slice(0, 2), slots)
         for t in arrival:
             width = T if t > 1 else T // 2
             nc.scalar.activation(w_dst[t][:, :width], w_src[t][:, :width], ACT.Copy)
 
-        w_codes, w_scales = quantize("w", w_bf[:].rearrange("p c t -> p (c t)"), E4M3, 1)
+        w_codes, w_scales = quantize("w", w_bf[:].rearrange("p c t -> p (c t)"), E4M3, 2)
 
         x_bf = tile([P, PACK, P, PACK], BF16, "x_bf")
         for h, tiles in ((0, slice(0, 4)), (1, slice(0, 2)), (1, slice(2, 4))):
@@ -190,7 +201,7 @@ def tile_attend_gkl_pl_mom_kernel(tc, xT, wT, y, wt, xm, mT, offs, out_0, out_1,
 
         xm_codes, xm_scales = quantize("xm", xm_bf[:].rearrange("p t m j -> p (t m j)"), E4M3, 1)
         gather_drift(0)
-        g_codes, g_scales = quantize("g", g_bf[:].rearrange("p c j -> p (c j)"), E5M2, 1)
+        g_codes, g_scales = quantize("g", g_bf[:].rearrange("p c j -> p (c j)"), E5M2, 2)
         form_base(0, "g_bf")
         gather_drift(1)
         form_base(1, None)

@@ -80,9 +80,11 @@ def tile_attend_gkl_pl_mom_kernel(tc, xT, wT, y, wt, xm, mT, offs, out_0, out_1,
             nc.sync.dma_start(y_sb[h][:], y[0].rearrange("(p j) i -> p j i", j=PACK)[:, 2 * h : 2 * h + 2, :])
         nc.sync.dma_start(xm_raw[:], xm[0].rearrange("(p j) d -> p j d", j=PACK))
         w_dst = [tile([P, T], F32, f"w_dst{t}") for t in range(PACK)]
-        for t in range(PACK):
+        for t in range(PACK - 1):
             nc.sync.dma_start(m_src[t][:], plane(mT, t))
         nc.sync.dma_start(w_dst[0][:, T // 2 :], plane(wT, 0)[:, T // 2 :])
+        nc.sync.dma_start(m_src[PACK - 1][:], plane(mT, PACK - 1))
+        nc.sync.dma_start(w_dst[1][:, T // 2 :], plane(wT, 1)[:, T // 2 :])
 
         w_g = tile([P, PACK, N], F32, "w_g")
         w_bf = tile([P, N, PACK], BF16, "w_bf")
@@ -102,7 +104,6 @@ def tile_attend_gkl_pl_mom_kernel(tc, xT, wT, y, wt, xm, mT, offs, out_0, out_1,
         gather_weights(3, slice(0, N))
         group_weights(slice(2, 4), slice(0, N))
         gather_weights(1, slice(0, N))
-        nc.vector.tensor_copy(w_dst[1][:, T // 2 :], w_src[1][:, T // 2 :])
         for slots in halves:
             gather_weights(0, slots)
         for slots in halves:
@@ -121,8 +122,8 @@ def tile_attend_gkl_pl_mom_kernel(tc, xT, wT, y, wt, xm, mT, offs, out_0, out_1,
                 ACT.Copy,
             )
         x_codes, x_scales = quantize("x", x_bf[:].rearrange("p j m t -> p (j m t)"), E4M3, PACK)
-        m_dst = [tile([P, T], F32, f"m_dst{t}", tag=f"table{(2, 0, 3, 1)[t]}") for t in range(PACK)]
-        for t in (0, 2, 3, 1):
+        m_dst = [tile([P, T], F32, f"m_dst{t}", tag=f"table{(0, 2, 3, 1)[t]}") for t in range(PACK)]
+        for t in (1, 2, 3, 0):
             nc.sync.dma_start(m_dst[t][:], plane(mT, t))
 
         target = [y_sb[j // 2][:, j % 2, :] for j in range(PACK)]
@@ -204,9 +205,7 @@ def tile_attend_gkl_pl_mom_kernel(tc, xT, wT, y, wt, xm, mT, offs, out_0, out_1,
         g_codes, g_scales = quantize("g", g_bf[:].rearrange("p c j -> p (c j)"), E5M2, 2)
         form_base(0, "g_bf")
         gather_drift(1)
-        form_base(1, None)
         gather_drift(2)
-        gather_drift(3)
 
         dw = []
         for t in range(PACK):
@@ -222,12 +221,10 @@ def tile_attend_gkl_pl_mom_kernel(tc, xT, wT, y, wt, xm, mT, offs, out_0, out_1,
                 stop=True,
             )
             dw.append(bank)
-        step = [tile([P, N], F32, f"step{t}", tag="momentum3" if t == 1 else None) for t in range(PACK)]
-        decayed = [tile([P, N], F32, f"decayed{t}") for t in range(2)]
+        step = [tile([P, N], F32, f"step{t}") for t in range(PACK)]
+        decayed = tile([P, N], F32, "decayed")
         for t in range(PACK):
             nc.scalar.activation(step[t][:], dw[t][:], ACT.Copy, scale=-LR)
-        for t in range(2):
-            nc.scalar.activation(decayed[t][:], drift[t][:], ACT.Copy, scale=-1.0 / LR)
 
         change = {}
 
@@ -243,11 +240,11 @@ def tile_attend_gkl_pl_mom_kernel(tc, xT, wT, y, wt, xm, mT, offs, out_0, out_1,
             for b in range(N // P):
                 cols = slice(b * P, (b + 1) * P)
                 nc.tensor.transpose(back[:, cols], turned_sb[:, cols], ident[:])
-            change[t] = tile([P, N], F32, f"change{t}")
+            change[t] = tile([P, N], F32, f"change{t}", tag="momentum3" if t == 2 else None)
             nc.scalar.copy(change[t][:], back[:])
+            return back
 
         chunks = [slice(a, a + CHUNK) for a in range(0, T, CHUNK)]
-        pairs = [tile([P, 2, CHUNK, 2], BF16, f"pairs{k}") for k in range(len(chunks))]
 
         def scatter_weights(t, first, second):
             nc.vector.tensor_tensor(w_dst[t][:].indirect(offsets[:]), first, second, ALU.add)
@@ -260,31 +257,36 @@ def tile_attend_gkl_pl_mom_kernel(tc, xT, wT, y, wt, xm, mT, offs, out_0, out_1,
             nc.vector.tensor_tensor(m_dst[t][:].indirect(offsets[:]), first, second, op)
             nc.sync.dma_start(plane(out_1, t), m_dst[t][:])
 
-        form_change(2, ("score0", "score1"))
-        form_change(3, ("score2", "score3"))
-        for t in (0, 1):
-            scatter_weights(t, base[t][:], step[t][:])
-        for t in (2, 3):
+        scatter_weights(0, base[0][:], step[0][:])
+        gather_drift(3)
+        first_back = form_change(1, ("score0", "score1"))
+        form_change(2, ("score2", "score3"))
+        form_change(3, ("dw1", "dw2"))
+        for t in (1, 2, 3):
             scatter_weights(t, w_g[:, t, :], change[t][:])
-        first_grad = tile([P, N], F32, "first_grad", tag="turned_sb3")
-        nc.scalar.activation(first_grad[:], dw[0][:], ACT.Copy)
+        first_new = tile([P, N], F32, "first_new", tag="turned_sb3")
+        nc.scalar.activation(first_new[:], first_back[:], ACT.Copy, scale=-1.0 / LR)
+        nc.scalar.activation(decayed[:], drift[0][:], ACT.Copy, scale=-1.0 / LR)
+        pair_tags = (None, None, "step3", "drift3")
+        pairs = [tile([P, 2, CHUNK, 2], BF16, f"pairs{k}", tag=pair_tags[k]) for k in range(len(chunks))]
         for t in range(PACK - 1):
             for k in range(len(chunks)):
                 cast_weights(t, k)
 
-        scatter_momentum(0, decayed[0][:], first_grad[:], ALU.add)
+        nc.vector.tensor_copy(m_dst[1][:].indirect(offsets[:]), first_new[:])
+        nc.sync.dma_start(plane(out_1, 1), m_dst[1][:])
         for t in (2, 3):
             scatter_momentum(t, change[t][:], undo_rate[:], ALU.mult)
 
-        out_codes = tile([P, T], U32, "out_codes", tag="change2")
+        out_codes = tile([P, T], U32, "out_codes", tag="momentum3")
         out_scales = tile([P, T], U8, "out_scales")
         words = out_2[0].rearrange("p c t -> p (c t)").bitcast(I32)
         for k, cols in enumerate(chunks):
             cast_weights(PACK - 1, k)
             grouped = tile([P, CHUNK * PACK], BF16, f"grouped{k}", tag=("x_raw0", "x_raw1", "w_bf", "x_bf")[k])
             nc.scalar.copy(
-                grouped[:].bitcast(U32).rearrange("p (c u) -> p c u", u=2),
-                pairs[k][:].rearrange("p u c e -> p (u c e)").bitcast(U32).rearrange("p (u c) -> p c u", u=2),
+                grouped[:].bitcast(U32).rearrange("p (c i u) -> p c u i", i=4, u=2),
+                pairs[k][:].rearrange("p u c e -> p (u c e)").bitcast(U32).rearrange("p (u c i) -> p c u i", u=2, i=4),
             )
             nc.vector.quantize_mx(
                 out=out_codes[:, cols].bitcast(E4M3),
@@ -296,6 +298,6 @@ def tile_attend_gkl_pl_mom_kernel(tc, xT, wT, y, wt, xm, mT, offs, out_0, out_1,
             nc.sync.dma_start(
                 out_3[0, 4 * q : 4 * q + 4, :].bitcast(I32), out_scales[32 * q : 32 * q + 4, :].bitcast(I32)
             )
-        last_grad = tile([P, N], F32, "last_grad", tag=f"pairs{len(chunks) - 1}")
-        nc.scalar.activation(last_grad[:], dw[1][:], ACT.Copy)
-        scatter_momentum(1, decayed[1][:], last_grad[:], ALU.add)
+        last_grad = tile([P, N], F32, "last_grad", tag=pair_tags[-1])
+        nc.scalar.activation(last_grad[:], dw[0][:], ACT.Copy)
+        scatter_momentum(0, decayed[:], last_grad[:], ALU.add)

@@ -1,7 +1,6 @@
 from contextlib import ExitStack
 
 import concourse.mybir as mybir
-from concourse.masks import make_identity
 
 D, T, N, R = 512, 2048, 512, 512
 LR, BETA = 0.1, 0.9
@@ -36,9 +35,9 @@ def tile_attend_gkl_pl_mom_kernel(tc, xT, wT, y, wt, xm, mT, offs, out_0, out_1,
         def plane(table, t):
             return table.rearrange("(p t) c -> p t c", t=PACK)[:, t, :]
 
-        def quantize(name, grouped, fmt, pieces, tag=None):
+        def quantize(name, grouped, fmt, pieces):
             width = grouped.shape[1] // PACK
-            codes = tile([P, width], U32, name + "_codes", tag=tag)
+            codes = tile([P, width], U32, name + "_codes")
             scales = tile([P, width], U8, name + "_scales")
             step = width // pieces
             for a in range(0, width, step):
@@ -49,12 +48,27 @@ def tile_attend_gkl_pl_mom_kernel(tc, xT, wT, y, wt, xm, mT, offs, out_0, out_1,
                 )
             return codes, scales
 
+        def product(bank, lhs, lhs_fmt, cols, rhs, rhs_fmt):
+            nc.tensor.matmul_mx(
+                out=bank[:],
+                lhsT=lhs[0][:, cols].bitcast(lhs_fmt),
+                lhsT_scale=lhs[1][:, cols],
+                rhs=rhs[0][:].bitcast(rhs_fmt),
+                rhs_scale=rhs[1][:],
+                start=True,
+                stop=True,
+            )
+
+        halves = (slice(0, N // 2), slice(N // 2, N))
         offsets = tile([P, N // 16], U16, "offsets")
-        arrival = (2, 3, 1, 0)
-        w_src = {t: tile([P, T], F32, f"w_src{t}", tag=f"table{t}") for t in arrival}
-        nc.sync.dma_start(w_src[arrival[0]][:], plane(wT, arrival[0]))
+
+        def listed(slots):
+            return offsets[:, slots.start // 16 : slots.stop // 16]
+
+        w_src = [tile([P, T], F32, f"w_src{t}") for t in range(PACK)]
+        nc.sync.dma_start(w_src[0][:], plane(wT, 0))
         nc.sync.dma_start(offsets[:], offs)
-        for t in arrival[1:]:
+        for t in range(1, PACK):
             nc.sync.dma_start(w_src[t][:], plane(wT, t))
 
         warm_in = tile([P, 1], F32, "warm_in")
@@ -62,10 +76,6 @@ def tile_attend_gkl_pl_mom_kernel(tc, xT, wT, y, wt, xm, mT, offs, out_0, out_1,
         nc.vector.memset(warm_in[:], 0.0)
         nc.scalar.activation(warm_out[:], warm_in[:], ACT.Exp)
 
-        ident = tile([P, P], F32, "ident")
-        make_identity(nc, ident[:])
-        undo_rate = tile([P, N], F32, "undo_rate")
-        nc.gpsimd.memset(undo_rate[:], -1.0 / LR)
         half = R // 2
         x_rows = xT[0].rearrange("(p t) r -> p t r", t=PACK)
         x_raw = [tile([P, PACK, half], F32, f"x_raw{h}") for h in range(2)]
@@ -73,58 +83,53 @@ def tile_attend_gkl_pl_mom_kernel(tc, xT, wT, y, wt, xm, mT, offs, out_0, out_1,
             nc.sync.dma_start(x_raw[h][:], x_rows[:, :, h * half : (h + 1) * half])
         wt_sb = tile([P, PACK], F32, "wt_sb")
         nc.sync.dma_start(wt_sb[:], wt[0].rearrange("(p j) one -> p (j one)", j=PACK))
-        xm_raw = tile([P, PACK, D], F32, "xm_raw")
         y_sb = [tile([P, 2, N], F32, f"y_sb{h}") for h in range(2)]
-        m_src = [tile([P, T], F32, f"m_src{t}", tag=f"momentum{t}") for t in range(PACK)]
         for h in range(2):
             nc.sync.dma_start(y_sb[h][:], y[0].rearrange("(p j) i -> p j i", j=PACK)[:, 2 * h : 2 * h + 2, :])
+        xm_raw = tile([P, PACK, D], F32, "xm_raw")
         nc.sync.dma_start(xm_raw[:], xm[0].rearrange("(p j) d -> p j d", j=PACK))
-        w_dst = [tile([P, T], F32, f"w_dst{t}") for t in range(PACK)]
+        m_src = [tile([P, T], F32, f"m_src{t}") for t in range(PACK)]
+        m_dst = {1: tile([P, T], F32, "m_dst1")}
         for t in range(PACK - 1):
             nc.sync.dma_start(m_src[t][:], plane(mT, t))
-        nc.sync.dma_start(w_dst[0][:, T // 2 :], plane(wT, 0)[:, T // 2 :])
+        nc.sync.dma_start(m_dst[1][:], plane(mT, 1))
         nc.sync.dma_start(m_src[PACK - 1][:], plane(mT, PACK - 1))
-        nc.sync.dma_start(w_dst[1][:, T // 2 :], plane(wT, 1)[:, T // 2 :])
 
-        w_g = tile([P, PACK, N], F32, "w_g")
+        w_pair = [tile([P, 2, N], F32, f"w_pair{u}") for u in range(2)]
+        w_g = [w_pair[t // 2][:, t % 2, :] for t in range(PACK)]
         w_bf = tile([P, N, PACK], BF16, "w_bf")
 
         def gather_weights(t, slots):
-            listed = offsets[:, slots.start // 16 : slots.stop // 16]
-            nc.vector.tensor_copy(w_g[:, t, slots], w_src[t][:].indirect(listed))
+            nc.vector.tensor_copy(w_g[t][:, slots], w_src[t][:].indirect(listed(slots)))
 
-        def group_weights(pair, slots):
+        def group_weights(u, slots):
             nc.vector.tensor_copy(
-                w_bf[:, slots, pair].rearrange("p (c i) t -> p c t i", i=4),
-                w_g[:, pair, slots].rearrange("p t (c i) -> p c t i", i=4),
+                w_bf[:, slots, 2 * u : 2 * u + 2].rearrange("p (c i) t -> p c t i", i=4),
+                w_pair[u][:, :, slots].rearrange("p t (c i) -> p c t i", i=4),
             )
 
-        halves = (slice(0, N // 2), slice(N // 2, N))
-        gather_weights(2, slice(0, N))
-        gather_weights(3, slice(0, N))
-        group_weights(slice(2, 4), slice(0, N))
+        gather_weights(0, slice(0, N))
         gather_weights(1, slice(0, N))
+        group_weights(0, slice(0, N))
+        gather_weights(2, slice(0, N))
         for slots in halves:
-            gather_weights(0, slots)
+            gather_weights(3, slots)
         for slots in halves:
-            group_weights(slice(0, 2), slots)
-        for t in arrival:
-            width = T if t > 1 else T // 2
-            nc.scalar.activation(w_dst[t][:, :width], w_src[t][:, :width], ACT.Copy)
-
-        w_codes, w_scales = quantize("w", w_bf[:].rearrange("p c t -> p (c t)"), E4M3, 2)
+            group_weights(1, slots)
+        w_dst = [tile([P, T], F32, f"w_dst{t}") for t in range(PACK)]
+        for t in range(PACK):
+            nc.scalar.activation(w_dst[t][:], w_src[t][:], ACT.Copy)
+        w_mx = quantize("w", w_bf[:].rearrange("p c t -> p (c t)"), E4M3, 2)
 
         x_bf = tile([P, PACK, P, PACK], BF16, "x_bf")
-        for h, tiles in ((0, slice(0, 4)), (1, slice(0, 2)), (1, slice(2, 4))):
-            nc.scalar.activation(
-                x_bf[:, tiles, h * (P // 2) : (h + 1) * (P // 2), :].rearrange("p j m t -> p m t j"),
-                x_raw[h][:].rearrange("p t (m j) -> p m t j", j=PACK)[:, :, :, tiles],
-                ACT.Copy,
-            )
-        x_codes, x_scales = quantize("x", x_bf[:].rearrange("p j m t -> p (j m t)"), E4M3, PACK)
-        m_dst = [tile([P, T], F32, f"m_dst{t}", tag=f"table{(0, 2, 3, 1)[t]}") for t in range(PACK)]
-        for t in (1, 2, 3, 0):
-            nc.sync.dma_start(m_dst[t][:], plane(mT, t))
+        for h in range(2):
+            dealt = x_bf[:, :, h * (P // 2) : (h + 1) * (P // 2), :].rearrange("p j m t -> p m t j")
+            given = x_raw[h][:].rearrange("p t (m j) -> p m t j", j=PACK)
+            if h == 0:
+                nc.scalar.activation(dealt, given, ACT.Copy)
+            else:
+                nc.vector.tensor_copy(dealt, given)
+        x_mx = quantize("x", x_bf[:].rearrange("p j m t -> p (j m t)"), E4M3, PACK)
 
         target = [y_sb[j // 2][:, j % 2, :] for j in range(PACK)]
         for j in range(2):
@@ -132,7 +137,7 @@ def tile_attend_gkl_pl_mom_kernel(tc, xT, wT, y, wt, xm, mT, offs, out_0, out_1,
         for j in range(2, PACK):
             nc.gpsimd.tensor_scalar(target[j], target[j], wt_sb[:, j : j + 1], 0.0, ALU.mult, ALU.add)
 
-        neg_max = tile([P, PACK], F32, "neg_max", tag="xm_bf")
+        neg_max = tile([P, PACK], F32, "neg_max")
         inv = tile([P, PACK], F32, "inv")
         coef = {}
         e = [tile([P, N], F32, f"e{j}") for j in range(PACK)]
@@ -140,16 +145,7 @@ def tile_attend_gkl_pl_mom_kernel(tc, xT, wT, y, wt, xm, mT, offs, out_0, out_1,
         g_rows = tile([P, PACK, N], BF16, "g_rows")
         for j in range(PACK):
             score = psum.tile([P, N], F32, name=f"score{j}")
-            cols = slice(j * P, (j + 1) * P)
-            nc.tensor.matmul_mx(
-                out=score[:],
-                lhsT=x_codes[:, cols].bitcast(E4M3),
-                lhsT_scale=x_scales[:, cols],
-                rhs=w_codes[:].bitcast(E4M3),
-                rhs_scale=w_scales[:],
-                start=True,
-                stop=True,
-            )
+            product(score, x_mx, E4M3, slice(j * P, (j + 1) * P), w_mx, E4M3)
             if j == PACK - 1:
                 nc.vector.reciprocal(inv[:, :2], sums[:, :2])
             nc.vector.tensor_reduce(neg_max[:, j : j + 1], score[:], AXIS.X, ALU.max, negate=True)
@@ -170,12 +166,12 @@ def tile_attend_gkl_pl_mom_kernel(tc, xT, wT, y, wt, xm, mT, offs, out_0, out_1,
         form_coef(nc.gpsimd, 0)
         gradient_rows(0)
         nc.vector.reciprocal(inv[:, 2:], sums[:, 2:])
-        gradient_rows(1, slice(0, N // 2))
+        gradient_rows(1, halves[0])
         form_coef(nc.vector, 2)
-        gradient_rows(1, slice(N // 2, N))
-        for a in range(0, N, N // 2):
+        gradient_rows(1, halves[1])
+        for cols in halves:
             for j in range(2, PACK):
-                gradient_rows(j, slice(a, a + N // 2))
+                gradient_rows(j, cols)
 
         xm_bf = tile([P, PACK, P, PACK], BF16, "xm_bf")
         for h in range(2):
@@ -185,119 +181,93 @@ def tile_attend_gkl_pl_mom_kernel(tc, xT, wT, y, wt, xm, mT, offs, out_0, out_1,
                 ACT.Copy,
             )
         g_bf = tile([P, N, PACK], BF16, "g_bf")
-        for a in range(0, N, N // 2):
-            nc.scalar.copy(
-                g_bf[:, a : a + N // 2, :].rearrange("p (c i) j -> p c j i", i=4),
-                g_rows[:, :, a : a + N // 2].rearrange("p j (c i) -> p c j i", i=4),
+        for cols in halves:
+            nc.vector.tensor_copy(
+                g_bf[:, cols, :].rearrange("p (c i) j -> p c j i", i=4),
+                g_rows[:, :, cols].rearrange("p j (c i) -> p c j i", i=4),
             )
-        drift = [tile([P, N], F32, f"drift{t}", tag="e2" if t == 0 else None) for t in range(PACK)]
-        base = {}
-
-        def gather_drift(t):
-            nc.vector.tensor_scalar(drift[t][:], m_src[t][:].indirect(offsets[:]), -LR * BETA, 0.0, ALU.mult, ALU.add)
-
-        def form_base(t, tag):
-            base[t] = tile([P, N], F32, f"base{t}", tag=tag)
-            nc.gpsimd.tensor_tensor(base[t][:], w_g[:, t, :], drift[t][:], ALU.add)
-
-        xm_codes, xm_scales = quantize("xm", xm_bf[:].rearrange("p t m j -> p (t m j)"), E4M3, 1)
-        gather_drift(0)
-        g_codes, g_scales = quantize("g", g_bf[:].rearrange("p c j -> p (c j)"), E5M2, 2)
-        form_base(0, "g_bf")
-        gather_drift(1)
-        gather_drift(2)
+        xm_mx = quantize("xm", xm_bf[:].rearrange("p t m j -> p (t m j)"), E4M3, 1)
+        g_mx = quantize("g", g_bf[:].rearrange("p c j -> p (c j)"), E5M2, 2)
 
         dw = []
         for t in range(PACK):
             bank = psum.tile([P, N], F32, name=f"dw{t}")
-            cols = slice(t * P, (t + 1) * P)
-            nc.tensor.matmul_mx(
-                out=bank[:],
-                lhsT=xm_codes[:, cols].bitcast(E4M3),
-                lhsT_scale=xm_scales[:, cols],
-                rhs=g_codes[:].bitcast(E5M2),
-                rhs_scale=g_scales[:],
-                start=True,
-                stop=True,
-            )
+            product(bank, xm_mx, E4M3, slice(t * P, (t + 1) * P), g_mx, E5M2)
             dw.append(bank)
-        step = [tile([P, N], F32, f"step{t}") for t in range(PACK)]
-        decayed = tile([P, N], F32, "decayed")
-        for t in range(PACK):
-            nc.scalar.activation(step[t][:], dw[t][:], ACT.Copy, scale=-LR)
 
+        drift = [tile([P, N], F32, f"drift{t}") for t in range(PACK)]
+        for t in range(2):
+            nc.scalar.activation(drift[t][:], m_src[t][:].indirect(offsets[:]), ACT.Copy, scale=-LR * BETA)
         change = {}
 
-        def form_change(t, banks):
-            turned = psum.tile([P, N], F32, name=f"turned{t}", tag=banks[0])
-            for b in range(N // P):
-                cols = slice(b * P, (b + 1) * P)
-                for i, term in enumerate((drift[t][:, cols], step[t][:, cols])):
-                    nc.tensor.matmul(turned[:, cols], term, ident[:], is_transpose=True, start=i == 0, stop=i == 1)
-            turned_sb = tile([P, N], F32, f"turned_sb{t}")
-            nc.scalar.copy(turned_sb[:], turned[:])
-            back = psum.tile([P, N], F32, name=f"back{t}", tag=banks[1])
-            for b in range(N // P):
-                cols = slice(b * P, (b + 1) * P)
-                nc.tensor.transpose(back[:, cols], turned_sb[:, cols], ident[:])
-            change[t] = tile([P, N], F32, f"change{t}", tag="momentum3" if t == 2 else None)
-            nc.scalar.copy(change[t][:], back[:])
-            return back
+        def gather_drift(t):
+            nc.vector.tensor_scalar(drift[t][:], m_src[t][:].indirect(offsets[:]), -LR * BETA, 0.0, ALU.mult, ALU.add)
 
-        chunks = [slice(a, a + CHUNK) for a in range(0, T, CHUNK)]
+        def form_change(t, tag=None):
+            change[t] = tile([P, N], F32, f"change{t}", tag=tag)
+            nc.vector.scalar_tensor_tensor(change[t][:], dw[t][:], -LR, drift[t][:], ALU.mult, ALU.add)
 
-        def scatter_weights(t, first, second):
-            nc.vector.tensor_tensor(w_dst[t][:].indirect(offsets[:]), first, second, ALU.add)
+        def scalar_scatter(window, values, scale):
+            for slots in halves:
+                nc.scalar.activation(window[:].indirect(listed(slots)), values[:, slots], ACT.Copy, scale=scale)
+
+        def weights_by_scalar(t):
+            new = tile([P, N], F32, f"w_new{t}")
+            nc.vector.tensor_tensor(new[:], w_g[t], change[t][:], ALU.add)
+            scalar_scatter(w_dst[t], new, 1.0)
             nc.sync.dma_start(plane(out_0, t), w_dst[t][:])
 
-        def cast_weights(t, k):
-            nc.scalar.activation(pairs[k][:, t // 2, :, t % 2], w_dst[t][:, chunks[k]], ACT.Copy)
+        def weights_by_vector(t):
+            nc.vector.tensor_tensor(w_dst[t][:].indirect(offsets[:]), w_g[t], change[t][:], ALU.add)
+            nc.sync.dma_start(plane(out_0, t), w_dst[t][:])
 
-        def scatter_momentum(t, first, second, op):
-            nc.vector.tensor_tensor(m_dst[t][:].indirect(offsets[:]), first, second, op)
+        def scatter_momentum(t):
+            scalar_scatter(m_dst[t], change[t], -1.0 / LR)
             nc.sync.dma_start(plane(out_1, t), m_dst[t][:])
 
-        scatter_weights(0, base[0][:], step[0][:])
+        m_dst[0] = tile([P, T], F32, "m_dst0", tag="g_bf")
+        nc.vector.tensor_copy(m_dst[0][:], m_src[0][:])
+        form_change(0, tag="m_src1")
+        weights_by_scalar(0)
+        form_change(1)
+        weights_by_vector(1)
+        scatter_momentum(0)
+        gather_drift(2)
+        form_change(2)
+        weights_by_scalar(2)
+        m_dst[2] = tile([P, T], F32, "m_dst2", tag="drift2")
+        nc.vector.tensor_copy(m_dst[2][:], m_src[2][:])
         gather_drift(3)
-        first_back = form_change(1, ("score0", "score1"))
-        form_change(2, ("score2", "score3"))
-        form_change(3, ("dw1", "dw2"))
-        for t in (1, 2, 3):
-            scatter_weights(t, w_g[:, t, :], change[t][:])
-        first_new = tile([P, N], F32, "first_new", tag="turned_sb3")
-        nc.scalar.activation(first_new[:], first_back[:], ACT.Copy, scale=-1.0 / LR)
-        nc.scalar.activation(decayed[:], drift[0][:], ACT.Copy, scale=-1.0 / LR)
-        pair_tags = (None, None, "step3", "drift3")
-        pairs = [tile([P, 2, CHUNK, 2], BF16, f"pairs{k}", tag=pair_tags[k]) for k in range(len(chunks))]
-        for t in range(PACK - 1):
-            for k in range(len(chunks)):
-                cast_weights(t, k)
+        form_change(3)
+        weights_by_vector(3)
+        scatter_momentum(1)
+        scatter_momentum(2)
+        m_dst[3] = tile([P, T], F32, "m_dst3", tag="change2")
+        nc.scalar.activation(m_dst[3][:], m_src[3][:], ACT.Copy)
+        scatter_momentum(3)
 
-        nc.vector.tensor_copy(m_dst[1][:].indirect(offsets[:]), first_new[:])
-        nc.sync.dma_start(plane(out_1, 1), m_dst[1][:])
-        for t in (2, 3):
-            scatter_momentum(t, change[t][:], undo_rate[:], ALU.mult)
-
-        out_codes = tile([P, T], U32, "out_codes", tag="momentum3")
+        rounded = tile([P, PACK, T], BF16, "rounded", tag="w_pair1")
+        out_codes = tile([P, T], U32, "out_codes", tag="w_src0")
         out_scales = tile([P, T], U8, "out_scales")
         words = out_2[0].rearrange("p c t -> p (c t)").bitcast(I32)
-        for k, cols in enumerate(chunks):
-            cast_weights(PACK - 1, k)
-            grouped = tile([P, CHUNK * PACK], BF16, f"grouped{k}", tag=("x_raw0", "x_raw1", "w_bf", "x_bf")[k])
-            nc.scalar.copy(
-                grouped[:].bitcast(U32).rearrange("p (c i u) -> p c u i", i=4, u=2),
-                pairs[k][:].rearrange("p u c e -> p (u c e)").bitcast(U32).rearrange("p (u c i) -> p c u i", u=2, i=4),
+        for k, a in enumerate(range(0, T, CHUNK)):
+            cols = slice(a, a + CHUNK)
+            if k % 2 == 0:
+                wide = slice(a, a + 2 * CHUNK)
+                for t in range(PACK):
+                    nc.vector.tensor_copy(rounded[:, t, wide], w_dst[t][:, wide])
+            grouped = tile([P, CHUNK, PACK], BF16, f"grouped{k}", tag=("w_src1", "w_src2", "w_src3", "x_raw0")[k])
+            nc.vector.tensor_copy(
+                grouped[:].rearrange("p (c i) t -> p c t i", i=4),
+                rounded[:, :, cols].rearrange("p t (c i) -> p c t i", i=4),
             )
             nc.vector.quantize_mx(
                 out=out_codes[:, cols].bitcast(E4M3),
                 scales=out_scales[:, cols],
-                in_=grouped[:],
+                in_=grouped[:].rearrange("p c t -> p (c t)"),
             )
             nc.sync.dma_start(words[:, cols], out_codes[:, cols].bitcast(I32))
         for q in range(4):
             nc.sync.dma_start(
                 out_3[0, 4 * q : 4 * q + 4, :].bitcast(I32), out_scales[32 * q : 32 * q + 4, :].bitcast(I32)
             )
-        last_grad = tile([P, N], F32, "last_grad", tag=pair_tags[-1])
-        nc.scalar.activation(last_grad[:], dw[0][:], ACT.Copy)
-        scatter_momentum(0, decayed[:], last_grad[:], ALU.add)

@@ -35,18 +35,21 @@ def tile_attend_gkl_pl_mom_kernel(tc, xT, wT, y, wt, xm, mT, offs, out_0, out_1,
         def plane(table, t):
             return table.rearrange("(p t) c -> p t c", t=PACK)[:, t, :]
 
+        def operand(name):
+            return tile([P, N], U32, name + "_codes"), tile([P, N], U8, name + "_scales")
+
+        def quantize_part(mx, grouped, fmt, cols):
+            nc.vector.quantize_mx(
+                out=mx[0][:, cols].bitcast(fmt),
+                scales=mx[1][:, cols],
+                in_=grouped[:, PACK * cols.start : PACK * cols.stop],
+            )
+
         def quantize(name, grouped, fmt, pieces):
-            width = grouped.shape[1] // PACK
-            codes = tile([P, width], U32, name + "_codes")
-            scales = tile([P, width], U8, name + "_scales")
-            step = width // pieces
-            for a in range(0, width, step):
-                nc.vector.quantize_mx(
-                    out=codes[:, a : a + step].bitcast(fmt),
-                    scales=scales[:, a : a + step],
-                    in_=grouped[:, PACK * a : PACK * (a + step)],
-                )
-            return codes, scales
+            mx = operand(name)
+            for a in range(0, N, N // pieces):
+                quantize_part(mx, grouped, fmt, slice(a, a + N // pieces))
+            return mx
 
         def product(bank, lhs, lhs_fmt, cols, rhs, rhs_fmt):
             nc.tensor.matmul_mx(
@@ -83,17 +86,20 @@ def tile_attend_gkl_pl_mom_kernel(tc, xT, wT, y, wt, xm, mT, offs, out_0, out_1,
             nc.sync.dma_start(x_raw[h][:], x_rows[:, :, h * half : (h + 1) * half])
         wt_sb = tile([P, PACK], F32, "wt_sb")
         nc.sync.dma_start(wt_sb[:], wt[0].rearrange("(p j) one -> p (j one)", j=PACK))
+        xm_rows = xm[0].rearrange("(p j) d -> p j d", j=PACK)
+        xm_raw = [tile([P, PACK, D // 2], F32, f"xm_raw{h}") for h in range(2)]
+        nc.sync.dma_start(xm_raw[0][:], xm_rows[:, :, : D // 2])
         y_sb = [tile([P, 2, N], F32, f"y_sb{h}") for h in range(2)]
         for h in range(2):
             nc.sync.dma_start(y_sb[h][:], y[0].rearrange("(p j) i -> p j i", j=PACK)[:, 2 * h : 2 * h + 2, :])
-        xm_raw = tile([P, PACK, D], F32, "xm_raw")
-        nc.sync.dma_start(xm_raw[:], xm[0].rearrange("(p j) d -> p j d", j=PACK))
+        nc.sync.dma_start(xm_raw[1][:], xm_rows[:, :, D // 2 :])
         m_src = [tile([P, T], F32, f"m_src{t}") for t in range(PACK)]
-        m_dst = {1: tile([P, T], F32, "m_dst1")}
-        for t in range(PACK - 1):
+        m_dst = {t: tile([P, T], F32, f"m_dst{t}") for t in range(2)}
+        w_dst = [tile([P, T], F32, f"w_dst{t}") for t in range(PACK)]
+        for t in range(PACK):
             nc.sync.dma_start(m_src[t][:], plane(mT, t))
-        nc.sync.dma_start(m_dst[1][:], plane(mT, 1))
-        nc.sync.dma_start(m_src[PACK - 1][:], plane(mT, PACK - 1))
+        for t in range(2):
+            nc.sync.dma_start(m_dst[t][:], plane(mT, t))
 
         w_pair = [tile([P, 2, N], F32, f"w_pair{u}") for u in range(2)]
         w_g = [w_pair[t // 2][:, t % 2, :] for t in range(PACK)]
@@ -116,9 +122,10 @@ def tile_attend_gkl_pl_mom_kernel(tc, xT, wT, y, wt, xm, mT, offs, out_0, out_1,
             gather_weights(3, slots)
         for slots in halves:
             group_weights(1, slots)
-        w_dst = [tile([P, T], F32, f"w_dst{t}") for t in range(PACK)]
+        early = 3 * T // 4
         for t in range(PACK):
-            nc.scalar.activation(w_dst[t][:], w_src[t][:], ACT.Copy)
+            width = early if t == PACK - 1 else T
+            nc.scalar.activation(w_dst[t][:, :width], w_src[t][:, :width], ACT.Copy)
         w_mx = quantize("w", w_bf[:].rearrange("p c t -> p (c t)"), E4M3, 2)
 
         x_bf = tile([P, PACK, P, PACK], BF16, "x_bf")
@@ -129,12 +136,21 @@ def tile_attend_gkl_pl_mom_kernel(tc, xT, wT, y, wt, xm, mT, offs, out_0, out_1,
                 nc.scalar.activation(dealt, given, ACT.Copy)
             else:
                 nc.vector.tensor_copy(dealt, given)
+        nc.scalar.activation(w_dst[PACK - 1][:, early:], w_src[PACK - 1][:, early:], ACT.Copy)
         x_mx = quantize("x", x_bf[:].rearrange("p j m t -> p (j m t)"), E4M3, PACK)
 
+        xm_bf = tile([P, PACK, P, PACK], BF16, "xm_bf")
+
+        def cast_xm(h):
+            nc.scalar.activation(
+                xm_bf[:, :, h * (P // 2) : (h + 1) * (P // 2), :].rearrange("p t m j -> p m j t"),
+                xm_raw[h][:].rearrange("p j (m t) -> p m j t", t=PACK),
+                ACT.Copy,
+            )
+
+        cast_xm(0)
         target = [y_sb[j // 2][:, j % 2, :] for j in range(PACK)]
         for j in range(2):
-            nc.scalar.activation(target[j], target[j], ACT.Copy, scale=wt_sb[:, j : j + 1])
-        for j in range(2, PACK):
             nc.gpsimd.tensor_scalar(target[j], target[j], wt_sb[:, j : j + 1], 0.0, ALU.mult, ALU.add)
 
         neg_max = tile([P, PACK], F32, "neg_max")
@@ -152,6 +168,9 @@ def tile_attend_gkl_pl_mom_kernel(tc, xT, wT, y, wt, xm, mT, offs, out_0, out_1,
             nc.scalar.activation(
                 e[j][:], score[:], ACT.Exp, bias=neg_max[:, j : j + 1], scale=1.0, accum_out=sums[:, j : j + 1]
             )
+
+        for j in range(2, PACK):
+            nc.scalar.activation(target[j], target[j], ACT.Copy, scale=wt_sb[:, j : j + 1])
 
         def gradient_rows(j, cols=slice(0, N)):
             nc.vector.scalar_tensor_tensor(
@@ -173,21 +192,18 @@ def tile_attend_gkl_pl_mom_kernel(tc, xT, wT, y, wt, xm, mT, offs, out_0, out_1,
             for j in range(2, PACK):
                 gradient_rows(j, cols)
 
-        xm_bf = tile([P, PACK, P, PACK], BF16, "xm_bf")
-        for h in range(2):
-            nc.scalar.activation(
-                xm_bf[:, :, h * (P // 2) : (h + 1) * (P // 2), :].rearrange("p t m j -> p m j t"),
-                xm_raw[:, :, h * (D // 2) : (h + 1) * (D // 2)].rearrange("p j (m t) -> p m j t", t=PACK),
-                ACT.Copy,
-            )
+        cast_xm(1)
         g_bf = tile([P, N, PACK], BF16, "g_bf")
         for cols in halves:
             nc.vector.tensor_copy(
                 g_bf[:, cols, :].rearrange("p (c i) j -> p c j i", i=4),
                 g_rows[:, :, cols].rearrange("p j (c i) -> p c j i", i=4),
             )
-        xm_mx = quantize("xm", xm_bf[:].rearrange("p t m j -> p (t m j)"), E4M3, 1)
+        xm_mx = operand("xm")
+        xm_grouped = xm_bf[:].rearrange("p t m j -> p (t m j)")
+        quantize_part(xm_mx, xm_grouped, E4M3, slice(0, P))
         g_mx = quantize("g", g_bf[:].rearrange("p c j -> p (c j)"), E5M2, 2)
+        quantize_part(xm_mx, xm_grouped, E4M3, slice(P, D))
 
         dw = []
         for t in range(PACK):
@@ -195,12 +211,13 @@ def tile_attend_gkl_pl_mom_kernel(tc, xT, wT, y, wt, xm, mT, offs, out_0, out_1,
             product(bank, xm_mx, E4M3, slice(t * P, (t + 1) * P), g_mx, E5M2)
             dw.append(bank)
 
-        drift = [tile([P, N], F32, f"drift{t}") for t in range(PACK)]
+        drift = {t: tile([P, N], F32, f"drift{t}") for t in range(2)}
         for t in range(2):
             nc.scalar.activation(drift[t][:], m_src[t][:].indirect(offsets[:]), ACT.Copy, scale=-LR * BETA)
         change = {}
 
         def gather_drift(t):
+            drift[t] = tile([P, N], F32, f"drift{t}", tag=None)
             nc.vector.tensor_scalar(drift[t][:], m_src[t][:].indirect(offsets[:]), -LR * BETA, 0.0, ALU.mult, ALU.add)
 
         def form_change(t, tag=None):
@@ -211,10 +228,14 @@ def tile_attend_gkl_pl_mom_kernel(tc, xT, wT, y, wt, xm, mT, offs, out_0, out_1,
             for slots in halves:
                 nc.scalar.activation(window[:].indirect(listed(slots)), values[:, slots], ACT.Copy, scale=scale)
 
+        w_new = {}
+
+        def form_weights(t):
+            w_new[t] = tile([P, N], F32, f"w_new{t}", tag=None)
+            nc.gpsimd.tensor_tensor(w_new[t][:], w_g[t], change[t][:], ALU.add)
+
         def weights_by_scalar(t):
-            new = tile([P, N], F32, f"w_new{t}")
-            nc.vector.tensor_tensor(new[:], w_g[t], change[t][:], ALU.add)
-            scalar_scatter(w_dst[t], new, 1.0)
+            scalar_scatter(w_dst[t], w_new[t], 1.0)
             nc.sync.dma_start(plane(out_0, t), w_dst[t][:])
 
         def weights_by_vector(t):
@@ -225,49 +246,66 @@ def tile_attend_gkl_pl_mom_kernel(tc, xT, wT, y, wt, xm, mT, offs, out_0, out_1,
             scalar_scatter(m_dst[t], change[t], -1.0 / LR)
             nc.sync.dma_start(plane(out_1, t), m_dst[t][:])
 
-        m_dst[0] = tile([P, T], F32, "m_dst0", tag="g_bf")
-        nc.vector.tensor_copy(m_dst[0][:], m_src[0][:])
-        form_change(0, tag="m_src1")
+        def copy_momentum(t, tag):
+            m_dst[t] = tile([P, T], F32, f"m_dst{t}", tag=tag)
+            nc.vector.tensor_copy(m_dst[t][:], m_src[t][:])
+
+        base = tile([P, N], F32, "base")
+        nc.gpsimd.tensor_tensor(base[:], w_g[0], drift[0][:], ALU.add)
+        w_new[0] = tile([P, N], F32, "w_new0", tag="m_src1")
+        nc.vector.scalar_tensor_tensor(w_new[0][:], dw[0][:], -LR, base[:], ALU.mult, ALU.add)
         weights_by_scalar(0)
-        form_change(1)
-        weights_by_vector(1)
-        scatter_momentum(0)
-        gather_drift(2)
-        form_change(2)
-        weights_by_scalar(2)
-        m_dst[2] = tile([P, T], F32, "m_dst2", tag="drift2")
-        nc.vector.tensor_copy(m_dst[2][:], m_src[2][:])
+        for t in (1, 2):
+            if t > 1:
+                gather_drift(t)
+            form_change(t)
+            form_weights(t)
+            weights_by_scalar(t)
         gather_drift(3)
         form_change(3)
         weights_by_vector(3)
-        scatter_momentum(1)
-        scatter_momentum(2)
-        m_dst[3] = tile([P, T], F32, "m_dst3", tag="change2")
-        nc.scalar.activation(m_dst[3][:], m_src[3][:], ACT.Copy)
-        scatter_momentum(3)
-
-        rounded = tile([P, PACK, T], BF16, "rounded", tag="w_pair1")
+        form_change(0, tag="w_pair1")
+        for t in range(2):
+            scatter_momentum(t)
+        rounded = tile([P, PACK, T], BF16, "rounded", tag="drift0")
+        for t in (0, 1, 3):
+            nc.vector.tensor_copy(rounded[:, t, :], w_dst[t][:])
         out_codes = tile([P, T], U32, "out_codes", tag="w_src0")
-        out_scales = tile([P, T], U8, "out_scales")
+        out_scales = tile([P, CHUNK], U8, "out_scales")
         words = out_2[0].rearrange("p c t -> p (c t)").bitcast(I32)
+        group_tags = ("w_src1", "w_src2", "w_src3", "x_raw0")
         for k, a in enumerate(range(0, T, CHUNK)):
             cols = slice(a, a + CHUNK)
             if k % 2 == 0:
                 wide = slice(a, a + 2 * CHUNK)
-                for t in range(PACK):
-                    nc.vector.tensor_copy(rounded[:, t, wide], w_dst[t][:, wide])
-            grouped = tile([P, CHUNK, PACK], BF16, f"grouped{k}", tag=("w_src1", "w_src2", "w_src3", "x_raw0")[k])
+                nc.vector.tensor_copy(rounded[:, 2, wide], w_dst[2][:, wide])
+            grouped = tile([P, CHUNK, PACK], BF16, f"grouped{k}", tag=group_tags[k])
             nc.vector.tensor_copy(
                 grouped[:].rearrange("p (c i) t -> p c t i", i=4),
                 rounded[:, :, cols].rearrange("p t (c i) -> p c t i", i=4),
             )
+            if k == 3:
+                last_new = tile([P, N // 2], F32, "last_new", tag="drift0")
+                nc.vector.tensor_scalar(last_new[:], change[3][:, halves[1]], -1.0 / LR, 0.0, ALU.mult, ALU.add)
             nc.vector.quantize_mx(
                 out=out_codes[:, cols].bitcast(E4M3),
-                scales=out_scales[:, cols],
+                scales=out_scales[4 * k :, :],
                 in_=grouped[:].rearrange("p c t -> p (c t)"),
             )
-            nc.sync.dma_start(words[:, cols], out_codes[:, cols].bitcast(I32))
+            if k % 2 == 1:
+                nc.sync.dma_start(words[:, wide], out_codes[:, wide].bitcast(I32))
+            if k == 0:
+                copy_momentum(2, group_tags[k])
+            if k == 1:
+                scatter_momentum(2)
+                copy_momentum(3, group_tags[k])
+                nc.scalar.activation(
+                    m_dst[3][:].indirect(listed(halves[0])), change[3][:, halves[0]], ACT.Copy, scale=-1.0 / LR
+                )
         for q in range(4):
             nc.sync.dma_start(
-                out_3[0, 4 * q : 4 * q + 4, :].bitcast(I32), out_scales[32 * q : 32 * q + 4, :].bitcast(I32)
+                out_3[0, 4 * q : 4 * q + 4, :].bitcast(I32).rearrange("r (k c) -> k r c", k=4),
+                out_scales[32 * q : 32 * q + 16, :].bitcast(I32),
             )
+        nc.vector.tensor_copy(m_dst[3][:].indirect(listed(halves[1])), last_new[:])
+        nc.sync.dma_start(plane(out_1, 3), m_dst[3][:])

@@ -51,13 +51,13 @@ def tile_attend_gkl_pl_mom_kernel(tc, xT, wT, y, wt, xm, mT, offs, out_0, out_1,
                 quantize_part(mx, grouped, fmt, slice(a, a + N // pieces))
             return mx
 
-        def product(bank, lhs, lhs_fmt, cols, rhs, rhs_fmt):
+        def product(bank, lhs, lhs_fmt, cols, rhs, rhs_fmt, slots=slice(0, N)):
             nc.tensor.matmul_mx(
                 out=bank[:],
                 lhsT=lhs[0][:, cols].bitcast(lhs_fmt),
                 lhsT_scale=lhs[1][:, cols],
-                rhs=rhs[0][:].bitcast(rhs_fmt),
-                rhs_scale=rhs[1][:],
+                rhs=rhs[0][:, slots].bitcast(rhs_fmt),
+                rhs_scale=rhs[1][:, slots],
                 start=True,
                 stop=True,
             )
@@ -94,11 +94,12 @@ def tile_attend_gkl_pl_mom_kernel(tc, xT, wT, y, wt, xm, mT, offs, out_0, out_1,
             nc.sync.dma_start(y_sb[h][:], y[0].rearrange("(p j) i -> p j i", j=PACK)[:, 2 * h : 2 * h + 2, :])
         nc.sync.dma_start(xm_raw[1][:], xm_rows[:, :, D // 2 :])
         m_src = [tile([P, T], F32, f"m_src{t}") for t in range(PACK)]
-        m_dst = {t: tile([P, T], F32, f"m_dst{t}") for t in range(2)}
+        m_dst = {t: tile([P, T], F32, f"m_dst{t}") for t in (1, 3)}
         w_dst = [tile([P, T], F32, f"w_dst{t}") for t in range(PACK)]
         for t in range(PACK):
             nc.sync.dma_start(m_src[t][:], plane(mT, t))
-        for t in range(2):
+        nc.sync.dma_start(w_dst[3][:, T // 2 :], plane(wT, 3)[:, T // 2 :])
+        for t in (1, 3):
             nc.sync.dma_start(m_dst[t][:], plane(mT, t))
 
         w_pair = [tile([P, 2, N], F32, f"w_pair{u}") for u in range(2)]
@@ -122,9 +123,8 @@ def tile_attend_gkl_pl_mom_kernel(tc, xT, wT, y, wt, xm, mT, offs, out_0, out_1,
             gather_weights(3, slots)
         for slots in halves:
             group_weights(1, slots)
-        early = 3 * T // 4
         for t in range(PACK):
-            width = early if t == PACK - 1 else T
+            width = T // 2 if t == PACK - 1 else T
             nc.scalar.activation(w_dst[t][:, :width], w_src[t][:, :width], ACT.Copy)
         w_mx = quantize("w", w_bf[:].rearrange("p c t -> p (c t)"), E4M3, 2)
 
@@ -136,7 +136,6 @@ def tile_attend_gkl_pl_mom_kernel(tc, xT, wT, y, wt, xm, mT, offs, out_0, out_1,
                 nc.scalar.activation(dealt, given, ACT.Copy)
             else:
                 nc.vector.tensor_copy(dealt, given)
-        nc.scalar.activation(w_dst[PACK - 1][:, early:], w_src[PACK - 1][:, early:], ACT.Copy)
         x_mx = quantize("x", x_bf[:].rearrange("p j m t -> p (j m t)"), E4M3, PACK)
 
         xm_bf = tile([P, PACK, P, PACK], BF16, "xm_bf")
@@ -150,7 +149,7 @@ def tile_attend_gkl_pl_mom_kernel(tc, xT, wT, y, wt, xm, mT, offs, out_0, out_1,
 
         cast_xm(0)
         target = [y_sb[j // 2][:, j % 2, :] for j in range(PACK)]
-        for j in range(2):
+        for j in range(PACK):
             nc.gpsimd.tensor_scalar(target[j], target[j], wt_sb[:, j : j + 1], 0.0, ALU.mult, ALU.add)
 
         neg_max = tile([P, PACK], F32, "neg_max")
@@ -169,9 +168,6 @@ def tile_attend_gkl_pl_mom_kernel(tc, xT, wT, y, wt, xm, mT, offs, out_0, out_1,
                 e[j][:], score[:], ACT.Exp, bias=neg_max[:, j : j + 1], scale=1.0, accum_out=sums[:, j : j + 1]
             )
 
-        for j in range(2, PACK):
-            nc.scalar.activation(target[j], target[j], ACT.Copy, scale=wt_sb[:, j : j + 1])
-
         def gradient_rows(j, cols=slice(0, N)):
             nc.vector.scalar_tensor_tensor(
                 g_rows[:, j, cols], e[j][:, cols], coef[j], target[j][:, cols], ALU.mult, ALU.subtract
@@ -182,34 +178,43 @@ def tile_attend_gkl_pl_mom_kernel(tc, xT, wT, y, wt, xm, mT, offs, out_0, out_1,
             engine.tensor_tensor(both[:], inv[:, j : j + 2], wt_sb[:, j : j + 2], ALU.mult)
             coef[j], coef[j + 1] = both[:, 0:1], both[:, 1:2]
 
-        form_coef(nc.gpsimd, 0)
-        gradient_rows(0)
-        nc.vector.reciprocal(inv[:, 2:], sums[:, 2:])
-        gradient_rows(1, halves[0])
-        form_coef(nc.vector, 2)
-        gradient_rows(1, halves[1])
-        for cols in halves:
-            for j in range(2, PACK):
-                gradient_rows(j, cols)
-
-        cast_xm(1)
         g_bf = tile([P, N, PACK], BF16, "g_bf")
-        for cols in halves:
+        g_grouped = g_bf[:].rearrange("p c j -> p (c j)")
+        xm_grouped = xm_bf[:].rearrange("p t m j -> p (t m j)")
+        g_mx, xm_mx = operand("g"), operand("xm")
+
+        def group_gradient(cols):
             nc.vector.tensor_copy(
                 g_bf[:, cols, :].rearrange("p (c i) j -> p c j i", i=4),
                 g_rows[:, :, cols].rearrange("p j (c i) -> p c j i", i=4),
             )
-        xm_mx = operand("xm")
-        xm_grouped = xm_bf[:].rearrange("p t m j -> p (t m j)")
-        quantize_part(xm_mx, xm_grouped, E4M3, slice(0, P))
-        g_mx = quantize("g", g_bf[:].rearrange("p c j -> p (c j)"), E5M2, 2)
-        quantize_part(xm_mx, xm_grouped, E4M3, slice(P, D))
 
-        dw = []
-        for t in range(PACK):
-            bank = psum.tile([P, N], F32, name=f"dw{t}")
-            product(bank, xm_mx, E4M3, slice(t * P, (t + 1) * P), g_mx, E5M2)
-            dw.append(bank)
+        form_coef(nc.gpsimd, 0)
+        gradient_rows(0, halves[0])
+        nc.vector.reciprocal(inv[:, 2:], sums[:, 2:])
+        gradient_rows(1, halves[0])
+        form_coef(nc.vector, 2)
+        gradient_rows(0, halves[1])
+        for j in (2, 3):
+            gradient_rows(j, halves[0])
+        gradient_rows(1, halves[1])
+        cast_xm(1)
+        group_gradient(halves[0])
+        quantize_part(xm_mx, xm_grouped, E4M3, slice(0, P))
+        quantize_part(g_mx, g_grouped, E5M2, halves[0])
+        for j in (2, 3):
+            gradient_rows(j, halves[1])
+        group_gradient(halves[1])
+        quantize_part(xm_mx, xm_grouped, E4M3, slice(P, D))
+        quantize_part(g_mx, g_grouped, E5M2, halves[1])
+
+        first = [psum.tile([P, N // 2], F32, name=f"dw0_{h}", tag=("score0", "dw0")[h]) for h in range(2)]
+        for h in range(2):
+            product(first[h], xm_mx, E4M3, slice(0, P), g_mx, E5M2, halves[h])
+        dw = {}
+        for t in range(1, PACK):
+            dw[t] = psum.tile([P, N], F32, name=f"dw{t}")
+            product(dw[t], xm_mx, E4M3, slice(t * P, (t + 1) * P), g_mx, E5M2)
 
         drift = {t: tile([P, N], F32, f"drift{t}") for t in range(2)}
         for t in range(2):
@@ -253,23 +258,26 @@ def tile_attend_gkl_pl_mom_kernel(tc, xT, wT, y, wt, xm, mT, offs, out_0, out_1,
         base = tile([P, N], F32, "base")
         nc.gpsimd.tensor_tensor(base[:], w_g[0], drift[0][:], ALU.add)
         w_new[0] = tile([P, N], F32, "w_new0", tag="m_src1")
-        nc.vector.scalar_tensor_tensor(w_new[0][:], dw[0][:], -LR, base[:], ALU.mult, ALU.add)
+        for h, slots in enumerate(halves):
+            nc.vector.scalar_tensor_tensor(w_new[0][:, slots], first[h][:], -LR, base[:, slots], ALU.mult, ALU.add)
         weights_by_scalar(0)
-        for t in (1, 2):
-            if t > 1:
-                gather_drift(t)
-            form_change(t)
-            form_weights(t)
-            weights_by_scalar(t)
-        gather_drift(3)
+        form_change(1)
+        form_weights(1)
+        weights_by_scalar(1)
+        for t in (2, 3):
+            gather_drift(t)
+        form_change(2, tag="m_src3")
+        form_weights(2)
+        weights_by_scalar(2)
         form_change(3)
+        change[0] = tile([P, N], F32, "change0", tag="drift3")
+        for h, slots in enumerate(halves):
+            nc.vector.scalar_tensor_tensor(change[0][:, slots], first[h][:], -LR, drift[0][:, slots], ALU.mult, ALU.add)
         weights_by_vector(3)
-        form_change(0, tag="w_pair1")
-        for t in range(2):
+        for t in (1, 3):
             scatter_momentum(t)
-        rounded = tile([P, PACK, T], BF16, "rounded", tag="drift0")
-        for t in (0, 1, 3):
-            nc.vector.tensor_copy(rounded[:, t, :], w_dst[t][:])
+        rounded = tile([P, 2, T, 2], BF16, "rounded", tag="w_pair1")
+        pair_words = rounded[:].rearrange("p u c e -> p (u c e)").bitcast(I32).rearrange("p (u c) -> p u c", u=2)
         out_codes = tile([P, T], U32, "out_codes", tag="w_src0")
         out_scales = tile([P, CHUNK], U8, "out_scales")
         words = out_2[0].rearrange("p c t -> p (c t)").bitcast(I32)
@@ -278,15 +286,16 @@ def tile_attend_gkl_pl_mom_kernel(tc, xT, wT, y, wt, xm, mT, offs, out_0, out_1,
             cols = slice(a, a + CHUNK)
             if k % 2 == 0:
                 wide = slice(a, a + 2 * CHUNK)
-                nc.vector.tensor_copy(rounded[:, 2, wide], w_dst[2][:, wide])
+                for t in (0, 1, 3, 2):
+                    nc.vector.tensor_copy(rounded[:, t // 2, wide, t % 2], w_dst[t][:, wide])
             grouped = tile([P, CHUNK, PACK], BF16, f"grouped{k}", tag=group_tags[k])
             nc.vector.tensor_copy(
-                grouped[:].rearrange("p (c i) t -> p c t i", i=4),
-                rounded[:, :, cols].rearrange("p t (c i) -> p c t i", i=4),
+                grouped[:].rearrange("p c t -> p (c t)").bitcast(I32).rearrange("p (c i u) -> p c u i", i=4, u=2),
+                pair_words[:, :, cols].rearrange("p u (c i) -> p c u i", i=4),
             )
             if k == 3:
-                last_new = tile([P, N // 2], F32, "last_new", tag="drift0")
-                nc.vector.tensor_scalar(last_new[:], change[3][:, halves[1]], -1.0 / LR, 0.0, ALU.mult, ALU.add)
+                last_new = tile([P, N // 2], F32, "last_new", tag="w_pair1")
+                nc.vector.tensor_scalar(last_new[:], change[2][:, halves[1]], -1.0 / LR, 0.0, ALU.mult, ALU.add)
             nc.vector.quantize_mx(
                 out=out_codes[:, cols].bitcast(E4M3),
                 scales=out_scales[4 * k :, :],
@@ -295,17 +304,17 @@ def tile_attend_gkl_pl_mom_kernel(tc, xT, wT, y, wt, xm, mT, offs, out_0, out_1,
             if k % 2 == 1:
                 nc.sync.dma_start(words[:, wide], out_codes[:, wide].bitcast(I32))
             if k == 0:
-                copy_momentum(2, group_tags[k])
+                copy_momentum(0, group_tags[k])
             if k == 1:
-                scatter_momentum(2)
-                copy_momentum(3, group_tags[k])
+                scatter_momentum(0)
+                copy_momentum(2, group_tags[k])
                 nc.scalar.activation(
-                    m_dst[3][:].indirect(listed(halves[0])), change[3][:, halves[0]], ACT.Copy, scale=-1.0 / LR
+                    m_dst[2][:].indirect(listed(halves[0])), change[2][:, halves[0]], ACT.Copy, scale=-1.0 / LR
                 )
         for q in range(4):
             nc.sync.dma_start(
                 out_3[0, 4 * q : 4 * q + 4, :].bitcast(I32).rearrange("r (k c) -> k r c", k=4),
                 out_scales[32 * q : 32 * q + 16, :].bitcast(I32),
             )
-        nc.vector.tensor_copy(m_dst[3][:].indirect(listed(halves[1])), last_new[:])
-        nc.sync.dma_start(plane(out_1, 3), m_dst[3][:])
+        nc.vector.tensor_copy(m_dst[2][:].indirect(listed(halves[1])), last_new[:])
+        nc.sync.dma_start(plane(out_1, 2), m_dst[2][:])

@@ -98,7 +98,6 @@ def tile_attend_gkl_pl_mom_kernel(tc, xT, wT, y, wt, xm, mT, offs, out_0, out_1,
         w_dst = [tile([P, T], F32, f"w_dst{t}") for t in range(PACK)]
         for t in range(PACK):
             nc.sync.dma_start(m_src[t][:], plane(mT, t))
-        nc.sync.dma_start(w_dst[3][:, T // 2 :], plane(wT, 3)[:, T // 2 :])
         for t in (1, 3):
             nc.sync.dma_start(m_dst[t][:], plane(mT, t))
 
@@ -123,8 +122,9 @@ def tile_attend_gkl_pl_mom_kernel(tc, xT, wT, y, wt, xm, mT, offs, out_0, out_1,
             gather_weights(3, slots)
         for slots in halves:
             group_weights(1, slots)
+        early = 3 * T // 4
         for t in range(PACK):
-            width = T // 2 if t == PACK - 1 else T
+            width = early if t == PACK - 1 else T
             nc.scalar.activation(w_dst[t][:, :width], w_src[t][:, :width], ACT.Copy)
         w_mx = quantize("w", w_bf[:].rearrange("p c t -> p (c t)"), E4M3, 2)
 
@@ -136,6 +136,7 @@ def tile_attend_gkl_pl_mom_kernel(tc, xT, wT, y, wt, xm, mT, offs, out_0, out_1,
                 nc.scalar.activation(dealt, given, ACT.Copy)
             else:
                 nc.vector.tensor_copy(dealt, given)
+        nc.scalar.activation(w_dst[PACK - 1][:, early:], w_src[PACK - 1][:, early:], ACT.Copy)
         x_mx = quantize("x", x_bf[:].rearrange("p j m t -> p (j m t)"), E4M3, PACK)
 
         xm_bf = tile([P, PACK, P, PACK], BF16, "xm_bf")

@@ -79,20 +79,15 @@ def tile_attend_gkl_pl_mom_kernel(tc, xT, wT, y, wt, xm, mT, offs, out_0, out_1,
         nc.vector.memset(warm_in[:], 0.0)
         nc.scalar.activation(warm_out[:], warm_in[:], ACT.Exp)
 
-        half = R // 2
-        x_rows = xT[0].rearrange("(p t) r -> p t r", t=PACK)
-        x_raw = [tile([P, PACK, half], F32, f"x_raw{h}") for h in range(2)]
-        for h in range(2):
-            nc.sync.dma_start(x_raw[h][:], x_rows[:, :, h * half : (h + 1) * half])
+        x_raw = tile([P, PACK, R], F32, "x_raw")
+        nc.sync.dma_start(x_raw[:], xT[0].rearrange("(p t) r -> p t r", t=PACK))
         wt_sb = tile([P, PACK], F32, "wt_sb")
         nc.sync.dma_start(wt_sb[:], wt[0].rearrange("(p j) one -> p (j one)", j=PACK))
-        xm_rows = xm[0].rearrange("(p j) d -> p j d", j=PACK)
-        xm_raw = [tile([P, PACK, D // 2], F32, f"xm_raw{h}") for h in range(2)]
-        nc.sync.dma_start(xm_raw[0][:], xm_rows[:, :, : D // 2])
         y_sb = [tile([P, 2, N], F32, f"y_sb{h}") for h in range(2)]
         for h in range(2):
             nc.sync.dma_start(y_sb[h][:], y[0].rearrange("(p j) i -> p j i", j=PACK)[:, 2 * h : 2 * h + 2, :])
-        nc.sync.dma_start(xm_raw[1][:], xm_rows[:, :, D // 2 :])
+        xm_raw = tile([P, PACK, D], F32, "xm_raw")
+        nc.sync.dma_start(xm_raw[:], xm[0].rearrange("(p j) d -> p j d", j=PACK))
         m_src = [tile([P, T], F32, f"m_src{t}") for t in range(PACK)]
         m_dst = {t: tile([P, T], F32, f"m_dst{t}") for t in (1, 3)}
         w_dst = [tile([P, T], F32, f"w_dst{t}") for t in range(PACK)]
@@ -122,21 +117,18 @@ def tile_attend_gkl_pl_mom_kernel(tc, xT, wT, y, wt, xm, mT, offs, out_0, out_1,
             gather_weights(3, slots)
         for slots in halves:
             group_weights(1, slots)
-        early = 3 * T // 4
         for t in range(PACK):
-            width = early if t == PACK - 1 else T
-            nc.scalar.activation(w_dst[t][:, :width], w_src[t][:, :width], ACT.Copy)
+            nc.scalar.activation(w_dst[t][:], w_src[t][:], ACT.Copy)
         w_mx = quantize("w", w_bf[:].rearrange("p c t -> p (c t)"), E4M3, 2)
 
         x_bf = tile([P, PACK, P, PACK], BF16, "x_bf")
         for h in range(2):
             dealt = x_bf[:, :, h * (P // 2) : (h + 1) * (P // 2), :].rearrange("p j m t -> p m t j")
-            given = x_raw[h][:].rearrange("p t (m j) -> p m t j", j=PACK)
+            given = x_raw[:, :, h * (R // 2) : (h + 1) * (R // 2)].rearrange("p t (m j) -> p m t j", j=PACK)
             if h == 0:
                 nc.scalar.activation(dealt, given, ACT.Copy)
             else:
                 nc.vector.tensor_copy(dealt, given)
-        nc.scalar.activation(w_dst[PACK - 1][:, early:], w_src[PACK - 1][:, early:], ACT.Copy)
         x_mx = quantize("x", x_bf[:].rearrange("p j m t -> p (j m t)"), E4M3, PACK)
 
         xm_bf = tile([P, PACK, P, PACK], BF16, "xm_bf")
@@ -144,13 +136,14 @@ def tile_attend_gkl_pl_mom_kernel(tc, xT, wT, y, wt, xm, mT, offs, out_0, out_1,
         def cast_xm(h):
             nc.scalar.activation(
                 xm_bf[:, :, h * (P // 2) : (h + 1) * (P // 2), :].rearrange("p t m j -> p m j t"),
-                xm_raw[h][:].rearrange("p j (m t) -> p m j t", t=PACK),
+                xm_raw[:, :, h * (D // 2) : (h + 1) * (D // 2)].rearrange("p j (m t) -> p m j t", t=PACK),
                 ACT.Copy,
             )
 
-        cast_xm(0)
         target = [y_sb[j // 2][:, j % 2, :] for j in range(PACK)]
-        for j in range(PACK):
+        for j in range(2):
+            nc.scalar.activation(target[j], target[j], ACT.Copy, scale=wt_sb[:, j : j + 1])
+        for j in range(2, PACK):
             nc.gpsimd.tensor_scalar(target[j], target[j], wt_sb[:, j : j + 1], 0.0, ALU.mult, ALU.add)
 
         neg_max = tile([P, PACK], F32, "neg_max")
@@ -199,7 +192,8 @@ def tile_attend_gkl_pl_mom_kernel(tc, xT, wT, y, wt, xm, mT, offs, out_0, out_1,
         for j in (2, 3):
             gradient_rows(j, halves[0])
         gradient_rows(1, halves[1])
-        cast_xm(1)
+        for h in range(2):
+            cast_xm(h)
         group_gradient(halves[0])
         quantize_part(xm_mx, xm_grouped, E4M3, slice(0, P))
         quantize_part(g_mx, g_grouped, E5M2, halves[0])
@@ -282,7 +276,7 @@ def tile_attend_gkl_pl_mom_kernel(tc, xT, wT, y, wt, xm, mT, offs, out_0, out_1,
         out_codes = tile([P, T], U32, "out_codes", tag="w_src0")
         out_scales = tile([P, CHUNK], U8, "out_scales")
         words = out_2[0].rearrange("p c t -> p (c t)").bitcast(I32)
-        group_tags = ("w_src1", "w_src2", "w_src3", "x_raw0")
+        group_tags = ("w_src1", "w_src2", "w_src3", "x_raw")
         for k, a in enumerate(range(0, T, CHUNK)):
             cols = slice(a, a + CHUNK)
             if k % 2 == 0:

@@ -269,8 +269,10 @@ def tile_attend_gkl_pl_mom_kernel(tc, xT, wT, y, wt, xm, mT, offs, out_0, out_1,
         for h, slots in enumerate(halves):
             nc.vector.scalar_tensor_tensor(change[0][:, slots], first[h][:], -LR, drift[0][:, slots], ALU.mult, ALU.add)
         weights_by_vector(3)
-        for t in (1, 3):
-            scatter_momentum(t)
+        scatter_momentum(1)
+        copy_momentum(0, "drift0")
+        scatter_momentum(0)
+        head, tail = slice(0, 3 * N // 4), slice(3 * N // 4, N)
         rounded = tile([P, 2, T, 2], BF16, "rounded", tag="w_pair1")
         pair_words = rounded[:].rearrange("p u c e -> p (u c e)").bitcast(I32).rearrange("p (u c) -> p u c", u=2)
         out_codes = tile([P, T], U32, "out_codes", tag="w_src0")
@@ -289,8 +291,8 @@ def tile_attend_gkl_pl_mom_kernel(tc, xT, wT, y, wt, xm, mT, offs, out_0, out_1,
                 pair_words[:, :, cols].rearrange("p u (c i) -> p c u i", i=4),
             )
             if k == 3:
-                last_new = tile([P, N // 2], F32, "last_new", tag="w_pair1")
-                nc.vector.tensor_scalar(last_new[:], change[2][:, halves[1]], -1.0 / LR, 0.0, ALU.mult, ALU.add)
+                last_half = tile([P, N // 4], F32, "last_half", tag="w_pair1")
+                nc.vector.tensor_scalar(last_half[:], change[2][:, tail], -0.5 / LR, 0.0, ALU.mult, ALU.add)
             nc.vector.quantize_mx(
                 out=out_codes[:, cols].bitcast(E4M3),
                 scales=out_scales[4 * k :, :],
@@ -299,17 +301,18 @@ def tile_attend_gkl_pl_mom_kernel(tc, xT, wT, y, wt, xm, mT, offs, out_0, out_1,
             if k % 2 == 1:
                 nc.sync.dma_start(words[:, wide], out_codes[:, wide].bitcast(I32))
             if k == 0:
-                copy_momentum(0, group_tags[k])
+                half_new = tile([P, N // 4], F32, "half_new", tag=group_tags[k])
+                nc.vector.tensor_scalar(half_new[:], change[3][:, tail], -0.5 / LR, 0.0, ALU.mult, ALU.add)
             if k == 1:
-                scatter_momentum(0)
+                nc.vector.tensor_tensor(m_dst[3][:].indirect(listed(tail)), half_new[:], half_new[:], ALU.add)
+                nc.scalar.activation(m_dst[3][:].indirect(listed(head)), change[3][:, head], ACT.Copy, scale=-1.0 / LR)
+                nc.sync.dma_start(plane(out_1, 3), m_dst[3][:])
                 copy_momentum(2, group_tags[k])
-                nc.scalar.activation(
-                    m_dst[2][:].indirect(listed(halves[0])), change[2][:, halves[0]], ACT.Copy, scale=-1.0 / LR
-                )
+                nc.scalar.activation(m_dst[2][:].indirect(listed(head)), change[2][:, head], ACT.Copy, scale=-1.0 / LR)
         for q in range(4):
             nc.sync.dma_start(
                 out_3[0, 4 * q : 4 * q + 4, :].bitcast(I32).rearrange("r (k c) -> k r c", k=4),
                 out_scales[32 * q : 32 * q + 16, :].bitcast(I32),
             )
-        nc.vector.tensor_copy(m_dst[2][:].indirect(listed(halves[1])), last_new[:])
+        nc.vector.tensor_tensor(m_dst[2][:].indirect(listed(tail)), last_half[:], last_half[:], ALU.add)
         nc.sync.dma_start(plane(out_1, 2), m_dst[2][:])

@@ -89,11 +89,11 @@ def tile_attend_gkl_pl_mom_kernel(tc, xT, wT, y, wt, xm, mT, offs, out_0, out_1,
         xm_raw = tile([P, PACK, D], F32, "xm_raw")
         nc.sync.dma_start(xm_raw[:], xm[0].rearrange("(p j) d -> p j d", j=PACK))
         m_src = [tile([P, T], F32, f"m_src{t}") for t in range(PACK)]
-        m_dst = {t: tile([P, T], F32, f"m_dst{t}") for t in (1, 3)}
+        m_dst = {t: tile([P, T], F32, f"m_dst{t}") for t in (1, 2)}
         w_dst = [tile([P, T], F32, f"w_dst{t}") for t in range(PACK)]
         for t in range(PACK):
             nc.sync.dma_start(m_src[t][:], plane(mT, t))
-        for t in (1, 3):
+        for t in (1, 2):
             nc.sync.dma_start(m_dst[t][:], plane(mT, t))
 
         w_pair = [tile([P, 2, N], F32, f"w_pair{u}") for u in range(2)]
@@ -250,27 +250,22 @@ def tile_attend_gkl_pl_mom_kernel(tc, xT, wT, y, wt, xm, mT, offs, out_0, out_1,
             m_dst[t] = tile([P, T], F32, f"m_dst{t}", tag=tag)
             nc.vector.tensor_copy(m_dst[t][:], m_src[t][:])
 
-        base = tile([P, N], F32, "base")
-        nc.gpsimd.tensor_tensor(base[:], w_g[0], drift[0][:], ALU.add)
-        w_new[0] = tile([P, N], F32, "w_new0", tag="m_src1")
-        for h, slots in enumerate(halves):
-            nc.vector.scalar_tensor_tensor(w_new[0][:, slots], first[h][:], -LR, base[:, slots], ALU.mult, ALU.add)
-        weights_by_scalar(0)
-        form_change(1)
-        form_weights(1)
-        weights_by_scalar(1)
-        for t in (2, 3):
-            gather_drift(t)
-        form_change(2, tag="m_src3")
-        form_weights(2)
-        weights_by_scalar(2)
-        form_change(3)
-        change[0] = tile([P, N], F32, "change0", tag="drift3")
+        change[0] = tile([P, N], F32, "change0", tag="m_src1")
+        w_new[0] = tile([P, N], F32, "w_new0")
         for h, slots in enumerate(halves):
             nc.vector.scalar_tensor_tensor(change[0][:, slots], first[h][:], -LR, drift[0][:, slots], ALU.mult, ALU.add)
+            nc.gpsimd.tensor_tensor(w_new[0][:, slots], w_g[0][:, slots], change[0][:, slots], ALU.add)
+        weights_by_scalar(0)
+        gather_drift(2)
+        for t in (1, 2):
+            form_change(t, tag="m_src2" if t == 1 else None)
+            form_weights(t)
+            weights_by_scalar(t)
+        gather_drift(3)
+        form_change(3)
         weights_by_vector(3)
         scatter_momentum(1)
-        copy_momentum(0, "drift0")
+        copy_momentum(0, "drift3")
         scatter_momentum(0)
         head, tail = slice(0, 3 * N // 4), slice(3 * N // 4, N)
         rounded = tile([P, 2, T, 2], BF16, "rounded", tag="w_pair1")
@@ -292,7 +287,7 @@ def tile_attend_gkl_pl_mom_kernel(tc, xT, wT, y, wt, xm, mT, offs, out_0, out_1,
             )
             if k == 3:
                 last_half = tile([P, N // 4], F32, "last_half", tag="w_pair1")
-                nc.vector.tensor_scalar(last_half[:], change[2][:, tail], -0.5 / LR, 0.0, ALU.mult, ALU.add)
+                nc.vector.tensor_scalar(last_half[:], change[3][:, tail], -0.5 / LR, 0.0, ALU.mult, ALU.add)
             nc.vector.quantize_mx(
                 out=out_codes[:, cols].bitcast(E4M3),
                 scales=out_scales[4 * k :, :],
@@ -302,17 +297,17 @@ def tile_attend_gkl_pl_mom_kernel(tc, xT, wT, y, wt, xm, mT, offs, out_0, out_1,
                 nc.sync.dma_start(words[:, wide], out_codes[:, wide].bitcast(I32))
             if k == 0:
                 half_new = tile([P, N // 4], F32, "half_new", tag=group_tags[k])
-                nc.vector.tensor_scalar(half_new[:], change[3][:, tail], -0.5 / LR, 0.0, ALU.mult, ALU.add)
+                nc.vector.tensor_scalar(half_new[:], change[2][:, tail], -0.5 / LR, 0.0, ALU.mult, ALU.add)
             if k == 1:
-                nc.vector.tensor_tensor(m_dst[3][:].indirect(listed(tail)), half_new[:], half_new[:], ALU.add)
-                nc.scalar.activation(m_dst[3][:].indirect(listed(head)), change[3][:, head], ACT.Copy, scale=-1.0 / LR)
-                nc.sync.dma_start(plane(out_1, 3), m_dst[3][:])
-                copy_momentum(2, group_tags[k])
+                nc.vector.tensor_tensor(m_dst[2][:].indirect(listed(tail)), half_new[:], half_new[:], ALU.add)
                 nc.scalar.activation(m_dst[2][:].indirect(listed(head)), change[2][:, head], ACT.Copy, scale=-1.0 / LR)
+                nc.sync.dma_start(plane(out_1, 2), m_dst[2][:])
+                copy_momentum(3, group_tags[k])
+                nc.scalar.activation(m_dst[3][:].indirect(listed(head)), change[3][:, head], ACT.Copy, scale=-1.0 / LR)
         for q in range(4):
             nc.sync.dma_start(
                 out_3[0, 4 * q : 4 * q + 4, :].bitcast(I32).rearrange("r (k c) -> k r c", k=4),
                 out_scales[32 * q : 32 * q + 16, :].bitcast(I32),
             )
-        nc.vector.tensor_tensor(m_dst[2][:].indirect(listed(tail)), last_half[:], last_half[:], ALU.add)
-        nc.sync.dma_start(plane(out_1, 2), m_dst[2][:])
+        nc.vector.tensor_tensor(m_dst[3][:].indirect(listed(tail)), last_half[:], last_half[:], ALU.add)
+        nc.sync.dma_start(plane(out_1, 3), m_dst[3][:])

@@ -217,7 +217,7 @@ def tile_attend_gkl_pl_mom_kernel(tc, xT, wT, y, wt, xm, mT, offs, out_0, out_1,
         change = {}
 
         def gather_drift(t):
-            drift[t] = tile([P, N], F32, f"drift{t}", tag=None)
+            drift[t] = tile([P, N], F32, f"drift{t}")
             nc.vector.tensor_scalar(drift[t][:], m_src[t][:].indirect(offsets[:]), -LR * BETA, 0.0, ALU.mult, ALU.add)
 
         def form_change(t, tag=None):
@@ -257,19 +257,20 @@ def tile_attend_gkl_pl_mom_kernel(tc, xT, wT, y, wt, xm, mT, offs, out_0, out_1,
             nc.gpsimd.tensor_tensor(w_new[0][:, slots], w_g[0][:, slots], change[0][:, slots], ALU.add)
         weights_by_scalar(0)
         gather_drift(2)
+        head, tail = slice(0, 3 * N // 4), slice(3 * N // 4, N)
+        form_change(1, tag="m_src2")
+        form_change(2)
         for t in (1, 2):
-            form_change(t, tag="m_src2" if t == 1 else None)
-            form_weights(t)
-            weights_by_scalar(t)
+            w_new[t] = tile([P, head.stop], F32, f"w_new{t}")
+            nc.gpsimd.tensor_tensor(w_new[t][:], w_g[t][:, head], change[t][:, head], ALU.add)
+            nc.vector.tensor_tensor(w_dst[t][:].indirect(listed(tail)), w_g[t][:, tail], change[t][:, tail], ALU.add)
+            nc.scalar.activation(w_dst[t][:].indirect(listed(head)), w_new[t][:], ACT.Copy)
+            nc.sync.dma_start(plane(out_0, t), w_dst[t][:])
         gather_drift(3)
         form_change(3)
         weights_by_vector(3)
-        scatter_momentum(1)
-        copy_momentum(0, "drift3")
-        scatter_momentum(0)
-        head, tail = slice(0, 3 * N // 4), slice(3 * N // 4, N)
-        rounded = tile([P, 2, T, 2], BF16, "rounded", tag="w_pair1")
-        pair_words = rounded[:].rearrange("p u c e -> p (u c e)").bitcast(I32).rearrange("p (u c) -> p u c", u=2)
+        for t in (1, 2):
+            scatter_momentum(t)
         out_codes = tile([P, T], U32, "out_codes", tag="w_src0")
         out_scales = tile([P, CHUNK], U8, "out_scales")
         words = out_2[0].rearrange("p c t -> p (c t)").bitcast(I32)
@@ -278,31 +279,35 @@ def tile_attend_gkl_pl_mom_kernel(tc, xT, wT, y, wt, xm, mT, offs, out_0, out_1,
             cols = slice(a, a + CHUNK)
             if k % 2 == 0:
                 wide = slice(a, a + 2 * CHUNK)
-                for t in (0, 1, 3, 2):
-                    nc.vector.tensor_copy(rounded[:, t // 2, wide, t % 2], w_dst[t][:, wide])
+                rounded_tag = ("w_pair1", "m_src0")[k // 2]
+                rounded = tile([P, 2, 2 * CHUNK, 2], BF16, f"rounded{k // 2}", tag=rounded_tag)
+                pair_words = rounded[:].rearrange("p u c e -> p (u c e)").bitcast(I32).rearrange("p (u c) -> p u c", u=2)
+                for t in (0, 1, 2, 3):
+                    nc.vector.tensor_copy(rounded[:, t // 2, :, t % 2], w_dst[t][:, wide])
             grouped = tile([P, CHUNK, PACK], BF16, f"grouped{k}", tag=group_tags[k])
             nc.vector.tensor_copy(
-                grouped[:].rearrange("p c t -> p (c t)").bitcast(I32).rearrange("p (c i u) -> p c u i", i=4, u=2),
-                pair_words[:, :, cols].rearrange("p u (c i) -> p c u i", i=4),
+                grouped[:].rearrange("p c t -> p (c t)").bitcast(I32).rearrange("p (c u) -> p c u", u=2),
+                pair_words[:, :, k % 2 * CHUNK : (k % 2 + 1) * CHUNK].rearrange("p u c -> p c u"),
             )
+            if k == 1:
+                copy_momentum(0, rounded_tag)
             if k == 3:
-                last_half = tile([P, N // 4], F32, "last_half", tag="w_pair1")
+                last_half = tile([P, N // 4], F32, "last_half", tag=rounded_tag)
                 nc.vector.tensor_scalar(last_half[:], change[3][:, tail], -0.5 / LR, 0.0, ALU.mult, ALU.add)
             nc.vector.quantize_mx(
                 out=out_codes[:, cols].bitcast(E4M3),
                 scales=out_scales[4 * k :, :],
                 in_=grouped[:].rearrange("p c t -> p (c t)"),
             )
-            if k % 2 == 1:
-                nc.sync.dma_start(words[:, wide], out_codes[:, wide].bitcast(I32))
-            if k == 0:
-                half_new = tile([P, N // 4], F32, "half_new", tag=group_tags[k])
-                nc.vector.tensor_scalar(half_new[:], change[2][:, tail], -0.5 / LR, 0.0, ALU.mult, ALU.add)
+            if k > 0:
+                done = wide if k == 1 else cols
+                nc.sync.dma_start(words[:, done], out_codes[:, done].bitcast(I32))
             if k == 1:
-                nc.vector.tensor_tensor(m_dst[2][:].indirect(listed(tail)), half_new[:], half_new[:], ALU.add)
-                nc.scalar.activation(m_dst[2][:].indirect(listed(head)), change[2][:, head], ACT.Copy, scale=-1.0 / LR)
-                nc.sync.dma_start(plane(out_1, 2), m_dst[2][:])
-                copy_momentum(3, group_tags[k])
+                scatter_momentum(0)
+                m_dst[3] = tile([P, T], F32, "m_dst3", tag=group_tags[0])
+                share = 5 * T // 8
+                nc.vector.tensor_copy(m_dst[3][:, :share], m_src[3][:, :share])
+                nc.scalar.activation(m_dst[3][:, share:], m_src[3][:, share:], ACT.Copy)
                 nc.scalar.activation(m_dst[3][:].indirect(listed(head)), change[3][:, head], ACT.Copy, scale=-1.0 / LR)
         for q in range(4):
             nc.sync.dma_start(

@@ -268,8 +268,11 @@ def tile_attend_gkl_pl_mom_kernel(tc, xT, wT, y, wt, xm, mT, offs, out_0, out_1,
             nc.sync.dma_start(plane(out_0, t), w_dst[t][:])
         gather_drift(3)
         form_change(3)
+        halved = tile([P, N // 4], F32, "halved", tag="drift2")
+        nc.vector.tensor_scalar(halved[:], change[2][:, tail], -0.5 / LR, 0.0, ALU.mult, ALU.add)
         weights_by_vector(3)
-        for t in (1, 2):
+        copy_momentum(0, "drift3")
+        for t in (1, 0):
             scatter_momentum(t)
         out_codes = tile([P, T], U32, "out_codes", tag="w_src0")
         out_scales = tile([P, CHUNK], U8, "out_scales")
@@ -279,21 +282,24 @@ def tile_attend_gkl_pl_mom_kernel(tc, xT, wT, y, wt, xm, mT, offs, out_0, out_1,
             cols = slice(a, a + CHUNK)
             if k % 2 == 0:
                 wide = slice(a, a + 2 * CHUNK)
-                rounded_tag = ("w_pair1", "m_src0")[k // 2]
+                rounded_tag = ("w_pair1", "m_src3")[k // 2]
                 rounded = tile([P, 2, 2 * CHUNK, 2], BF16, f"rounded{k // 2}", tag=rounded_tag)
                 pair_words = rounded[:].rearrange("p u c e -> p (u c e)").bitcast(I32).rearrange("p (u c) -> p u c", u=2)
                 for t in (0, 1, 2, 3):
                     nc.vector.tensor_copy(rounded[:, t // 2, :, t % 2], w_dst[t][:, wide])
+                    if k == 0 and t == 0:
+                        nc.vector.tensor_tensor(m_dst[2][:].indirect(listed(tail)), halved[:], halved[:], ALU.add)
+                        nc.scalar.activation(
+                            m_dst[2][:].indirect(listed(head)), change[2][:, head], ACT.Copy, scale=-1.0 / LR
+                        )
+                        nc.sync.dma_start(plane(out_1, 2), m_dst[2][:])
             grouped = tile([P, CHUNK, PACK], BF16, f"grouped{k}", tag=group_tags[k])
             nc.vector.tensor_copy(
                 grouped[:].rearrange("p c t -> p (c t)").bitcast(I32).rearrange("p (c u) -> p c u", u=2),
                 pair_words[:, :, k % 2 * CHUNK : (k % 2 + 1) * CHUNK].rearrange("p u c -> p c u"),
             )
             if k == 1:
-                copy_momentum(0, rounded_tag)
-            if k == 3:
-                last_half = tile([P, N // 4], F32, "last_half", tag=rounded_tag)
-                nc.vector.tensor_scalar(last_half[:], change[3][:, tail], -0.5 / LR, 0.0, ALU.mult, ALU.add)
+                copy_momentum(3, rounded_tag)
             nc.vector.quantize_mx(
                 out=out_codes[:, cols].bitcast(E4M3),
                 scales=out_scales[4 * k :, :],
@@ -303,16 +309,9 @@ def tile_attend_gkl_pl_mom_kernel(tc, xT, wT, y, wt, xm, mT, offs, out_0, out_1,
                 done = wide if k == 1 else cols
                 nc.sync.dma_start(words[:, done], out_codes[:, done].bitcast(I32))
             if k == 1:
-                scatter_momentum(0)
-                m_dst[3] = tile([P, T], F32, "m_dst3", tag=group_tags[0])
-                share = 5 * T // 8
-                nc.vector.tensor_copy(m_dst[3][:, :share], m_src[3][:, :share])
-                nc.scalar.activation(m_dst[3][:, share:], m_src[3][:, share:], ACT.Copy)
-                nc.scalar.activation(m_dst[3][:].indirect(listed(head)), change[3][:, head], ACT.Copy, scale=-1.0 / LR)
+                scatter_momentum(3)
         for q in range(4):
             nc.sync.dma_start(
                 out_3[0, 4 * q : 4 * q + 4, :].bitcast(I32).rearrange("r (k c) -> k r c", k=4),
                 out_scales[32 * q : 32 * q + 16, :].bitcast(I32),
             )
-        nc.vector.tensor_tensor(m_dst[3][:].indirect(listed(tail)), last_half[:], last_half[:], ALU.add)
-        nc.sync.dma_start(plane(out_1, 3), m_dst[3][:])

@@ -133,13 +133,6 @@ def tile_attend_gkl_pl_mom_kernel(tc, xT, wT, y, wt, xm, mT, offs, out_0, out_1,
 
         xm_bf = tile([P, PACK, P, PACK], BF16, "xm_bf")
 
-        def cast_xm(h):
-            nc.scalar.activation(
-                xm_bf[:, :, h * (P // 2) : (h + 1) * (P // 2), :].rearrange("p t m j -> p m j t"),
-                xm_raw[:, :, h * (D // 2) : (h + 1) * (D // 2)].rearrange("p j (m t) -> p m j t", t=PACK),
-                ACT.Copy,
-            )
-
         target = [y_sb[j // 2][:, j % 2, :] for j in range(PACK)]
         for j in range(2):
             nc.scalar.activation(target[j], target[j], ACT.Copy, scale=wt_sb[:, j : j + 1])
@@ -184,24 +177,28 @@ def tile_attend_gkl_pl_mom_kernel(tc, xT, wT, y, wt, xm, mT, offs, out_0, out_1,
             )
 
         form_coef(nc.gpsimd, 0)
-        gradient_rows(0, halves[0])
+        gradient_rows(0)
         nc.vector.reciprocal(inv[:, 2:], sums[:, 2:])
         gradient_rows(1, halves[0])
         form_coef(nc.vector, 2)
-        gradient_rows(0, halves[1])
-        for j in (2, 3):
-            gradient_rows(j, halves[0])
         gradient_rows(1, halves[1])
-        for h in range(2):
-            cast_xm(h)
-        group_gradient(halves[0])
+        for cols in halves:
+            for j in (2, 3):
+                gradient_rows(j, cols)
+        split = 3 * P // 4
+        for part in (slice(0, split), slice(split, P)):
+            dealt = xm_bf[:, :, part, :].rearrange("p t m j -> p m j t")
+            given = xm_raw[:, :, PACK * part.start : PACK * part.stop].rearrange("p j (m t) -> p m j t", t=PACK)
+            if part.start == 0:
+                nc.scalar.activation(dealt, given, ACT.Copy)
+            else:
+                nc.vector.tensor_copy(dealt, given)
+        for cols in halves:
+            group_gradient(cols)
         quantize_part(xm_mx, xm_grouped, E4M3, slice(0, P))
-        quantize_part(g_mx, g_grouped, E5M2, halves[0])
-        for j in (2, 3):
-            gradient_rows(j, halves[1])
-        group_gradient(halves[1])
+        for cols in halves:
+            quantize_part(g_mx, g_grouped, E5M2, cols)
         quantize_part(xm_mx, xm_grouped, E4M3, slice(P, D))
-        quantize_part(g_mx, g_grouped, E5M2, halves[1])
 
         first = [psum.tile([P, N // 2], F32, name=f"dw0_{h}", tag=("score0", "dw0")[h]) for h in range(2)]
         for h in range(2):
@@ -261,7 +258,7 @@ def tile_attend_gkl_pl_mom_kernel(tc, xT, wT, y, wt, xm, mT, offs, out_0, out_1,
         form_change(1, tag="m_src2")
         form_change(2)
         for t in (1, 2):
-            w_new[t] = tile([P, head.stop], F32, f"w_new{t}")
+            w_new[t] = tile([P, head.stop], F32, f"w_new{t}", tag="w_pair0" if t == 2 else None)
             nc.gpsimd.tensor_tensor(w_new[t][:], w_g[t][:, head], change[t][:, head], ALU.add)
             nc.vector.tensor_tensor(w_dst[t][:].indirect(listed(tail)), w_g[t][:, tail], change[t][:, tail], ALU.add)
             nc.scalar.activation(w_dst[t][:].indirect(listed(head)), w_new[t][:], ACT.Copy)
@@ -280,10 +277,10 @@ def tile_attend_gkl_pl_mom_kernel(tc, xT, wT, y, wt, xm, mT, offs, out_0, out_1,
         group_tags = ("w_src1", "w_src2", "w_src3", "x_raw")
         for k, a in enumerate(range(0, T, CHUNK)):
             cols = slice(a, a + CHUNK)
-            if k % 2 == 0:
-                wide = slice(a, a + 2 * CHUNK)
-                rounded_tag = ("w_pair1", "m_src3")[k // 2]
-                rounded = tile([P, 2, 2 * CHUNK, 2], BF16, f"rounded{k // 2}", tag=rounded_tag)
+            if k != 1:
+                wide = slice(a, a + (2 * CHUNK if k == 0 else CHUNK))
+                rounded_tag = {0: "w_pair1", 2: "m_src3", 3: group_tags[1]}[k]
+                rounded = tile([P, 2, wide.stop - wide.start, 2], BF16, f"rounded{k}", tag=rounded_tag)
                 pair_words = rounded[:].rearrange("p u c e -> p (u c e)").bitcast(I32).rearrange("p (u c) -> p u c", u=2)
                 for t in (0, 1, 2, 3):
                     nc.vector.tensor_copy(rounded[:, t // 2, :, t % 2], w_dst[t][:, wide])
@@ -296,7 +293,7 @@ def tile_attend_gkl_pl_mom_kernel(tc, xT, wT, y, wt, xm, mT, offs, out_0, out_1,
             grouped = tile([P, CHUNK, PACK], BF16, f"grouped{k}", tag=group_tags[k])
             nc.vector.tensor_copy(
                 grouped[:].rearrange("p c t -> p (c t)").bitcast(I32).rearrange("p (c u) -> p c u", u=2),
-                pair_words[:, :, k % 2 * CHUNK : (k % 2 + 1) * CHUNK].rearrange("p u c -> p c u"),
+                pair_words[:, :, a - wide.start : a - wide.start + CHUNK].rearrange("p u c -> p c u"),
             )
             if k == 1:
                 copy_momentum(3, rounded_tag)
@@ -308,7 +305,7 @@ def tile_attend_gkl_pl_mom_kernel(tc, xT, wT, y, wt, xm, mT, offs, out_0, out_1,
             if k > 0:
                 done = wide if k == 1 else cols
                 nc.sync.dma_start(words[:, done], out_codes[:, done].bitcast(I32))
-            if k == 1:
+            if k == 2:
                 scatter_momentum(3)
         for q in range(4):
             nc.sync.dma_start(

@@ -93,8 +93,9 @@ def tile_attend_gkl_pl_mom_kernel(tc, xT, wT, y, wt, xm, mT, offs, out_0, out_1,
         w_dst = [tile([P, T], F32, f"w_dst{t}") for t in range(PACK)]
         for t in range(PACK):
             nc.sync.dma_start(m_src[t][:], plane(mT, t))
-        for t in (1, 2):
-            nc.sync.dma_start(m_dst[t][:], plane(mT, t))
+        loaded = 3 * T // 4
+        nc.sync.dma_start(m_dst[1][:, :loaded], plane(mT, 1)[:, :loaded])
+        nc.sync.dma_start(m_dst[2][:], plane(mT, 2))
 
         w_pair = [tile([P, 2, N], F32, f"w_pair{u}") for u in range(2)]
         w_g = [w_pair[t // 2][:, t % 2, :] for t in range(PACK)]
@@ -211,6 +212,7 @@ def tile_attend_gkl_pl_mom_kernel(tc, xT, wT, y, wt, xm, mT, offs, out_0, out_1,
         drift = {t: tile([P, N], F32, f"drift{t}") for t in range(2)}
         for t in range(2):
             nc.scalar.activation(drift[t][:], m_src[t][:].indirect(offsets[:]), ACT.Copy, scale=-LR * BETA)
+        nc.scalar.activation(m_dst[1][:, loaded:], m_src[1][:, loaded:], ACT.Copy)
         change = {}
 
         def gather_drift(t):
@@ -247,8 +249,8 @@ def tile_attend_gkl_pl_mom_kernel(tc, xT, wT, y, wt, xm, mT, offs, out_0, out_1,
             m_dst[t] = tile([P, T], F32, f"m_dst{t}", tag=tag)
             nc.vector.tensor_copy(m_dst[t][:], m_src[t][:])
 
-        change[0] = tile([P, N], F32, "change0", tag="m_src1")
-        w_new[0] = tile([P, N], F32, "w_new0")
+        change[0] = tile([P, N], F32, "change0")
+        w_new[0] = tile([P, N], F32, "w_new0", tag="m_src1")
         for h, slots in enumerate(halves):
             nc.vector.scalar_tensor_tensor(change[0][:, slots], first[h][:], -LR, drift[0][:, slots], ALU.mult, ALU.add)
             nc.gpsimd.tensor_tensor(w_new[0][:, slots], w_g[0][:, slots], change[0][:, slots], ALU.add)
@@ -282,8 +284,14 @@ def tile_attend_gkl_pl_mom_kernel(tc, xT, wT, y, wt, xm, mT, offs, out_0, out_1,
                 rounded_tag = {0: "w_pair1", 2: "m_src3", 3: group_tags[1]}[k]
                 rounded = tile([P, 2, wide.stop - wide.start, 2], BF16, f"rounded{k}", tag=rounded_tag)
                 pair_words = rounded[:].rearrange("p u c e -> p (u c e)").bitcast(I32).rearrange("p (u c) -> p u c", u=2)
-                for t in (0, 1, 2, 3):
-                    nc.vector.tensor_copy(rounded[:, t // 2, :, t % 2], w_dst[t][:, wide])
+                parts = halves if k == 3 else (slice(0, CHUNK),)
+                for t in range(PACK):
+                    if k == 3 and t == PACK - 1:
+                        for part in parts:
+                            source = w_dst[t][:, a + part.start : a + part.stop]
+                            nc.vector.tensor_copy(rounded[:, t // 2, part, t % 2], source)
+                    else:
+                        nc.vector.tensor_copy(rounded[:, t // 2, :, t % 2], w_dst[t][:, wide])
                     if k == 0 and t == 0:
                         nc.vector.tensor_tensor(m_dst[2][:].indirect(listed(tail)), halved[:], halved[:], ALU.add)
                         nc.scalar.activation(
@@ -291,17 +299,21 @@ def tile_attend_gkl_pl_mom_kernel(tc, xT, wT, y, wt, xm, mT, offs, out_0, out_1,
                         )
                         nc.sync.dma_start(plane(out_1, 2), m_dst[2][:])
             grouped = tile([P, CHUNK, PACK], BF16, f"grouped{k}", tag=group_tags[k])
-            nc.vector.tensor_copy(
-                grouped[:].rearrange("p c t -> p (c t)").bitcast(I32).rearrange("p (c u) -> p c u", u=2),
-                pair_words[:, :, a - wide.start : a - wide.start + CHUNK].rearrange("p u c -> p c u"),
-            )
+            group_words = grouped[:].rearrange("p c t -> p (c t)").bitcast(I32).rearrange("p (c u) -> p c u", u=2)
+            first_col = a - wide.start
+            for part in parts:
+                nc.vector.tensor_copy(
+                    group_words[:, part, :],
+                    pair_words[:, :, first_col + part.start : first_col + part.stop].rearrange("p u c -> p c u"),
+                )
             if k == 1:
                 copy_momentum(3, rounded_tag)
-            nc.vector.quantize_mx(
-                out=out_codes[:, cols].bitcast(E4M3),
-                scales=out_scales[4 * k :, :],
-                in_=grouped[:].rearrange("p c t -> p (c t)"),
-            )
+            for part in parts:
+                nc.vector.quantize_mx(
+                    out=out_codes[:, a + part.start : a + part.stop].bitcast(E4M3),
+                    scales=out_scales[4 * k :, part],
+                    in_=grouped[:, part, :].rearrange("p c t -> p (c t)"),
+                )
             if k > 0:
                 done = wide if k == 1 else cols
                 nc.sync.dma_start(words[:, done], out_codes[:, done].bitcast(I32))

@@ -74,11 +74,6 @@ def tile_attend_gkl_pl_mom_kernel(tc, xT, wT, y, wt, xm, mT, offs, out_0, out_1,
         for t in range(1, PACK):
             nc.sync.dma_start(w_src[t][:], plane(wT, t))
 
-        warm_in = tile([P, 1], F32, "warm_in")
-        warm_out = tile([P, 1], F32, "warm_out")
-        nc.vector.memset(warm_in[:], 0.0)
-        nc.scalar.activation(warm_out[:], warm_in[:], ACT.Exp)
-
         x_raw = tile([P, PACK, R], F32, "x_raw")
         nc.sync.dma_start(x_raw[:], xT[0].rearrange("(p t) r -> p t r", t=PACK))
         wt_sb = tile([P, PACK], F32, "wt_sb")

@@ -224,10 +224,6 @@ def tile_attend_gkl_pl_mom_kernel(tc, xT, wT, y, wt, xm, mT, offs, out_0, out_1,
 
         w_new = {}
 
-        def form_weights(t):
-            w_new[t] = tile([P, N], F32, f"w_new{t}", tag=None)
-            nc.gpsimd.tensor_tensor(w_new[t][:], w_g[t], change[t][:], ALU.add)
-
         def weights_by_scalar(t):
             scalar_scatter(w_dst[t], w_new[t], 1.0)
             nc.sync.dma_start(plane(out_0, t), w_dst[t][:])
@@ -292,7 +288,6 @@ def tile_attend_gkl_pl_mom_kernel(tc, xT, wT, y, wt, xm, mT, offs, out_0, out_1,
                         nc.scalar.activation(
                             m_dst[2][:].indirect(listed(head)), change[2][:, head], ACT.Copy, scale=-1.0 / LR
                         )
-                        nc.sync.dma_start(plane(out_1, 2), m_dst[2][:])
             grouped = tile([P, CHUNK, PACK], BF16, f"grouped{k}", tag=group_tags[k])
             group_words = grouped[:].rearrange("p c t -> p (c t)").bitcast(I32).rearrange("p (c u) -> p c u", u=2)
             first_col = a - wide.start
@@ -312,6 +307,8 @@ def tile_attend_gkl_pl_mom_kernel(tc, xT, wT, y, wt, xm, mT, offs, out_0, out_1,
             if k > 0:
                 done = wide if k == 1 else cols
                 nc.sync.dma_start(words[:, done], out_codes[:, done].bitcast(I32))
+            if k == 1:
+                nc.sync.dma_start(plane(out_1, 2), m_dst[2][:])
             if k == 2:
                 scatter_momentum(3)
         for q in range(4):

@@ -209,6 +209,8 @@ def tile_attend_gkl_pl_mom_kernel(tc, xT, wT, y, wt, xm, mT, offs, out_0, out_1,
             nc.scalar.activation(drift[t][:], m_src[t][:].indirect(offsets[:]), ACT.Copy, scale=-LR * BETA)
         nc.scalar.activation(m_dst[1][:, loaded:], m_src[1][:, loaded:], ACT.Copy)
         change = {}
+        undo_rate = tile([P, 1], F32, "undo_rate")
+        nc.gpsimd.memset(undo_rate[:], -1.0 / LR)
 
         def gather_drift(t):
             drift[t] = tile([P, N], F32, f"drift{t}")
@@ -233,7 +235,7 @@ def tile_attend_gkl_pl_mom_kernel(tc, xT, wT, y, wt, xm, mT, offs, out_0, out_1,
             nc.sync.dma_start(plane(out_0, t), w_dst[t][:])
 
         def scatter_momentum(t):
-            scalar_scatter(m_dst[t], change[t], -1.0 / LR)
+            nc.scalar.activation(m_dst[t][:].indirect(offsets[:]), change[t][:], ACT.Copy, scale=undo_rate[:])
             nc.sync.dma_start(plane(out_1, t), m_dst[t][:])
 
         def copy_momentum(t, tag):
@@ -251,6 +253,8 @@ def tile_attend_gkl_pl_mom_kernel(tc, xT, wT, y, wt, xm, mT, offs, out_0, out_1,
         form_change(1, tag="m_src2")
         form_change(2)
         for t in (1, 2):
+            if t == 2:
+                head, tail = slice(0, 5 * N // 8), slice(5 * N // 8, N)
             w_new[t] = tile([P, head.stop], F32, f"w_new{t}", tag="w_pair0" if t == 2 else None)
             nc.gpsimd.tensor_tensor(w_new[t][:], w_g[t][:, head], change[t][:, head], ALU.add)
             nc.vector.tensor_tensor(w_dst[t][:].indirect(listed(tail)), w_g[t][:, tail], change[t][:, tail], ALU.add)
@@ -258,8 +262,6 @@ def tile_attend_gkl_pl_mom_kernel(tc, xT, wT, y, wt, xm, mT, offs, out_0, out_1,
             nc.sync.dma_start(plane(out_0, t), w_dst[t][:])
         gather_drift(3)
         form_change(3)
-        halved = tile([P, N // 4], F32, "halved", tag="drift2")
-        nc.vector.tensor_scalar(halved[:], change[2][:, tail], -0.5 / LR, 0.0, ALU.mult, ALU.add)
         weights_by_vector(3)
         copy_momentum(0, "drift3")
         for t in (1, 0):
@@ -284,9 +286,8 @@ def tile_attend_gkl_pl_mom_kernel(tc, xT, wT, y, wt, xm, mT, offs, out_0, out_1,
                     else:
                         nc.vector.tensor_copy(rounded[:, t // 2, :, t % 2], w_dst[t][:, wide])
                     if k == 0 and t == 0:
-                        nc.vector.tensor_tensor(m_dst[2][:].indirect(listed(tail)), halved[:], halved[:], ALU.add)
                         nc.scalar.activation(
-                            m_dst[2][:].indirect(listed(head)), change[2][:, head], ACT.Copy, scale=-1.0 / LR
+                            m_dst[2][:].indirect(offsets[:]), change[2][:], ACT.Copy, scale=undo_rate[:]
                         )
             grouped = tile([P, CHUNK, PACK], BF16, f"grouped{k}", tag=group_tags[k])
             group_words = grouped[:].rearrange("p c t -> p (c t)").bitcast(I32).rearrange("p (c u) -> p c u", u=2)

@@ -62,6 +62,10 @@ def tile_attend_gkl_pl_mom_kernel(tc, xT, wT, y, wt, xm, mT, offs, out_0, out_1,
                 stop=True,
             )
 
+        one = tile([P, 1], F32, "one")
+        nc.gpsimd.memset(one[:], 1.0)
+        decay = tile([P, 1], F32, "decay")
+        nc.gpsimd.tensor_scalar(decay[:], one[:], -LR * BETA, 0.0, ALU.mult, ALU.add)
         halves = (slice(0, N // 2), slice(N // 2, N))
         offsets = tile([P, N // 16], U16, "offsets")
 
@@ -118,79 +122,79 @@ def tile_attend_gkl_pl_mom_kernel(tc, xT, wT, y, wt, xm, mT, offs, out_0, out_1,
         w_mx = quantize("w", w_bf[:].rearrange("p c t -> p (c t)"), E4M3, 2)
 
         x_bf = tile([P, PACK, P, PACK], BF16, "x_bf")
-        for h in range(2):
-            dealt = x_bf[:, :, h * (P // 2) : (h + 1) * (P // 2), :].rearrange("p j m t -> p m t j")
-            given = x_raw[:, :, h * (R // 2) : (h + 1) * (R // 2)].rearrange("p t (m j) -> p m t j", j=PACK)
-            if h == 0:
-                nc.scalar.activation(dealt, given, ACT.Copy)
-            else:
-                nc.vector.tensor_copy(dealt, given)
+        for u in range(2):
+            for h in range(2):
+                rows = slice(h * (P // 2), (h + 1) * (P // 2))
+                dealt = x_bf[:, 2 * u : 2 * u + 2, rows, :].rearrange("p j m t -> p m t j")
+                given = x_raw[:].rearrange("p t (m j) -> p m t j", j=PACK)[:, rows, :, 2 * u : 2 * u + 2]
+                if h == 0:
+                    nc.scalar.activation(dealt, given, ACT.Copy)
+                else:
+                    nc.vector.tensor_copy(dealt, given)
         x_mx = quantize("x", x_bf[:].rearrange("p j m t -> p (j m t)"), E4M3, PACK)
 
         xm_bf = tile([P, PACK, P, PACK], BF16, "xm_bf")
 
-        target = [y_sb[j // 2][:, j % 2, :] for j in range(PACK)]
+        target = tile([P, PACK, N], F32, "target")
         for j in range(2):
-            nc.scalar.activation(target[j], target[j], ACT.Copy, scale=wt_sb[:, j : j + 1])
+            nc.scalar.activation(target[:, j, :], y_sb[0][:, j, :], ACT.Copy, scale=wt_sb[:, j : j + 1])
         for j in range(2, PACK):
-            nc.gpsimd.tensor_scalar(target[j], target[j], wt_sb[:, j : j + 1], 0.0, ALU.mult, ALU.add)
+            nc.gpsimd.tensor_scalar(target[:, j, :], y_sb[1][:, j - 2, :], wt_sb[:, j : j + 1], 0.0, ALU.mult, ALU.add)
 
         neg_max = tile([P, PACK], F32, "neg_max")
         inv = tile([P, PACK], F32, "inv")
-        coef = {}
         e = [tile([P, N], F32, f"e{j}") for j in range(PACK)]
+        weighted = tile([P, PACK, N], F32, "weighted")
         sums = tile([P, PACK], F32, "sums")
-        g_rows = tile([P, PACK, N], BF16, "g_rows")
         for j in range(PACK):
             score = psum.tile([P, N], F32, name=f"score{j}")
             product(score, x_mx, E4M3, slice(j * P, (j + 1) * P), w_mx, E4M3)
             if j == PACK - 1:
-                nc.vector.reciprocal(inv[:, :2], sums[:, :2])
+                nc.vector.reciprocal(inv[:, :1], sums[:, :1])
             nc.vector.tensor_reduce(neg_max[:, j : j + 1], score[:], AXIS.X, ALU.max, negate=True)
             nc.scalar.activation(
                 e[j][:], score[:], ACT.Exp, bias=neg_max[:, j : j + 1], scale=1.0, accum_out=sums[:, j : j + 1]
             )
 
-        def gradient_rows(j, cols=slice(0, N)):
-            nc.vector.scalar_tensor_tensor(
-                g_rows[:, j, cols], e[j][:, cols], coef[j], target[j][:, cols], ALU.mult, ALU.subtract
+        def normalise(engine, j, cols=slice(0, N)):
+            engine.tensor_scalar(
+                weighted[:, j, cols], e[j][:, cols], inv[:, j : j + 1], wt_sb[:, j : j + 1], ALU.mult, ALU.mult
             )
-
-        def form_coef(engine, j):
-            both = tile([P, 2], F32, f"coef{j}")
-            engine.tensor_tensor(both[:], inv[:, j : j + 2], wt_sb[:, j : j + 2], ALU.mult)
-            coef[j], coef[j + 1] = both[:, 0:1], both[:, 1:2]
 
         g_bf = tile([P, N, PACK], BF16, "g_bf")
         g_grouped = g_bf[:].rearrange("p c j -> p (c j)")
         xm_grouped = xm_bf[:].rearrange("p t m j -> p (t m j)")
         g_mx, xm_mx = operand("g"), operand("xm")
 
-        def group_gradient(cols):
-            nc.vector.tensor_copy(
+        def form_gradient(cols):
+            nc.vector.tensor_tensor(
                 g_bf[:, cols, :].rearrange("p (c i) j -> p c j i", i=4),
-                g_rows[:, :, cols].rearrange("p j (c i) -> p c j i", i=4),
+                weighted[:, :, cols].rearrange("p j (c i) -> p c j i", i=4),
+                target[:, :, cols].rearrange("p j (c i) -> p c j i", i=4),
+                ALU.subtract,
             )
 
-        form_coef(nc.gpsimd, 0)
-        gradient_rows(0)
-        nc.vector.reciprocal(inv[:, 2:], sums[:, 2:])
-        gradient_rows(1, halves[0])
-        form_coef(nc.vector, 2)
-        gradient_rows(1, halves[1])
-        for cols in halves:
-            for j in (2, 3):
-                gradient_rows(j, cols)
-        split = 3 * P // 4
-        for part in (slice(0, split), slice(split, P)):
+        def cast_xm(part):
             dealt = xm_bf[:, :, part, :].rearrange("p t m j -> p m j t")
             given = xm_raw[:, :, PACK * part.start : PACK * part.stop].rearrange("p j (m t) -> p m j t", t=PACK)
             if part.start == 0:
                 nc.scalar.activation(dealt, given, ACT.Copy)
             else:
                 nc.vector.tensor_copy(dealt, given)
+
+        split = 3 * P // 4
+        normalise(nc.gpsimd, 0)
+        nc.vector.reciprocal(inv[:, 1:2], sums[:, 1:2])
+        cast_xm(slice(0, split))
+        cast_xm(slice(split, P))
+        nc.vector.reciprocal(inv[:, 2:3], sums[:, 2:3])
+        normalise(nc.vector, 1)
+        nc.vector.reciprocal(inv[:, 3:], sums[:, 3:])
+        normalise(nc.vector, 2)
         for cols in halves:
-            group_gradient(cols)
+            normalise(nc.vector, 3, cols)
+        for cols in halves:
+            form_gradient(cols)
         quantize_part(xm_mx, xm_grouped, E4M3, slice(0, P))
         for cols in halves:
             quantize_part(g_mx, g_grouped, E5M2, cols)
@@ -206,7 +210,7 @@ def tile_attend_gkl_pl_mom_kernel(tc, xT, wT, y, wt, xm, mT, offs, out_0, out_1,
 
         drift = {t: tile([P, N], F32, f"drift{t}") for t in range(2)}
         for t in range(2):
-            nc.scalar.activation(drift[t][:], m_src[t][:].indirect(offsets[:]), ACT.Copy, scale=-LR * BETA)
+            nc.scalar.activation(drift[t][:], m_src[t][:].indirect(offsets[:]), ACT.Copy, scale=decay[:])
         nc.scalar.activation(m_dst[1][:, loaded:], m_src[1][:, loaded:], ACT.Copy)
         change = {}
         undo_rate = tile([P, 1], F32, "undo_rate")
@@ -243,7 +247,7 @@ def tile_attend_gkl_pl_mom_kernel(tc, xT, wT, y, wt, xm, mT, offs, out_0, out_1,
             nc.vector.tensor_copy(m_dst[t][:], m_src[t][:])
 
         change[0] = tile([P, N], F32, "change0")
-        w_new[0] = tile([P, N], F32, "w_new0", tag="m_src1")
+        w_new[0] = tile([P, N], F32, "w_new0", tag="decay")
         for h, slots in enumerate(halves):
             nc.vector.scalar_tensor_tensor(change[0][:, slots], first[h][:], -LR, drift[0][:, slots], ALU.mult, ALU.add)
             nc.gpsimd.tensor_tensor(w_new[0][:, slots], w_g[0][:, slots], change[0][:, slots], ALU.add)
@@ -254,7 +258,7 @@ def tile_attend_gkl_pl_mom_kernel(tc, xT, wT, y, wt, xm, mT, offs, out_0, out_1,
         form_change(2)
         for t in (1, 2):
             if t == 2:
-                head, tail = slice(0, 5 * N // 8), slice(5 * N // 8, N)
+                head, tail = slice(0, 11 * N // 16), slice(11 * N // 16, N)
             w_new[t] = tile([P, head.stop], F32, f"w_new{t}", tag="w_pair0" if t == 2 else None)
             nc.gpsimd.tensor_tensor(w_new[t][:], w_g[t][:, head], change[t][:, head], ALU.add)
             nc.vector.tensor_tensor(w_dst[t][:].indirect(listed(tail)), w_g[t][:, tail], change[t][:, tail], ALU.add)

@@ -92,7 +92,7 @@ def tile_attend_gkl_pl_mom_kernel(tc, xT, wT, y, wt, xm, mT, offs, out_0, out_1,
         w_dst = [tile([P, T], F32, f"w_dst{t}") for t in range(PACK)]
         for t in range(PACK):
             nc.sync.dma_start(m_src[t][:], plane(mT, t))
-        loaded = 3 * T // 4
+        loaded = 5 * T // 8
         nc.sync.dma_start(m_dst[1][:, :loaded], plane(mT, 1)[:, :loaded])
         nc.sync.dma_start(m_dst[2][:], plane(mT, 2))
 
@@ -279,27 +279,25 @@ def tile_attend_gkl_pl_mom_kernel(tc, xT, wT, y, wt, xm, mT, offs, out_0, out_1,
             if k != 1:
                 wide = slice(a, a + (2 * CHUNK if k == 0 else CHUNK))
                 rounded_tag = {0: "w_pair1", 2: "m_src3", 3: group_tags[1]}[k]
-                rounded = tile([P, 2, wide.stop - wide.start, 2], BF16, f"rounded{k}", tag=rounded_tag)
-                pair_words = rounded[:].rearrange("p u c e -> p (u c e)").bitcast(I32).rearrange("p (u c) -> p u c", u=2)
+                rounded = tile([P, PACK, wide.stop - wide.start], BF16, f"rounded{k}", tag=rounded_tag)
                 parts = halves if k == 3 else (slice(0, CHUNK),)
                 for t in range(PACK):
                     if k == 3 and t == PACK - 1:
                         for part in parts:
                             source = w_dst[t][:, a + part.start : a + part.stop]
-                            nc.vector.tensor_copy(rounded[:, t // 2, part, t % 2], source)
+                            nc.vector.tensor_copy(rounded[:, t, part], source)
                     else:
-                        nc.vector.tensor_copy(rounded[:, t // 2, :, t % 2], w_dst[t][:, wide])
+                        nc.vector.tensor_copy(rounded[:, t, :], w_dst[t][:, wide])
                     if k == 0 and t == 0:
                         nc.scalar.activation(
                             m_dst[2][:].indirect(offsets[:]), change[2][:], ACT.Copy, scale=undo_rate[:]
                         )
             grouped = tile([P, CHUNK, PACK], BF16, f"grouped{k}", tag=group_tags[k])
-            group_words = grouped[:].rearrange("p c t -> p (c t)").bitcast(I32).rearrange("p (c u) -> p c u", u=2)
             first_col = a - wide.start
             for part in parts:
                 nc.vector.tensor_copy(
-                    group_words[:, part, :],
-                    pair_words[:, :, first_col + part.start : first_col + part.stop].rearrange("p u c -> p c u"),
+                    grouped[:, part, :].rearrange("p (c i) t -> p c t i", i=4),
+                    rounded[:, :, first_col + part.start : first_col + part.stop].rearrange("p t (c i) -> p c t i", i=4),
                 )
             if k == 1:
                 copy_momentum(3, rounded_tag)

@@ -30,7 +30,7 @@ def tile_attend_gkl_pl_mom_kernel(tc, xT, wT, y, wt, xm, mT, offs, out_0, out_1,
         psum = ctx.enter_context(tc.psum_pool(name="psum", bufs=1))
 
         def tile(shape, dtype, name, tag=None):
-            return sb.tile(shape, dtype, name=name, tag=tag or name, align_bytes=64)
+            return sb.tile(shape, dtype, name=name, tag=tag or name, align_bytes=256)
 
         def plane(table, t):
             return table.rearrange("(p t) c -> p t c", t=PACK)[:, t, :]

@@ -92,7 +92,7 @@ def tile_attend_gkl_pl_mom_kernel(tc, xT, wT, y, wt, xm, mT, offs, out_0, out_1,
         w_dst = [tile([P, T], F32, f"w_dst{t}") for t in range(PACK)]
         for t in range(PACK):
             nc.sync.dma_start(m_src[t][:], plane(mT, t))
-        loaded = 5 * T // 8
+        loaded, early = T // 2, 5 * T // 8
         nc.sync.dma_start(m_dst[1][:, :loaded], plane(mT, 1)[:, :loaded])
         nc.sync.dma_start(m_dst[2][:], plane(mT, 2))
 
@@ -211,7 +211,7 @@ def tile_attend_gkl_pl_mom_kernel(tc, xT, wT, y, wt, xm, mT, offs, out_0, out_1,
         drift = {t: tile([P, N], F32, f"drift{t}") for t in range(2)}
         for t in range(2):
             nc.scalar.activation(drift[t][:], m_src[t][:].indirect(offsets[:]), ACT.Copy, scale=decay[:])
-        nc.scalar.activation(m_dst[1][:, loaded:], m_src[1][:, loaded:], ACT.Copy)
+        nc.scalar.activation(m_dst[1][:, early:], m_src[1][:, early:], ACT.Copy)
         change = {}
         undo_rate = tile([P, 1], F32, "undo_rate")
         nc.gpsimd.memset(undo_rate[:], -1.0 / LR)
@@ -252,6 +252,7 @@ def tile_attend_gkl_pl_mom_kernel(tc, xT, wT, y, wt, xm, mT, offs, out_0, out_1,
             nc.vector.scalar_tensor_tensor(change[0][:, slots], first[h][:], -LR, drift[0][:, slots], ALU.mult, ALU.add)
             nc.gpsimd.tensor_tensor(w_new[0][:, slots], w_g[0][:, slots], change[0][:, slots], ALU.add)
         weights_by_scalar(0)
+        nc.scalar.activation(m_dst[1][:, loaded:early], m_src[1][:, loaded:early], ACT.Copy)
         gather_drift(2)
         head, tail = slice(0, 3 * N // 4), slice(3 * N // 4, N)
         form_change(1, tag="m_src2")

@@ -53,7 +53,7 @@ def tile_attend_gkl_pl_mom_kernel(tc, xT, wT, y, wt, xm, mT, offs, out_0, out_1,
 
         def product(bank, lhs, lhs_fmt, cols, rhs, rhs_fmt, slots=slice(0, N)):
             nc.tensor.matmul_mx(
-                out=bank[:],
+                out=bank,
                 lhsT=lhs[0][:, cols].bitcast(lhs_fmt),
                 lhsT_scale=lhs[1][:, cols],
                 rhs=rhs[0][:, slots].bitcast(rhs_fmt),
@@ -62,10 +62,6 @@ def tile_attend_gkl_pl_mom_kernel(tc, xT, wT, y, wt, xm, mT, offs, out_0, out_1,
                 stop=True,
             )
 
-        one = tile([P, 1], F32, "one")
-        nc.gpsimd.memset(one[:], 1.0)
-        decay = tile([P, 1], F32, "decay")
-        nc.gpsimd.tensor_scalar(decay[:], one[:], -LR * BETA, 0.0, ALU.mult, ALU.add)
         halves = (slice(0, N // 2), slice(N // 2, N))
         offsets = tile([P, N // 16], U16, "offsets")
 
@@ -90,9 +86,9 @@ def tile_attend_gkl_pl_mom_kernel(tc, xT, wT, y, wt, xm, mT, offs, out_0, out_1,
         m_src = [tile([P, T], F32, f"m_src{t}") for t in range(PACK)]
         m_dst = {t: tile([P, T], F32, f"m_dst{t}") for t in (1, 2)}
         w_dst = [tile([P, T], F32, f"w_dst{t}") for t in range(PACK)]
-        for t in range(PACK):
+        for t in (0, 2, 1, 3):
             nc.sync.dma_start(m_src[t][:], plane(mT, t))
-        loaded, early = T // 2, 5 * T // 8
+        loaded = 3 * T // 4
         nc.sync.dma_start(m_dst[1][:, :loaded], plane(mT, 1)[:, :loaded])
         nc.sync.dma_start(m_dst[2][:], plane(mT, 2))
 
@@ -113,13 +109,16 @@ def tile_attend_gkl_pl_mom_kernel(tc, xT, wT, y, wt, xm, mT, offs, out_0, out_1,
         gather_weights(1, slice(0, N))
         group_weights(0, slice(0, N))
         gather_weights(2, slice(0, N))
-        for slots in halves:
-            gather_weights(3, slots)
+        for t in range(PACK - 1):
+            nc.scalar.activation(w_dst[t][:], w_src[t][:], ACT.Copy)
+        gather_weights(3, halves[0])
+        nc.scalar.activation(w_g[3][:, halves[1]], w_src[3][:].indirect(listed(halves[1])), ACT.Copy)
         for slots in halves:
             group_weights(1, slots)
-        for t in range(PACK):
-            nc.scalar.activation(w_dst[t][:], w_src[t][:], ACT.Copy)
+        shared = 11 * T // 16
+        nc.scalar.activation(w_dst[3][:, :shared], w_src[3][:, :shared], ACT.Copy)
         w_mx = quantize("w", w_bf[:].rearrange("p c t -> p (c t)"), E4M3, 2)
+        nc.vector.tensor_copy(w_dst[3][:, shared:], w_src[3][:, shared:])
 
         x_bf = tile([P, PACK, P, PACK], BF16, "x_bf")
         for u in range(2):
@@ -148,7 +147,7 @@ def tile_attend_gkl_pl_mom_kernel(tc, xT, wT, y, wt, xm, mT, offs, out_0, out_1,
         sums = tile([P, PACK], F32, "sums")
         for j in range(PACK):
             score = psum.tile([P, N], F32, name=f"score{j}")
-            product(score, x_mx, E4M3, slice(j * P, (j + 1) * P), w_mx, E4M3)
+            product(score[:], x_mx, E4M3, slice(j * P, (j + 1) * P), w_mx, E4M3)
             if j == PACK - 1:
                 nc.vector.reciprocal(inv[:, :1], sums[:, :1])
             nc.vector.tensor_reduce(neg_max[:, j : j + 1], score[:], AXIS.X, ALU.max, negate=True)
@@ -200,19 +199,20 @@ def tile_attend_gkl_pl_mom_kernel(tc, xT, wT, y, wt, xm, mT, offs, out_0, out_1,
             quantize_part(g_mx, g_grouped, E5M2, cols)
         quantize_part(xm_mx, xm_grouped, E4M3, slice(P, D))
 
-        first = [psum.tile([P, N // 2], F32, name=f"dw0_{h}", tag=("score0", "dw0")[h]) for h in range(2)]
-        for h in range(2):
-            product(first[h], xm_mx, E4M3, slice(0, P), g_mx, E5M2, halves[h])
-        dw = {}
+        dw = {0: psum.tile([P, N], F32, name="dw0")}
+        for slots in halves:
+            product(dw[0][:, slots], xm_mx, E4M3, slice(0, P), g_mx, E5M2, slots)
         for t in range(1, PACK):
             dw[t] = psum.tile([P, N], F32, name=f"dw{t}")
-            product(dw[t], xm_mx, E4M3, slice(t * P, (t + 1) * P), g_mx, E5M2)
+            product(dw[t][:], xm_mx, E4M3, slice(t * P, (t + 1) * P), g_mx, E5M2)
 
-        drift = {t: tile([P, N], F32, f"drift{t}") for t in range(2)}
-        for t in range(2):
-            nc.scalar.activation(drift[t][:], m_src[t][:].indirect(offsets[:]), ACT.Copy, scale=decay[:])
-        nc.scalar.activation(m_dst[1][:, early:], m_src[1][:, early:], ACT.Copy)
+        drift = {0: tile([P, N], F32, "drift0")}
+        nc.scalar.activation(drift[0][:], m_src[0][:].indirect(offsets[:]), ACT.Copy, scale=-LR * BETA)
+        m_dst[0] = tile([P, T], F32, "m_dst0", tag="xm_raw")
+        nc.scalar.activation(m_dst[0][:], m_src[0][:], ACT.Copy)
         change = {}
+        one = tile([P, 1], F32, "one")
+        nc.gpsimd.memset(one[:], 1.0)
         undo_rate = tile([P, 1], F32, "undo_rate")
         nc.gpsimd.memset(undo_rate[:], -1.0 / LR)
 
@@ -224,15 +224,7 @@ def tile_attend_gkl_pl_mom_kernel(tc, xT, wT, y, wt, xm, mT, offs, out_0, out_1,
             change[t] = tile([P, N], F32, f"change{t}", tag=tag)
             nc.vector.scalar_tensor_tensor(change[t][:], dw[t][:], -LR, drift[t][:], ALU.mult, ALU.add)
 
-        def scalar_scatter(window, values, scale):
-            for slots in halves:
-                nc.scalar.activation(window[:].indirect(listed(slots)), values[:, slots], ACT.Copy, scale=scale)
-
         w_new = {}
-
-        def weights_by_scalar(t):
-            scalar_scatter(w_dst[t], w_new[t], 1.0)
-            nc.sync.dma_start(plane(out_0, t), w_dst[t][:])
 
         def weights_by_vector(t):
             nc.vector.tensor_tensor(w_dst[t][:].indirect(offsets[:]), w_g[t], change[t][:], ALU.add)
@@ -246,31 +238,32 @@ def tile_attend_gkl_pl_mom_kernel(tc, xT, wT, y, wt, xm, mT, offs, out_0, out_1,
             m_dst[t] = tile([P, T], F32, f"m_dst{t}", tag=tag)
             nc.vector.tensor_copy(m_dst[t][:], m_src[t][:])
 
-        change[0] = tile([P, N], F32, "change0")
-        w_new[0] = tile([P, N], F32, "w_new0", tag="decay")
-        for h, slots in enumerate(halves):
-            nc.vector.scalar_tensor_tensor(change[0][:, slots], first[h][:], -LR, drift[0][:, slots], ALU.mult, ALU.add)
-            nc.gpsimd.tensor_tensor(w_new[0][:, slots], w_g[0][:, slots], change[0][:, slots], ALU.add)
-        weights_by_scalar(0)
-        nc.scalar.activation(m_dst[1][:, loaded:early], m_src[1][:, loaded:early], ACT.Copy)
+        form_change(0)
+        scatter_momentum(0)
+        w_new[0] = tile([P, N], F32, "w_new0")
+        nc.gpsimd.tensor_tensor(w_new[0][:], w_g[0], change[0][:], ALU.add)
+        nc.scalar.activation(w_dst[0][:].indirect(offsets[:]), w_new[0][:], ACT.Copy, scale=one[:])
+        nc.sync.dma_start(plane(out_0, 0), w_dst[0][:])
         gather_drift(2)
+        gather_drift(1)
+        nc.vector.tensor_copy(m_dst[1][:, loaded:], m_src[1][:, loaded:])
         head, tail = slice(0, 3 * N // 4), slice(3 * N // 4, N)
-        form_change(1, tag="m_src2")
-        form_change(2)
+        form_change(1)
+        form_change(2, tag="m_src1")
         for t in (1, 2):
             if t == 2:
-                head, tail = slice(0, 11 * N // 16), slice(11 * N // 16, N)
+                head, tail = slice(0, 13 * N // 16), slice(13 * N // 16, N)
             w_new[t] = tile([P, head.stop], F32, f"w_new{t}", tag="w_pair0" if t == 2 else None)
             nc.gpsimd.tensor_tensor(w_new[t][:], w_g[t][:, head], change[t][:, head], ALU.add)
             nc.vector.tensor_tensor(w_dst[t][:].indirect(listed(tail)), w_g[t][:, tail], change[t][:, tail], ALU.add)
-            nc.scalar.activation(w_dst[t][:].indirect(listed(head)), w_new[t][:], ACT.Copy)
-            nc.sync.dma_start(plane(out_0, t), w_dst[t][:])
+            nc.scalar.activation(w_dst[t][:].indirect(listed(head)), w_new[t][:], ACT.Copy, scale=one[:])
+            if t == 1:
+                nc.sync.dma_start(plane(out_0, t), w_dst[t][:])
         gather_drift(3)
         form_change(3)
         weights_by_vector(3)
-        copy_momentum(0, "drift3")
-        for t in (1, 0):
-            scatter_momentum(t)
+        nc.sync.dma_start(plane(out_0, 2), w_dst[2][:])
+        scatter_momentum(1)
         out_codes = tile([P, T], U32, "out_codes", tag="w_src0")
         out_scales = tile([P, CHUNK], U8, "out_scales")
         words = out_2[0].rearrange("p c t -> p (c t)").bitcast(I32)
@@ -279,12 +272,12 @@ def tile_attend_gkl_pl_mom_kernel(tc, xT, wT, y, wt, xm, mT, offs, out_0, out_1,
             cols = slice(a, a + CHUNK)
             if k != 1:
                 wide = slice(a, a + (2 * CHUNK if k == 0 else CHUNK))
-                rounded_tag = {0: "w_pair1", 2: "m_src3", 3: group_tags[1]}[k]
+                rounded_tag = {0: "drift3", 2: "m_src3", 3: group_tags[1]}[k]
                 rounded = tile([P, PACK, wide.stop - wide.start], BF16, f"rounded{k}", tag=rounded_tag)
                 parts = halves if k == 3 else (slice(0, CHUNK),)
-                for t in range(PACK):
-                    if k == 3 and t == PACK - 1:
-                        for part in parts:
+                for t in (0, 1, 3, 2) if k == 0 else range(PACK):
+                    if (k, t) in ((0, 2), (3, 3)):
+                        for part in parts if k == 3 else (slice(0, CHUNK), slice(CHUNK, 2 * CHUNK)):
                             source = w_dst[t][:, a + part.start : a + part.stop]
                             nc.vector.tensor_copy(rounded[:, t, part], source)
                     else:

@@ -108,6 +108,8 @@ def tile_attend_gkl_pl_mom_kernel(tc, xT, wT, y, wt, xm, mT, offs, out_0, out_1,
         gather_weights(0, slice(0, N))
         gather_weights(1, slice(0, N))
         group_weights(0, slice(0, N))
+        w_share = tile([P, N // 4], F32, "w_share")
+        nc.vector.tensor_copy(w_share[:], w_src[1][:].indirect(listed(slice(3 * N // 4, N))))
         gather_weights(2, slice(0, N))
         for t in range(PACK - 1):
             nc.scalar.activation(w_dst[t][:], w_src[t][:], ACT.Copy)
@@ -253,9 +255,10 @@ def tile_attend_gkl_pl_mom_kernel(tc, xT, wT, y, wt, xm, mT, offs, out_0, out_1,
         for t in (1, 2):
             if t == 2:
                 head, tail = slice(0, 13 * N // 16), slice(13 * N // 16, N)
-            w_new[t] = tile([P, head.stop], F32, f"w_new{t}", tag="w_pair0" if t == 2 else None)
+            old = w_share[:] if t == 1 else w_g[t][:, tail]
+            nc.vector.tensor_tensor(w_dst[t][:].indirect(listed(tail)), old, change[t][:, tail], ALU.add)
+            w_new[t] = tile([P, head.stop], F32, f"w_new{t}", tag="w_pair0" if t == 2 else "w_share")
             nc.gpsimd.tensor_tensor(w_new[t][:], w_g[t][:, head], change[t][:, head], ALU.add)
-            nc.vector.tensor_tensor(w_dst[t][:].indirect(listed(tail)), w_g[t][:, tail], change[t][:, tail], ALU.add)
             nc.scalar.activation(w_dst[t][:].indirect(listed(head)), w_new[t][:], ACT.Copy, scale=one[:])
             if t == 1:
                 nc.sync.dma_start(plane(out_0, t), w_dst[t][:])
@@ -263,6 +266,7 @@ def tile_attend_gkl_pl_mom_kernel(tc, xT, wT, y, wt, xm, mT, offs, out_0, out_1,
         form_change(3)
         weights_by_vector(3)
         nc.sync.dma_start(plane(out_0, 2), w_dst[2][:])
+        copy_momentum(3, "drift3")
         scatter_momentum(1)
         out_codes = tile([P, T], U32, "out_codes", tag="w_src0")
         out_scales = tile([P, CHUNK], U8, "out_scales")
@@ -272,7 +276,7 @@ def tile_attend_gkl_pl_mom_kernel(tc, xT, wT, y, wt, xm, mT, offs, out_0, out_1,
             cols = slice(a, a + CHUNK)
             if k != 1:
                 wide = slice(a, a + (2 * CHUNK if k == 0 else CHUNK))
-                rounded_tag = {0: "drift3", 2: "m_src3", 3: group_tags[1]}[k]
+                rounded_tag = {0: "w_pair1", 2: "m_src3", 3: group_tags[1]}[k]
                 rounded = tile([P, PACK, wide.stop - wide.start], BF16, f"rounded{k}", tag=rounded_tag)
                 parts = halves if k == 3 else (slice(0, CHUNK),)
                 for t in (0, 1, 3, 2) if k == 0 else range(PACK):
@@ -284,17 +288,22 @@ def tile_attend_gkl_pl_mom_kernel(tc, xT, wT, y, wt, xm, mT, offs, out_0, out_1,
                         nc.vector.tensor_copy(rounded[:, t, :], w_dst[t][:, wide])
                     if k == 0 and t == 0:
                         nc.scalar.activation(
-                            m_dst[2][:].indirect(offsets[:]), change[2][:], ACT.Copy, scale=undo_rate[:]
+                            m_dst[3][:].indirect(offsets[:]), change[3][:], ACT.Copy, scale=undo_rate[:]
                         )
             grouped = tile([P, CHUNK, PACK], BF16, f"grouped{k}", tag=group_tags[k])
             first_col = a - wide.start
-            for part in parts:
-                nc.vector.tensor_copy(
+            helped = 11 * CHUNK // 16
+            shares = [(nc.vector.tensor_copy, part) for part in parts]
+            if k == 3:
+                shares[1:] = [
+                    (nc.vector.tensor_copy, slice(CHUNK // 2, helped)),
+                    (nc.scalar.copy, slice(helped, CHUNK)),
+                ]
+            for move, part in shares:
+                move(
                     grouped[:, part, :].rearrange("p (c i) t -> p c t i", i=4),
                     rounded[:, :, first_col + part.start : first_col + part.stop].rearrange("p t (c i) -> p c t i", i=4),
                 )
-            if k == 1:
-                copy_momentum(3, rounded_tag)
             for part in parts:
                 nc.vector.quantize_mx(
                     out=out_codes[:, a + part.start : a + part.stop].bitcast(E4M3),
@@ -305,9 +314,9 @@ def tile_attend_gkl_pl_mom_kernel(tc, xT, wT, y, wt, xm, mT, offs, out_0, out_1,
                 done = wide if k == 1 else cols
                 nc.sync.dma_start(words[:, done], out_codes[:, done].bitcast(I32))
             if k == 1:
-                nc.sync.dma_start(plane(out_1, 2), m_dst[2][:])
+                nc.sync.dma_start(plane(out_1, 3), m_dst[3][:])
             if k == 2:
-                scatter_momentum(3)
+                scatter_momentum(2)
         for q in range(4):
             nc.sync.dma_start(
                 out_3[0, 4 * q : 4 * q + 4, :].bitcast(I32).rearrange("r (k c) -> k r c", k=4),

from contextlib import ExitStack

import concourse.mybir as mybir

D, T, N, R = 512, 2048, 512, 512
LR, BETA = 0.1, 0.9
FLOPS = 2 * 2 * D * N * R

F32 = mybir.dt.float32
BF16 = mybir.dt.bfloat16
I32 = mybir.dt.int32
U32 = mybir.dt.uint32
U16 = mybir.dt.uint16
U8 = mybir.dt.uint8
E4M3 = mybir.dt.float8_e4m3fn_x4
E5M2 = mybir.dt.float8_e5m2_x4
ALU = mybir.AluOpType
ACT = mybir.ActivationFunctionType
AXIS = mybir.AxisListType

P = 128
PACK = 4
CHUNK = 512


def tile_attend_gkl_pl_mom_kernel(tc, xT, wT, y, wt, xm, mT, offs, out_0, out_1, out_2, out_3):
    nc = tc.nc
    with ExitStack() as ctx:
        sb = ctx.enter_context(tc.tile_pool(name="sb", bufs=1))
        psum = ctx.enter_context(tc.psum_pool(name="psum", bufs=1))

        def tile(shape, dtype, name, tag=None):
            return sb.tile(shape, dtype, name=name, tag=tag or name, align_bytes=256)

        def plane(table, t):
            return table.rearrange("(p t) c -> p t c", t=PACK)[:, t, :]

        def operand(name):
            return tile([P, N], U32, name + "_codes"), tile([P, N], U8, name + "_scales")

        def quantize_part(mx, grouped, fmt, cols):
            nc.vector.quantize_mx(
                out=mx[0][:, cols].bitcast(fmt),
                scales=mx[1][:, cols],
                in_=grouped[:, PACK * cols.start : PACK * cols.stop],
            )

        def quantize(name, grouped, fmt, pieces):
            mx = operand(name)
            for a in range(0, N, N // pieces):
                quantize_part(mx, grouped, fmt, slice(a, a + N // pieces))
            return mx

        def product(bank, lhs, lhs_fmt, cols, rhs, rhs_fmt, slots=slice(0, N)):
            nc.tensor.matmul_mx(
                out=bank,
                lhsT=lhs[0][:, cols].bitcast(lhs_fmt),
                lhsT_scale=lhs[1][:, cols],
                rhs=rhs[0][:, slots].bitcast(rhs_fmt),
                rhs_scale=rhs[1][:, slots],
                start=True,
                stop=True,
            )

        halves = (slice(0, N // 2), slice(N // 2, N))
        offsets = tile([P, N // 16], U16, "offsets")

        def listed(slots):
            return offsets[:, slots.start // 16 : slots.stop // 16]

        w_src = [tile([P, T], F32, f"w_src{t}") for t in range(PACK)]
        nc.sync.dma_start(w_src[0][:], plane(wT, 0))
        nc.sync.dma_start(offsets[:], offs)
        for t in range(1, PACK):
            nc.sync.dma_start(w_src[t][:], plane(wT, t))

        x_raw = tile([P, PACK, R], F32, "x_raw")
        nc.sync.dma_start(x_raw[:], xT[0].rearrange("(p t) r -> p t r", t=PACK))
        wt_sb = tile([P, PACK], F32, "wt_sb")
        nc.sync.dma_start(wt_sb[:], wt[0].rearrange("(p j) one -> p (j one)", j=PACK))
        y_sb = [tile([P, 2, N], F32, f"y_sb{h}") for h in range(2)]
        for h in range(2):
            nc.sync.dma_start(y_sb[h][:], y[0].rearrange("(p j) i -> p j i", j=PACK)[:, 2 * h : 2 * h + 2, :])
        xm_raw = tile([P, PACK, D], F32, "xm_raw")
        nc.sync.dma_start(xm_raw[:], xm[0].rearrange("(p j) d -> p j d", j=PACK))
        m_src = [tile([P, T], F32, f"m_src{t}") for t in range(PACK)]
        m_dst = {t: tile([P, T], F32, f"m_dst{t}") for t in (1, 2)}
        w_dst = [tile([P, T], F32, f"w_dst{t}") for t in range(PACK)]
        for t in (0, 2, 1, 3):
            nc.sync.dma_start(m_src[t][:], plane(mT, t))
        loaded = 3 * T // 4
        nc.sync.dma_start(m_dst[1][:, :loaded], plane(mT, 1)[:, :loaded])
        nc.sync.dma_start(m_dst[2][:], plane(mT, 2))

        w_pair = [tile([P, 2, N], F32, f"w_pair{u}") for u in range(2)]
        w_g = [w_pair[t // 2][:, t % 2, :] for t in range(PACK)]
        w_bf = tile([P, N, PACK], BF16, "w_bf")

        def gather_weights(t, slots):
            nc.vector.tensor_copy(w_g[t][:, slots], w_src[t][:].indirect(listed(slots)))

        def group_weights(u, slots):
            nc.vector.tensor_copy(
                w_bf[:, slots, 2 * u : 2 * u + 2].rearrange("p (c i) t -> p c t i", i=4),
                w_pair[u][:, :, slots].rearrange("p t (c i) -> p c t i", i=4),
            )

        gather_weights(0, slice(0, N))
        gather_weights(1, slice(0, N))
        group_weights(0, slice(0, N))
        w_share = tile([P, N // 4], F32, "w_share")
        nc.vector.tensor_copy(w_share[:], w_src[1][:].indirect(listed(slice(3 * N // 4, N))))
        gather_weights(2, slice(0, N))
        for t in range(PACK - 1):
            nc.scalar.activation(w_dst[t][:], w_src[t][:], ACT.Copy)
        gather_weights(3, halves[0])
        nc.scalar.activation(w_g[3][:, halves[1]], w_src[3][:].indirect(listed(halves[1])), ACT.Copy)
        for slots in halves:
            group_weights(1, slots)
        shared = 11 * T // 16
        nc.scalar.activation(w_dst[3][:, :shared], w_src[3][:, :shared], ACT.Copy)
        w_mx = quantize("w", w_bf[:].rearrange("p c t -> p (c t)"), E4M3, 2)
        nc.vector.tensor_copy(w_dst[3][:, shared:], w_src[3][:, shared:])

        x_bf = tile([P, PACK, P, PACK], BF16, "x_bf")
        for u in range(2):
            for h in range(2):
                rows = slice(h * (P // 2), (h + 1) * (P // 2))
                dealt = x_bf[:, 2 * u : 2 * u + 2, rows, :].rearrange("p j m t -> p m t j")
                given = x_raw[:].rearrange("p t (m j) -> p m t j", j=PACK)[:, rows, :, 2 * u : 2 * u + 2]
                if h == 0:
                    nc.scalar.activation(dealt, given, ACT.Copy)
                else:
                    nc.vector.tensor_copy(dealt, given)
        x_mx = quantize("x", x_bf[:].rearrange("p j m t -> p (j m t)"), E4M3, PACK)

        xm_bf = tile([P, PACK, P, PACK], BF16, "xm_bf")

        target = tile([P, PACK, N], F32, "target")
        for j in range(2):
            nc.scalar.activation(target[:, j, :], y_sb[0][:, j, :], ACT.Copy, scale=wt_sb[:, j : j + 1])
        for j in range(2, PACK):
            nc.gpsimd.tensor_scalar(target[:, j, :], y_sb[1][:, j - 2, :], wt_sb[:, j : j + 1], 0.0, ALU.mult, ALU.add)

        neg_max = tile([P, PACK], F32, "neg_max")
        inv = tile([P, PACK], F32, "inv")
        e = [tile([P, N], F32, f"e{j}") for j in range(PACK)]
        weighted = tile([P, PACK, N], F32, "weighted")
        sums = tile([P, PACK], F32, "sums")
        for j in range(PACK):
            score = psum.tile([P, N], F32, name=f"score{j}")
            product(score[:], x_mx, E4M3, slice(j * P, (j + 1) * P), w_mx, E4M3)
            if j == PACK - 1:
                nc.vector.reciprocal(inv[:, :1], sums[:, :1])
            nc.vector.tensor_reduce(neg_max[:, j : j + 1], score[:], AXIS.X, ALU.max, negate=True)
            nc.scalar.activation(
                e[j][:], score[:], ACT.Exp, bias=neg_max[:, j : j + 1], scale=1.0, accum_out=sums[:, j : j + 1]
            )

        def normalise(engine, j, cols=slice(0, N)):
            engine.tensor_scalar(
                weighted[:, j, cols], e[j][:, cols], inv[:, j : j + 1], wt_sb[:, j : j + 1], ALU.mult, ALU.mult
            )

        g_bf = tile([P, N, PACK], BF16, "g_bf")
        g_grouped = g_bf[:].rearrange("p c j -> p (c j)")
        xm_grouped = xm_bf[:].rearrange("p t m j -> p (t m j)")
        g_mx, xm_mx = operand("g"), operand("xm")

        def form_gradient(cols):
            nc.vector.tensor_tensor(
                g_bf[:, cols, :].rearrange("p (c i) j -> p c j i", i=4),
                weighted[:, :, cols].rearrange("p j (c i) -> p c j i", i=4),
                target[:, :, cols].rearrange("p j (c i) -> p c j i", i=4),
                ALU.subtract,
            )

        def cast_xm(part):
            dealt = xm_bf[:, :, part, :].rearrange("p t m j -> p m j t")
            given = xm_raw[:, :, PACK * part.start : PACK * part.stop].rearrange("p j (m t) -> p m j t", t=PACK)
            if part.start == 0:
                nc.scalar.activation(dealt, given, ACT.Copy)
            else:
                nc.vector.tensor_copy(dealt, given)

        split = 3 * P // 4
        normalise(nc.gpsimd, 0)
        nc.vector.reciprocal(inv[:, 1:2], sums[:, 1:2])
        cast_xm(slice(0, split))
        cast_xm(slice(split, P))
        nc.vector.reciprocal(inv[:, 2:3], sums[:, 2:3])
        normalise(nc.vector, 1)
        nc.vector.reciprocal(inv[:, 3:], sums[:, 3:])
        normalise(nc.vector, 2)
        for cols in halves:
            normalise(nc.vector, 3, cols)
        for cols in halves:
            form_gradient(cols)
        quantize_part(xm_mx, xm_grouped, E4M3, slice(0, P))
        for cols in halves:
            quantize_part(g_mx, g_grouped, E5M2, cols)
        quantize_part(xm_mx, xm_grouped, E4M3, slice(P, D))

        dw = {0: psum.tile([P, N], F32, name="dw0")}
        for slots in halves:
            product(dw[0][:, slots], xm_mx, E4M3, slice(0, P), g_mx, E5M2, slots)
        for t in range(1, PACK):
            dw[t] = psum.tile([P, N], F32, name=f"dw{t}")
            product(dw[t][:], xm_mx, E4M3, slice(t * P, (t + 1) * P), g_mx, E5M2)

        drift = {0: tile([P, N], F32, "drift0")}
        nc.scalar.activation(drift[0][:], m_src[0][:].indirect(offsets[:]), ACT.Copy, scale=-LR * BETA)
        m_dst[0] = tile([P, T], F32, "m_dst0", tag="xm_raw")
        nc.scalar.activation(m_dst[0][:], m_src[0][:], ACT.Copy)
        change = {}
        one = tile([P, 1], F32, "one")
        nc.gpsimd.memset(one[:], 1.0)
        undo_rate = tile([P, 1], F32, "undo_rate")
        nc.gpsimd.memset(undo_rate[:], -1.0 / LR)

        def gather_drift(t):
            drift[t] = tile([P, N], F32, f"drift{t}")
            nc.vector.tensor_scalar(drift[t][:], m_src[t][:].indirect(offsets[:]), -LR * BETA, 0.0, ALU.mult, ALU.add)

        def form_change(t, tag=None):
            change[t] = tile([P, N], F32, f"change{t}", tag=tag)
            nc.vector.scalar_tensor_tensor(change[t][:], dw[t][:], -LR, drift[t][:], ALU.mult, ALU.add)

        w_new = {}

        def weights_by_vector(t):
            nc.vector.tensor_tensor(w_dst[t][:].indirect(offsets[:]), w_g[t], change[t][:], ALU.add)
            nc.sync.dma_start(plane(out_0, t), w_dst[t][:])

        def scatter_momentum(t):
            nc.scalar.activation(m_dst[t][:].indirect(offsets[:]), change[t][:], ACT.Copy, scale=undo_rate[:])
            nc.sync.dma_start(plane(out_1, t), m_dst[t][:])

        def copy_momentum(t, tag):
            m_dst[t] = tile([P, T], F32, f"m_dst{t}", tag=tag)
            nc.vector.tensor_copy(m_dst[t][:], m_src[t][:])

        form_change(0)
        scatter_momentum(0)
        w_new[0] = tile([P, N], F32, "w_new0")
        nc.gpsimd.tensor_tensor(w_new[0][:], w_g[0], change[0][:], ALU.add)
        nc.scalar.activation(w_dst[0][:].indirect(offsets[:]), w_new[0][:], ACT.Copy, scale=one[:])
        nc.sync.dma_start(plane(out_0, 0), w_dst[0][:])
        gather_drift(2)
        gather_drift(1)
        nc.vector.tensor_copy(m_dst[1][:, loaded:], m_src[1][:, loaded:])
        head, tail = slice(0, 3 * N // 4), slice(3 * N // 4, N)
        form_change(1)
        form_change(2, tag="m_src1")
        for t in (1, 2):
            if t == 2:
                head, tail = slice(0, 13 * N // 16), slice(13 * N // 16, N)
            old = w_share[:] if t == 1 else w_g[t][:, tail]
            nc.vector.tensor_tensor(w_dst[t][:].indirect(listed(tail)), old, change[t][:, tail], ALU.add)
            w_new[t] = tile([P, head.stop], F32, f"w_new{t}", tag="w_pair0" if t == 2 else "w_share")
            nc.gpsimd.tensor_tensor(w_new[t][:], w_g[t][:, head], change[t][:, head], ALU.add)
            nc.scalar.activation(w_dst[t][:].indirect(listed(head)), w_new[t][:], ACT.Copy, scale=one[:])
            if t == 1:
                nc.sync.dma_start(plane(out_0, t), w_dst[t][:])
        gather_drift(3)
        form_change(3)
        weights_by_vector(3)
        nc.sync.dma_start(plane(out_0, 2), w_dst[2][:])
        copy_momentum(3, "drift3")
        scatter_momentum(1)
        out_codes = tile([P, T], U32, "out_codes", tag="w_src0")
        out_scales = tile([P, CHUNK], U8, "out_scales")
        words = out_2[0].rearrange("p c t -> p (c t)").bitcast(I32)
        group_tags = ("w_src1", "w_src2", "w_src3", "x_raw")
        for k, a in enumerate(range(0, T, CHUNK)):
            cols = slice(a, a + CHUNK)
            if k != 1:
                wide = slice(a, a + (2 * CHUNK if k == 0 else CHUNK))
                rounded_tag = {0: "w_pair1", 2: "m_src3", 3: group_tags[1]}[k]
                rounded = tile([P, PACK, wide.stop - wide.start], BF16, f"rounded{k}", tag=rounded_tag)
                parts = halves if k == 3 else (slice(0, CHUNK),)
                for t in (0, 1, 3, 2) if k == 0 else range(PACK):
                    if (k, t) in ((0, 2), (3, 3)):
                        for part in parts if k == 3 else (slice(0, CHUNK), slice(CHUNK, 2 * CHUNK)):
                            source = w_dst[t][:, a + part.start : a + part.stop]
                            nc.vector.tensor_copy(rounded[:, t, part], source)
                    else:
                        nc.vector.tensor_copy(rounded[:, t, :], w_dst[t][:, wide])
                    if k == 0 and t == 0:
                        nc.scalar.activation(
                            m_dst[3][:].indirect(offsets[:]), change[3][:], ACT.Copy, scale=undo_rate[:]
                        )
            grouped = tile([P, CHUNK, PACK], BF16, f"grouped{k}", tag=group_tags[k])
            first_col = a - wide.start
            helped = 11 * CHUNK // 16
            shares = [(nc.vector.tensor_copy, part) for part in parts]
            if k == 3:
                shares[1:] = [
                    (nc.vector.tensor_copy, slice(CHUNK // 2, helped)),
                    (nc.scalar.copy, slice(helped, CHUNK)),
                ]
            for move, part in shares:
                move(
                    grouped[:, part, :].rearrange("p (c i) t -> p c t i", i=4),
                    rounded[:, :, first_col + part.start : first_col + part.stop].rearrange("p t (c i) -> p c t i", i=4),
                )
            for part in parts:
                nc.vector.quantize_mx(
                    out=out_codes[:, a + part.start : a + part.stop].bitcast(E4M3),
                    scales=out_scales[4 * k :, part],
                    in_=grouped[:, part, :].rearrange("p c t -> p (c t)"),
                )
            if k > 0:
                done = wide if k == 1 else cols
                nc.sync.dma_start(words[:, done], out_codes[:, done].bitcast(I32))
            if k == 1:
                nc.sync.dma_start(plane(out_1, 3), m_dst[3][:])
            if k == 2:
                scatter_momentum(2)
        for q in range(4):
            nc.sync.dma_start(
                out_3[0, 4 * q : 4 * q + 4, :].bitcast(I32).rearrange("r (k c) -> k r c", k=4),
                out_scales[32 * q : 32 * q + 16, :].bitcast(I32),
            )
